import numpy as np
import ml_dtypes


def mxq(x, axis, fmt="e4m3"):
    dtype, down = {"e4m3": (ml_dtypes.float8_e4m3fn, 7), "e5m2": (ml_dtypes.float8_e5m2, 14)}[fmt]
    v = np.moveaxis(np.asarray(x, np.float32).astype(ml_dtypes.bfloat16).astype(np.float64), axis, -1)
    blocks = v.reshape(v.shape[:-1] + (-1, 32))
    amax = np.abs(blocks).max(-1, keepdims=True)
    byte = np.maximum(np.where(amax > 0, np.frexp(amax)[1] - 1 + 127, 0) - down, 1)
    scale = np.exp2(byte - 127.0)
    codes = (blocks / scale).astype(np.float32).astype(dtype).astype(np.float64)
    return np.moveaxis((codes * scale).reshape(v.shape), -1, axis)


WIDE = False


def mx_kscale(k):
    if not WIDE:
        return np.ones(k)
    levels = np.array([10, -10, 5, -5, 0])
    if k % 512:
        return np.exp2(np.random.permutation(np.resize(levels, k // 32))).repeat(32)
    a = np.empty((k // 512, 16))
    for p in range(k // 512):
        a[p, :8] = np.random.permutation(np.resize(levels, 8))
        for g in range(8):
            far = levels[np.abs(levels - a[p, g]) >= 10]
            a[p, g + 8] = far[np.random.randint(len(far))]
    return np.exp2(a.ravel()).repeat(32)


def f64(x):
    return np.asarray(x).astype(np.float64)


def striped(idx):
    return np.tile(idx.reshape(-1, 16).T, (8, 1)).astype(np.uint16)


def unstriped(offs):
    return offs[:16].T.reshape(-1).astype(np.int64)


E2M1 = np.array([0.0, 0.5, 1.0, 1.5, 2.0, 3.0, 4.0, 6.0, -0.0, -0.5, -1.0, -1.5, -2.0, -3.0, -4.0, -6.0])


def pack_weight(w, fmt):
    k, n = w.shape
    w = f64(np.asarray(w, np.float32).astype(ml_dtypes.bfloat16)).reshape(k // 32, 32, n)
    amax = np.abs(w).max(1)
    if fmt == "e4m3":
        byte = np.frexp(amax)[1] - 1 + 127 - 7
    else:
        mant, ex = np.frexp(amax / 6.0)
        byte = np.where(mant > 0.5, ex, ex - 1) + 127
    byte = np.clip(np.where(amax > 0, byte, 1), 1, 254)
    scaled = (w * np.exp2(127.0 - byte)[:, None, :]).reshape(k, n).astype(np.float32)
    by_word = np.ascontiguousarray(scaled.reshape(k // 512, 128, 4, n).transpose(0, 1, 3, 2))
    if fmt == "e4m3":
        words = by_word.astype(ml_dtypes.float8_e4m3fn).view(np.uint8)
    else:
        c = by_word.astype(ml_dtypes.float4_e2m1fn).view(np.uint8) & 0xF
        words = (c[..., 0::2] | (c[..., 1::2] << 4)).reshape(k // 512, 128, 2 * n)
    return np.ascontiguousarray(words), np.ascontiguousarray(byte.astype(np.uint8).reshape(k // 512, 16, n))


def unpack_weight(words, scales, fmt):
    g, _, n = scales.shape
    words = np.ascontiguousarray(words).reshape(g, 128, n, -1)
    if fmt == "e4m3":
        vals = words.view(ml_dtypes.float8_e4m3fn).astype(np.float64)
    else:
        nib = np.empty((g, 128, n, 4), np.uint8)
        nib[..., 0::2] = words & 0xF
        nib[..., 1::2] = words >> 4
        vals = E2M1[nib]
    vals = vals * np.repeat(np.exp2(scales.astype(np.float64) - 127.0), 8, axis=1)[..., None]
    return vals.transpose(0, 1, 3, 2).reshape(g * 512, n)


def silu(v):
    return v / (1.0 + np.exp(-np.maximum(v, -700.0)))


K, T, E, C, N = 512, 1536, 8, 128, 128


def by_expert(wq, xq):
    return np.concatenate([wq[e].T @ xq[:, e * C:(e + 1) * C] for e in range(E)], axis=1)


def setup_inputs():
    n = np.random.standard_normal
    s = mx_kscale(K)[:, None]
    w = [pack_weight(m, "e2m1") for m in n((E, K, N)) / np.sqrt(K) / s[None]]
    return {
        "xT": (n((K, T)) * s).astype(np.float32),
        "xr": n((N, T)).astype(np.float32),
        "w_words": np.stack([m[0] for m in w]),
        "w_scales": np.stack([m[1] for m in w]),
        "b": (0.3 * n((N, E))).astype(np.float32),
        "gate": np.tile(np.random.uniform(0.2, 1.0, E * C), (N, 1)).astype(np.float32),
        "offs": striped(np.random.permutation(T)[:E * C]),
    }


def reference(xT, xr, w_words, w_scales, b, gate, offs):
    idx = unstriped(offs)
    w = np.stack([unpack_weight(w_words[e], w_scales[e], "e2m1") for e in range(E)])
    xq = mxq(f64(xT)[:, idx], 0, "e4m3")
    y = by_expert(w, xq)
    y = silu(y + np.repeat(f64(b), C, axis=1))
    out = f64(xr).copy()
    out[:, idx] += f64(gate) * y
    return out

@@ -1,0 +1,121 @@
+import concourse.mybir as mybir
+
+K, T, E, C, N = 512, 1536, 8, 128, 128
+FLOPS = 2 * K * N * E * C
+
+F32 = mybir.dt.float32
+BF16 = mybir.dt.bfloat16
+I32 = mybir.dt.int32
+U32 = mybir.dt.uint32
+U16 = mybir.dt.uint16
+U8 = mybir.dt.uint8
+FP8X4 = mybir.dt.float8_e4m3fn_x4
+FP4X4 = mybir.dt.float4_e2m1fn_x4
+MULT, ADD = mybir.AluOpType.mult, mybir.AluOpType.add
+SILU = mybir.ActivationFunctionType.Silu
+COPY = mybir.ActivationFunctionType.Copy
+
+P = 128
+PACK = 4
+
+CHUNKS = ((0, 768, 384, (512, 256)), (768, 512, 256, (512,)), (1280, 256, 160, (256,)))
+GROUPS = ((0, 1, 2, 3), (4, 5, 6, 7))
+STORES = ((0, 512), (512, 1024), (1024, 1344), (1344, 1536))
+
+
+def interleaved(grouped, a, b):
+    return grouped[:, a:b, :].rearrange("p (c i) t -> p c t i", i=4)
+
+
+def by_rows(raw, a, b):
+    return raw[:, :, a:b].rearrange("p t (c i) -> p c t i", i=4)
+
+
+def tile_moe_res_lin_silu_kernel(tc, xT, xr, w_words, w_scales, b, gate, offs, out):
+    nc = tc.nc
+    with (
+        tc.tile_pool(name="keep", bufs=1) as keep,
+        tc.psum_pool(name="psum", bufs=1) as psum,
+    ):
+        offsets = keep.tile([P, E * C // 16], U16, name="offsets")
+        words = keep.tile([P, T], U32, name="words", align_bytes=64)
+        scales = keep.tile([P, T], U8, name="scales", align_bytes=64)
+        w_codes = keep.tile([P, E, 2 * N], U8, name="w_codes", align_bytes=64)
+        w_bytes = keep.tile([P, E, N], U8, name="w_bytes", align_bytes=64)
+        bias = keep.tile([P, E], F32, name="bias")
+        gates = keep.tile([P, E * C], F32, name="gates")
+        residual = keep.tile([P, T], F32, name="residual")
+        placed = keep.tile([P, T], F32, name="placed")
+        warm = keep.tile([P, 1], F32, name="warm")
+        warmed = keep.tile([P, 1], F32, name="warmed")
+
+        tokens = xT.rearrange("(p j) t -> p j t", j=PACK)
+        raws = []
+        for i, (t0, width, share, pieces) in enumerate(CHUNKS):
+            raw = keep.tile([P, PACK, width], F32, name=f"raw{i}")
+            nc.sync.dma_start(out=raw[:], in_=tokens[:, :, t0 : t0 + width])
+            raws.append(raw)
+
+        nc.sync.dma_start(offsets[:], offs)
+
+        nc.vector.memset(warm[:], 0.0)
+        nc.scalar.activation(warmed[:], warm[:], SILU)
+        nc.gpsimd.memset(scales[:], 0)
+        nc.vector.memset(w_bytes[:].rearrange("p e n -> p (e n)").bitcast(I32), 0)
+        nc.vector.memset(placed[:], 0.0)
+
+        for q in range(4):
+            nc.sync.dma_start(
+                out=w_bytes[32 * q : 32 * q + 4, :, :].bitcast(I32),
+                in_=w_scales[:, 0, 4 * q : 4 * q + 4, :].rearrange("e q n -> q e n").bitcast(I32),
+            )
+        nc.sync.dma_start(out=w_codes[:].bitcast(I32), in_=w_words.rearrange("e a p n -> p (e a) n").bitcast(I32))
+        nc.sync.dma_start(out=bias[:], in_=b)
+        nc.sync.dma_start(out=gates[:], in_=gate)
+        nc.sync.dma_start(out=residual[:], in_=xr)
+
+        for i, (t0, width, share, pieces) in enumerate(CHUNKS):
+            grouped = keep.tile([P, width, PACK], BF16, name=f"grouped{i}", align_bytes=64)
+            nc.vector.tensor_copy(interleaved(grouped, 0, share), by_rows(raws[i], 0, share))
+            nc.scalar.activation(interleaved(grouped, share, width), by_rows(raws[i], share, width), COPY)
+            q0 = 0
+            for piece in pieces:
+                nc.vector.quantize_mx(
+                    out=words[:, t0 + q0 : t0 + q0 + piece].bitcast(FP8X4),
+                    scales=scales[:, t0 + q0 : t0 + q0 + piece],
+                    in_=grouped[:, q0 : q0 + piece, :].rearrange("p t j -> p (t j)"),
+                )
+                q0 += piece
+
+        results = []
+        for g, experts in enumerate(GROUPS):
+            s0, s1 = experts[0] * C, (experts[-1] + 1) * C
+            listed = offsets[:, s0 // 16 : s1 // 16]
+            slot_words = keep.tile([P, s1 - s0], U32, name=f"slot_words{g}", align_bytes=64)
+            slot_scales = keep.tile([P, s1 - s0], U8, name=f"slot_scales{g}", align_bytes=64)
+            nc.vector.tensor_copy(slot_words[:], words[:].indirect(listed))
+            nc.vector.tensor_copy(slot_scales[:], scales[:].indirect(listed))
+            y = keep.tile([P, s1 - s0], F32, name=f"y{g}")
+            for e in experts:
+                cols = slice(e * C - s0, (e + 1) * C - s0)
+                acc = psum.tile([P, C], F32, name=f"acc{e}")
+                nc.tensor.matmul_mx(
+                    out=acc[:],
+                    lhsT=w_codes[:, e, :].bitcast(FP4X4),
+                    lhsT_scale=w_bytes[:, e, :],
+                    rhs=slot_words[:, cols].bitcast(FP8X4),
+                    rhs_scale=slot_scales[:, cols],
+                    start=True,
+                    stop=True,
+                )
+                nc.scalar.activation(y[:, cols], acc[:], SILU, bias=bias[:, e : e + 1])
+            results.append((s0, s1, y))
+
+        for s0, s1, y in results:
+            nc.vector.tensor_tensor(placed[:].indirect(offsets[:, s0 // 16 : s1 // 16]), y[:], gates[:, s0:s1], MULT)
+
+        for i, (t0, t1) in enumerate(STORES):
+            total = keep.tile([P, t1 - t0], F32, name=f"total{i}")
+            nc.vector.tensor_tensor(total[:], placed[:, t0:t1], residual[:, t0:t1], ADD)
+            queue = nc.scalar if i % 2 == 0 else nc.sync
+            queue.dma_start(out=out[:, t0:t1], in_=total[:])

@@ -18,17 +18,13 @@ COPY = mybir.ActivationFunctionType.Copy
 P = 128
 PACK = 4
 
-CHUNKS = ((0, 768, 384, (512, 256)), (768, 512, 256, (512,)), (1280, 256, 160, (256,)))
-GROUPS = ((0, 1, 2, 3), (4, 5, 6, 7))
+CHUNKS = (
+    ((0, 1024, 640), (1024, 512, 320)),
+    ((0, 640, 0), (640, 640, 256), (1280, 256, 160)),
+)
+GROUP = 2
+SCATTERS = ((0, 256), (256, 1024))
 STORES = ((0, 512), (512, 1024), (1024, 1344), (1344, 1536))
-
-
-def interleaved(grouped, a, b):
-    return grouped[:, a:b, :].rearrange("p (c i) t -> p c t i", i=4)
-
-
-def by_rows(raw, a, b):
-    return raw[:, :, a:b].rearrange("p t (c i) -> p c t i", i=4)
 
 
 def tile_moe_res_lin_silu_kernel(tc, xT, xr, w_words, w_scales, b, gate, offs, out):
@@ -38,8 +34,6 @@ def tile_moe_res_lin_silu_kernel(tc, xT, xr, w_words, w_scales, b, gate, offs, o
         tc.psum_pool(name="psum", bufs=1) as psum,
     ):
         offsets = keep.tile([P, E * C // 16], U16, name="offsets")
-        words = keep.tile([P, T], U32, name="words", align_bytes=64)
-        scales = keep.tile([P, T], U8, name="scales", align_bytes=64)
         w_codes = keep.tile([P, E, 2 * N], U8, name="w_codes", align_bytes=64)
         w_bytes = keep.tile([P, E, N], U8, name="w_bytes", align_bytes=64)
         bias = keep.tile([P, E], F32, name="bias")
@@ -50,17 +44,17 @@ def tile_moe_res_lin_silu_kernel(tc, xT, xr, w_words, w_scales, b, gate, offs, o
         warmed = keep.tile([P, 1], F32, name="warmed")
 
         tokens = xT.rearrange("(p j) t -> p j t", j=PACK)
-        raws = []
-        for i, (t0, width, share, pieces) in enumerate(CHUNKS):
-            raw = keep.tile([P, PACK, width], F32, name=f"raw{i}")
-            nc.sync.dma_start(out=raw[:], in_=tokens[:, :, t0 : t0 + width])
-            raws.append(raw)
-
-        nc.sync.dma_start(offsets[:], offs)
+        raws = {}
+        for u, chunks in enumerate(CHUNKS):
+            for i, (t0, width, share) in enumerate(chunks):
+                raw = keep.tile([P, 2, width], F32, name=f"raw{u}_{i}")
+                nc.sync.dma_start(out=raw[:], in_=tokens[:, 2 * u : 2 * u + 2, t0 : t0 + width])
+                raws[u, i] = raw
+            if u == 0:
+                nc.sync.dma_start(offsets[:], offs)
 
         nc.vector.memset(warm[:], 0.0)
         nc.scalar.activation(warmed[:], warm[:], SILU)
-        nc.gpsimd.memset(scales[:], 0)
         nc.vector.memset(w_bytes[:].rearrange("p e n -> p (e n)").bitcast(I32), 0)
         nc.vector.memset(placed[:], 0.0)
 
@@ -74,30 +68,47 @@ def tile_moe_res_lin_silu_kernel(tc, xT, xr, w_words, w_scales, b, gate, offs, o
         nc.sync.dma_start(out=gates[:], in_=gate)
         nc.sync.dma_start(out=residual[:], in_=xr)
 
-        for i, (t0, width, share, pieces) in enumerate(CHUNKS):
-            grouped = keep.tile([P, width, PACK], BF16, name=f"grouped{i}", align_bytes=64)
-            nc.vector.tensor_copy(interleaved(grouped, 0, share), by_rows(raws[i], 0, share))
-            nc.scalar.activation(interleaved(grouped, share, width), by_rows(raws[i], share, width), COPY)
-            q0 = 0
-            for piece in pieces:
-                nc.vector.quantize_mx(
-                    out=words[:, t0 + q0 : t0 + q0 + piece].bitcast(FP8X4),
-                    scales=scales[:, t0 + q0 : t0 + q0 + piece],
-                    in_=grouped[:, q0 : q0 + piece, :].rearrange("p t j -> p (t j)"),
-                )
-                q0 += piece
+        width_g = GROUP * C
+        groups = range(E // GROUP)
+        halves = [keep.tile([P, 2, width_g], U32, name=f"halves{g}") for g in groups]
 
-        results = []
-        for g, experts in enumerate(GROUPS):
-            s0, s1 = experts[0] * C, (experts[-1] + 1) * C
-            listed = offsets[:, s0 // 16 : s1 // 16]
-            slot_words = keep.tile([P, s1 - s0], U32, name=f"slot_words{g}", align_bytes=64)
-            slot_scales = keep.tile([P, s1 - s0], U8, name=f"slot_scales{g}", align_bytes=64)
-            nc.vector.tensor_copy(slot_words[:], words[:].indirect(listed))
-            nc.vector.tensor_copy(slot_scales[:], scales[:].indirect(listed))
-            y = keep.tile([P, s1 - s0], F32, name=f"y{g}")
-            for e in experts:
-                cols = slice(e * C - s0, (e + 1) * C - s0)
+        for u, chunks in enumerate(CHUNKS):
+            pairs = keep.tile([P, T, 2], BF16, name=f"pairs{u}")
+            for i, (t0, width, share) in enumerate(chunks):
+                raw = raws[u, i]
+                if share:
+                    nc.vector.tensor_copy(pairs[:, t0 : t0 + share, :], raw[:, :, 0:share].rearrange("p j t -> p t j"))
+                nc.scalar.activation(
+                    pairs[:, t0 + share : t0 + width, :], raw[:, :, share:width].rearrange("p j t -> p t j"), COPY
+                )
+            window = pairs[:].rearrange("p t j -> p (t j)").bitcast(U32)
+            for g in groups:
+                listed = offsets[:, g * width_g // 16 : (g + 1) * width_g // 16]
+                nc.vector.tensor_copy(halves[g][:, u, :], window.indirect(listed))
+
+        grouped = []
+        for g in groups:
+            merged = keep.tile([P, width_g, 2], U32, name=f"merged{g}", align_bytes=64)
+            nc.scalar.copy(merged[:], halves[g][:].rearrange("p u s -> p s u"))
+            grouped.append(merged)
+
+        quantised = []
+        for g in groups:
+            slot_words = keep.tile([P, width_g], U32, name=f"slot_words{g}", align_bytes=64)
+            slot_scales = keep.tile([P, width_g], U8, name=f"slot_scales{g}", align_bytes=64)
+            nc.vector.quantize_mx(
+                out=slot_words[:].bitcast(FP8X4),
+                scales=slot_scales[:],
+                in_=grouped[g][:].rearrange("p s u -> p (s u)").bitcast(BF16),
+            )
+            quantised.append((slot_words, slot_scales))
+
+        y = keep.tile([P, E * C], F32, name="y")
+        for g in groups:
+            slot_words, slot_scales = quantised[g]
+            for i in range(GROUP):
+                e = g * GROUP + i
+                cols = slice(i * C, (i + 1) * C)
                 acc = psum.tile([P, C], F32, name=f"acc{e}")
                 nc.tensor.matmul_mx(
                     out=acc[:],
@@ -108,11 +119,10 @@ def tile_moe_res_lin_silu_kernel(tc, xT, xr, w_words, w_scales, b, gate, offs, o
                     start=True,
                     stop=True,
                 )
-                nc.scalar.activation(y[:, cols], acc[:], SILU, bias=bias[:, e : e + 1])
-            results.append((s0, s1, y))
+                nc.scalar.activation(y[:, e * C : (e + 1) * C], acc[:], SILU, bias=bias[:, e : e + 1])
 
-        for s0, s1, y in results:
-            nc.vector.tensor_tensor(placed[:].indirect(offsets[:, s0 // 16 : s1 // 16]), y[:], gates[:, s0:s1], MULT)
+        for s0, s1 in SCATTERS:
+            nc.vector.tensor_tensor(placed[:].indirect(offsets[:, s0 // 16 : s1 // 16]), y[:, s0:s1], gates[:, s0:s1], MULT)
 
         for i, (t0, t1) in enumerate(STORES):
             total = keep.tile([P, t1 - t0], F32, name=f"total{i}")

@@ -19,8 +19,8 @@ P = 128
 PACK = 4
 
 CHUNKS = (
-    ((0, 1024, 640), (1024, 512, 320)),
-    ((0, 640, 0), (640, 640, 256), (1280, 256, 160)),
+    ((0, 896, 544), (896, 384, 240), (1280, 256, 160)),
+    ((0, 384, 0), (384, 512, 0), (896, 384, 384), (1280, 256, 128)),
 )
 GROUP = 2
 SCATTERS = ((0, 256), (256, 1024))
@@ -70,7 +70,7 @@ def tile_moe_res_lin_silu_kernel(tc, xT, xr, w_words, w_scales, b, gate, offs, o
 
         width_g = GROUP * C
         groups = range(E // GROUP)
-        halves = [keep.tile([P, 2, width_g], U32, name=f"halves{g}") for g in groups]
+        halves = keep.tile([P, len(groups), 2, width_g], U32, name="halves")
 
         for u, chunks in enumerate(CHUNKS):
             pairs = keep.tile([P, T, 2], BF16, name=f"pairs{u}")
@@ -78,18 +78,22 @@ def tile_moe_res_lin_silu_kernel(tc, xT, xr, w_words, w_scales, b, gate, offs, o
                 raw = raws[u, i]
                 if share:
                     nc.vector.tensor_copy(pairs[:, t0 : t0 + share, :], raw[:, :, 0:share].rearrange("p j t -> p t j"))
-                nc.scalar.activation(
-                    pairs[:, t0 + share : t0 + width, :], raw[:, :, share:width].rearrange("p j t -> p t j"), COPY
-                )
+                if share < width:
+                    nc.scalar.activation(
+                        pairs[:, t0 + share : t0 + width, :], raw[:, :, share:width].rearrange("p j t -> p t j"), COPY
+                    )
             window = pairs[:].rearrange("p t j -> p (t j)").bitcast(U32)
-            for g in groups:
-                listed = offsets[:, g * width_g // 16 : (g + 1) * width_g // 16]
-                nc.vector.tensor_copy(halves[g][:, u, :], window.indirect(listed))
+            if u == 0:
+                nc.vector.tensor_copy(halves[:, :, u, :], window.indirect(offsets[:]))
+            else:
+                for g in groups:
+                    listed = offsets[:, g * width_g // 16 : (g + 1) * width_g // 16]
+                    nc.vector.tensor_copy(halves[:, g, u, :], window.indirect(listed))
 
         grouped = []
         for g in groups:
             merged = keep.tile([P, width_g, 2], U32, name=f"merged{g}", align_bytes=64)
-            nc.scalar.copy(merged[:], halves[g][:].rearrange("p u s -> p s u"))
+            nc.scalar.copy(merged[:], halves[:, g, :, :].rearrange("p u s -> p s u"))
             grouped.append(merged)
 
         quantised = []

@@ -19,8 +19,8 @@ P = 128
 PACK = 4
 
 CHUNKS = (
-    ((0, 896, 544), (896, 384, 240), (1280, 256, 160)),
-    ((0, 384, 0), (384, 512, 0), (896, 384, 384), (1280, 256, 128)),
+    ((0, 1024, 640), (1024, 512, 320)),
+    ((0, 512, 0), (512, 640, 448), (1152, 384, 256)),
 )
 GROUP = 2
 SCATTERS = ((0, 256), (256, 1024))
@@ -43,13 +43,14 @@ def tile_moe_res_lin_silu_kernel(tc, xT, xr, w_words, w_scales, b, gate, offs, o
         warm = keep.tile([P, 1], F32, name="warm")
         warmed = keep.tile([P, 1], F32, name="warmed")
 
-        tokens = xT.rearrange("(p j) t -> p j t", j=PACK)
-        raws = {}
+        tokens = xT.rearrange("(p j) t -> p (j t)", j=PACK)
+        raw = keep.tile([P, PACK * T], F32, name="raw")
         for u, chunks in enumerate(CHUNKS):
-            for i, (t0, width, share) in enumerate(chunks):
-                raw = keep.tile([P, 2, width], F32, name=f"raw{u}_{i}")
-                nc.sync.dma_start(out=raw[:], in_=tokens[:, 2 * u : 2 * u + 2, t0 : t0 + width])
-                raws[u, i] = raw
+            begin = 2 * u * T
+            for t0, width, share in chunks:
+                end = (2 * u + 1) * T + t0 + width
+                nc.sync.dma_start(out=raw[:, begin:end], in_=tokens[:, begin:end])
+                begin = end
             if u == 0:
                 nc.sync.dma_start(offsets[:], offs)
 
@@ -74,14 +75,12 @@ def tile_moe_res_lin_silu_kernel(tc, xT, xr, w_words, w_scales, b, gate, offs, o
 
         for u, chunks in enumerate(CHUNKS):
             pairs = keep.tile([P, T, 2], BF16, name=f"pairs{u}")
-            for i, (t0, width, share) in enumerate(chunks):
-                raw = raws[u, i]
+            rows = raw[:, 2 * u * T : (2 * u + 2) * T].rearrange("p (j t) -> p t j", j=2)
+            for t0, width, share in chunks:
                 if share:
-                    nc.vector.tensor_copy(pairs[:, t0 : t0 + share, :], raw[:, :, 0:share].rearrange("p j t -> p t j"))
+                    nc.vector.tensor_copy(pairs[:, t0 : t0 + share, :], rows[:, t0 : t0 + share, :])
                 if share < width:
-                    nc.scalar.activation(
-                        pairs[:, t0 + share : t0 + width, :], raw[:, :, share:width].rearrange("p j t -> p t j"), COPY
-                    )
+                    nc.scalar.activation(pairs[:, t0 + share : t0 + width, :], rows[:, t0 + share : t0 + width, :], COPY)
             window = pairs[:].rearrange("p t j -> p (t j)").bitcast(U32)
             if u == 0:
                 nc.vector.tensor_copy(halves[:, :, u, :], window.indirect(offsets[:]))

@@ -27,6 +27,10 @@ SCATTERS = ((0, 256), (256, 1024))
 STORES = ((0, 512), (512, 1024), (1024, 1344), (1344, 1536))
 
 
+def woven(ap):
+    return ap.rearrange("p (c i) j -> p c j i", i=4)
+
+
 def tile_moe_res_lin_silu_kernel(tc, xT, xr, w_words, w_scales, b, gate, offs, out):
     nc = tc.nc
     with (
@@ -78,9 +82,11 @@ def tile_moe_res_lin_silu_kernel(tc, xT, xr, w_words, w_scales, b, gate, offs, o
             rows = raw[:, 2 * u * T : (2 * u + 2) * T].rearrange("p (j t) -> p t j", j=2)
             for t0, width, share in chunks:
                 if share:
-                    nc.vector.tensor_copy(pairs[:, t0 : t0 + share, :], rows[:, t0 : t0 + share, :])
+                    nc.vector.tensor_copy(woven(pairs[:, t0 : t0 + share, :]), woven(rows[:, t0 : t0 + share, :]))
                 if share < width:
-                    nc.scalar.activation(pairs[:, t0 + share : t0 + width, :], rows[:, t0 + share : t0 + width, :], COPY)
+                    nc.scalar.activation(
+                        woven(pairs[:, t0 + share : t0 + width, :]), woven(rows[:, t0 + share : t0 + width, :]), COPY
+                    )
             window = pairs[:].rearrange("p t j -> p (t j)").bitcast(U32)
             if u == 0:
                 nc.vector.tensor_copy(halves[:, :, u, :], window.indirect(offsets[:]))
@@ -92,7 +98,7 @@ def tile_moe_res_lin_silu_kernel(tc, xT, xr, w_words, w_scales, b, gate, offs, o
         grouped = []
         for g in groups:
             merged = keep.tile([P, width_g, 2], U32, name=f"merged{g}", align_bytes=64)
-            nc.scalar.copy(merged[:], halves[:, g, :, :].rearrange("p u s -> p s u"))
+            nc.scalar.copy(woven(merged[:]), woven(halves[:, g, :, :].rearrange("p u s -> p s u")))
             grouped.append(merged)
 
         quantised = []

@@ -38,10 +38,11 @@ def tile_moe_res_lin_silu_kernel(tc, xT, xr, w_words, w_scales, b, gate, offs, o
         tc.psum_pool(name="psum", bufs=1) as psum,
     ):
         offsets = keep.tile([P, E * C // 16], U16, name="offsets")
-        w_codes = keep.tile([P, E, 2 * N], U8, name="w_codes", align_bytes=64)
+        w_first = keep.tile([P, GROUP, 2 * N], U8, name="w_first", align_bytes=64)
+        w_later = keep.tile([P, E - GROUP, 2 * N], U8, name="w_later", align_bytes=64)
         w_bytes = keep.tile([P, E, N], U8, name="w_bytes", align_bytes=64)
         bias = keep.tile([P, E], F32, name="bias")
-        gates = keep.tile([P, E * C], F32, name="gates")
+        gates = [keep.tile([P, s1 - s0], F32, name=f"gates{s0}") for s0, s1 in SCATTERS]
         residual = keep.tile([P, T], F32, name="residual")
         placed = keep.tile([P, T], F32, name="placed")
         warm = keep.tile([P, 1], F32, name="warm")
@@ -63,14 +64,17 @@ def tile_moe_res_lin_silu_kernel(tc, xT, xr, w_words, w_scales, b, gate, offs, o
         nc.vector.memset(w_bytes[:].rearrange("p e n -> p (e n)").bitcast(I32), 0)
         nc.vector.memset(placed[:], 0.0)
 
+        codes = w_words.rearrange("e a p n -> p (e a) n").bitcast(I32)
+        nc.sync.dma_start(out=w_first[:].bitcast(I32), in_=codes[:, 0:GROUP, :])
         for q in range(4):
             nc.sync.dma_start(
                 out=w_bytes[32 * q : 32 * q + 4, :, :].bitcast(I32),
                 in_=w_scales[:, 0, 4 * q : 4 * q + 4, :].rearrange("e q n -> q e n").bitcast(I32),
             )
-        nc.sync.dma_start(out=w_codes[:].bitcast(I32), in_=w_words.rearrange("e a p n -> p (e a) n").bitcast(I32))
         nc.sync.dma_start(out=bias[:], in_=b)
-        nc.sync.dma_start(out=gates[:], in_=gate)
+        nc.sync.dma_start(out=gates[0][:], in_=gate[:, SCATTERS[0][0] : SCATTERS[0][1]])
+        nc.sync.dma_start(out=w_later[:].bitcast(I32), in_=codes[:, GROUP:E, :])
+        nc.sync.dma_start(out=gates[1][:], in_=gate[:, SCATTERS[1][0] : SCATTERS[1][1]])
         nc.sync.dma_start(out=residual[:], in_=xr)
 
         width_g = GROUP * C
@@ -121,7 +125,7 @@ def tile_moe_res_lin_silu_kernel(tc, xT, xr, w_words, w_scales, b, gate, offs, o
                 acc = psum.tile([P, C], F32, name=f"acc{e}")
                 nc.tensor.matmul_mx(
                     out=acc[:],
-                    lhsT=w_codes[:, e, :].bitcast(FP4X4),
+                    lhsT=(w_first[:, e, :] if g == 0 else w_later[:, e - GROUP, :]).bitcast(FP4X4),
                     lhsT_scale=w_bytes[:, e, :],
                     rhs=slot_words[:, cols].bitcast(FP8X4),
                     rhs_scale=slot_scales[:, cols],
@@ -130,8 +134,8 @@ def tile_moe_res_lin_silu_kernel(tc, xT, xr, w_words, w_scales, b, gate, offs, o
                 )
                 nc.scalar.activation(y[:, e * C : (e + 1) * C], acc[:], SILU, bias=bias[:, e : e + 1])
 
-        for s0, s1 in SCATTERS:
-            nc.vector.tensor_tensor(placed[:].indirect(offsets[:, s0 // 16 : s1 // 16]), y[:, s0:s1], gates[:, s0:s1], MULT)
+        for (s0, s1), weight in zip(SCATTERS, gates):
+            nc.vector.tensor_tensor(placed[:].indirect(offsets[:, s0 // 16 : s1 // 16]), y[:, s0:s1], weight[:], MULT)
 
         for i, (t0, t1) in enumerate(STORES):
             total = keep.tile([P, t1 - t0], F32, name=f"total{i}")

@@ -19,12 +19,12 @@ P = 128
 PACK = 4
 
 CHUNKS = (
-    ((0, 1024, 640), (1024, 512, 320)),
-    ((0, 512, 0), (512, 640, 448), (1152, 384, 256)),
+    ((0, 896, 576), (896, 640, 416)),
+    ((0, 384, 0), (384, 640, 416), (1024, 512, 352)),
 )
 GROUP = 2
 SCATTERS = ((0, 256), (256, 1024))
-STORES = ((0, 512), (512, 1024), (1024, 1344), (1344, 1536))
+STORES = ((0, 128), (128, 384), (384, 768), (768, 1280), (1280, 1536))
 
 
 def woven(ap):

@@ -23,6 +23,7 @@ CHUNKS = (
     ((0, 384, 0), (384, 640, 416), (1024, 512, 352)),
 )
 GROUP = 2
+GATHERS = (((0, 1024),), ((0, 256), (256, 512), (512, 768), (768, 1024)))
 SCATTERS = ((0, 256), (256, 1024))
 STORES = ((0, 128), (128, 384), (384, 768), (768, 1280), (1280, 1536))
 
@@ -79,7 +80,7 @@ def tile_moe_res_lin_silu_kernel(tc, xT, xr, w_words, w_scales, b, gate, offs, o
 
         width_g = GROUP * C
         groups = range(E // GROUP)
-        halves = keep.tile([P, len(groups), 2, width_g], U32, name="halves")
+        halves = keep.tile([P, 2 * E * C], U32, name="halves")
 
         for u, chunks in enumerate(CHUNKS):
             pairs = keep.tile([P, T, 2], BF16, name=f"pairs{u}")
@@ -92,17 +93,16 @@ def tile_moe_res_lin_silu_kernel(tc, xT, xr, w_words, w_scales, b, gate, offs, o
                         woven(pairs[:, t0 + share : t0 + width, :]), woven(rows[:, t0 + share : t0 + width, :]), COPY
                     )
             window = pairs[:].rearrange("p t j -> p (t j)").bitcast(U32)
-            if u == 0:
-                nc.vector.tensor_copy(halves[:, :, u, :], window.indirect(offsets[:]))
-            else:
-                for g in groups:
-                    listed = offsets[:, g * width_g // 16 : (g + 1) * width_g // 16]
-                    nc.vector.tensor_copy(halves[:, g, u, :], window.indirect(listed))
+            for s0, s1 in GATHERS[u]:
+                nc.vector.tensor_copy(
+                    halves[:, u * E * C + s0 : u * E * C + s1], window.indirect(offsets[:, s0 // 16 : s1 // 16])
+                )
 
+        both = halves[:].rearrange("p (u s) -> p s u", u=2)
         grouped = []
         for g in groups:
             merged = keep.tile([P, width_g, 2], U32, name=f"merged{g}", align_bytes=64)
-            nc.scalar.copy(woven(merged[:]), woven(halves[:, g, :, :].rearrange("p u s -> p s u")))
+            nc.scalar.copy(woven(merged[:]), woven(both[:, g * width_g : (g + 1) * width_g, :]))
             grouped.append(merged)
 
         quantised = []

@@ -1,4 +1,5 @@
 import concourse.mybir as mybir
+from concourse.masks import make_identity
 
 K, T, E, C, N = 512, 1536, 8, 128, 128
 FLOPS = 2 * K * N * E * C
@@ -25,7 +26,8 @@ CHUNKS = (
 GROUP = 2
 GATHERS = (((0, 1024),), ((0, 256), (256, 512), (512, 768), (768, 1024)))
 SCATTERS = ((0, 256), (256, 1024))
-STORES = ((0, 128), (128, 384), (384, 768), (768, 1280), (1280, 1536))
+STORES = ((0, 192), (192, 512), (512, 1024), (1024, 1344), (1344, 1536))
+BANK = 512
 
 
 def woven(ap):
@@ -45,7 +47,8 @@ def tile_moe_res_lin_silu_kernel(tc, xT, xr, w_words, w_scales, b, gate, offs, o
         bias = keep.tile([P, E], F32, name="bias")
         gates = [keep.tile([P, s1 - s0], F32, name=f"gates{s0}") for s0, s1 in SCATTERS]
         residual = keep.tile([P, T], F32, name="residual")
-        placed = keep.tile([P, T], F32, name="placed")
+        placed = [keep.tile([P, T], F32, name=f"placed{s0}") for s0, s1 in SCATTERS]
+        ident = keep.tile([P, P], F32, name="ident")
         warm = keep.tile([P, 1], F32, name="warm")
         warmed = keep.tile([P, 1], F32, name="warmed")
 
@@ -63,7 +66,9 @@ def tile_moe_res_lin_silu_kernel(tc, xT, xr, w_words, w_scales, b, gate, offs, o
         nc.vector.memset(warm[:], 0.0)
         nc.scalar.activation(warmed[:], warm[:], SILU)
         nc.vector.memset(w_bytes[:].rearrange("p e n -> p (e n)").bitcast(I32), 0)
-        nc.vector.memset(placed[:], 0.0)
+        for tile in placed:
+            nc.vector.memset(tile[:], 0.0)
+        make_identity(nc, ident[:])
 
         codes = w_words.rearrange("e a p n -> p (e a) n").bitcast(I32)
         nc.sync.dma_start(out=w_first[:].bitcast(I32), in_=codes[:, 0:GROUP, :])
@@ -134,11 +139,29 @@ def tile_moe_res_lin_silu_kernel(tc, xT, xr, w_words, w_scales, b, gate, offs, o
                 )
                 nc.scalar.activation(y[:, e * C : (e + 1) * C], acc[:], SILU, bias=bias[:, e : e + 1])
 
-        for (s0, s1), weight in zip(SCATTERS, gates):
-            nc.vector.tensor_tensor(placed[:].indirect(offsets[:, s0 // 16 : s1 // 16]), y[:, s0:s1], weight[:], MULT)
+        for (s0, s1), weight, tile in zip(SCATTERS, gates, placed):
+            nc.vector.tensor_tensor(tile[:].indirect(offsets[:, s0 // 16 : s1 // 16]), y[:, s0:s1], weight[:], MULT)
+
+        turned = []
+        for k in range(T // BANK):
+            summed = psum.tile([P, BANK], F32, name=f"acc{k}")
+            for c0 in range(0, BANK, P):
+                cols = slice(k * BANK + c0, k * BANK + c0 + P)
+                nc.tensor.matmul(summed[:, c0 : c0 + P], residual[:, cols], ident[:], is_transpose=True, start=True, stop=False)
+                nc.tensor.matmul(summed[:, c0 : c0 + P], placed[0][:, cols], ident[:], is_transpose=True, start=False, stop=True)
+            by_token = keep.tile([P, BANK], F32, name=f"by_token{k}")
+            nc.scalar.copy(by_token[:], summed[:])
+            turned.append(by_token)
+        partial = []
+        for k in range(T // BANK):
+            back = psum.tile([P, BANK], F32, name=f"acc{T // BANK + k}")
+            for c0 in range(0, BANK, P):
+                nc.tensor.transpose(back[:, c0 : c0 + P], turned[k][:, c0 : c0 + P], ident[:])
+            partial.append(back)
 
         for i, (t0, t1) in enumerate(STORES):
             total = keep.tile([P, t1 - t0], F32, name=f"total{i}")
-            nc.vector.tensor_tensor(total[:], placed[:, t0:t1], residual[:, t0:t1], ADD)
+            k = t0 // BANK
+            nc.vector.tensor_tensor(total[:], placed[1][:, t0:t1], partial[k][:, t0 - k * BANK : t1 - k * BANK], ADD)
             queue = nc.scalar if i % 2 == 0 else nc.sync
             queue.dma_start(out=out[:, t0:t1], in_=total[:])

@@ -26,7 +26,7 @@ CHUNKS = (
 GROUP = 2
 GATHERS = (((0, 1024),), ((0, 256), (256, 512), (512, 768), (768, 1024)))
 SCATTERS = ((0, 256), (256, 1024))
-STORES = ((0, 192), (192, 512), (512, 1024), (1024, 1344), (1344, 1536))
+STORES = ((0, 128), (128, 384), (384, 640), (640, 1024), (1024, 1536))
 BANK = 512
 
 
@@ -153,15 +153,14 @@ def tile_moe_res_lin_silu_kernel(tc, xT, xr, w_words, w_scales, b, gate, offs, o
             nc.scalar.copy(by_token[:], summed[:])
             turned.append(by_token)
         partial = []
-        for k in range(T // BANK):
-            back = psum.tile([P, BANK], F32, name=f"acc{T // BANK + k}")
-            for c0 in range(0, BANK, P):
-                nc.tensor.transpose(back[:, c0 : c0 + P], turned[k][:, c0 : c0 + P], ident[:])
+        for i, (t0, t1) in enumerate(STORES):
+            back = psum.tile([P, t1 - t0], F32, name=f"acc{T // BANK + i}")
+            for c0 in range(t0, t1, P):
+                nc.tensor.transpose(back[:, c0 - t0 : c0 - t0 + P], turned[c0 // BANK][:, c0 % BANK : c0 % BANK + P], ident[:])
             partial.append(back)
 
         for i, (t0, t1) in enumerate(STORES):
             total = keep.tile([P, t1 - t0], F32, name=f"total{i}")
-            k = t0 // BANK
-            nc.vector.tensor_tensor(total[:], placed[1][:, t0:t1], partial[k][:, t0 - k * BANK : t1 - k * BANK], ADD)
+            nc.vector.tensor_tensor(total[:], placed[1][:, t0:t1], partial[i][:], ADD)
             queue = nc.scalar if i % 2 == 0 else nc.sync
             queue.dma_start(out=out[:, t0:t1], in_=total[:])

@@ -24,8 +24,7 @@ CHUNKS = (
     ((0, 384, 0), (384, 640, 416), (1024, 512, 352)),
 )
 GROUP = 2
-GATHERS = (((0, 1024),), ((0, 256), (256, 512), (512, 768), (768, 1024)))
-SCATTERS = ((0, 256), (256, 1024))
+GATES = ((832, 1024), (0, 832))
 STORES = ((0, 128), (128, 384), (384, 640), (640, 1024), (1024, 1536))
 BANK = 512
 
@@ -45,9 +44,9 @@ def tile_moe_res_lin_silu_kernel(tc, xT, xr, w_words, w_scales, b, gate, offs, o
         w_later = keep.tile([P, E - GROUP, 2 * N], U8, name="w_later", align_bytes=64)
         w_bytes = keep.tile([P, E, N], U8, name="w_bytes", align_bytes=64)
         bias = keep.tile([P, E], F32, name="bias")
-        gates = [keep.tile([P, s1 - s0], F32, name=f"gates{s0}") for s0, s1 in SCATTERS]
+        gates = [keep.tile([P, s1 - s0], F32, name=f"gates{s0}") for s0, s1 in GATES]
         residual = keep.tile([P, T], F32, name="residual")
-        placed = [keep.tile([P, T], F32, name=f"placed{s0}") for s0, s1 in SCATTERS]
+        placed = [keep.tile([P, T], F32, name=f"placed{s0}") for s0, s1 in GATES]
         ident = keep.tile([P, P], F32, name="ident")
         warm = keep.tile([P, 1], F32, name="warm")
         warmed = keep.tile([P, 1], F32, name="warmed")
@@ -71,22 +70,23 @@ def tile_moe_res_lin_silu_kernel(tc, xT, xr, w_words, w_scales, b, gate, offs, o
         make_identity(nc, ident[:])
 
         codes = w_words.rearrange("e a p n -> p (e a) n").bitcast(I32)
-        nc.sync.dma_start(out=w_first[:].bitcast(I32), in_=codes[:, 0:GROUP, :])
+        nc.sync.dma_start(out=bias[:], in_=b)
+        nc.sync.dma_start(out=gates[0][:], in_=gate[:, GATES[0][0] : GATES[0][1]])
+        nc.sync.dma_start(out=w_first[:].bitcast(I32), in_=codes[:, E - GROUP : E, :])
         for q in range(4):
             nc.sync.dma_start(
                 out=w_bytes[32 * q : 32 * q + 4, :, :].bitcast(I32),
                 in_=w_scales[:, 0, 4 * q : 4 * q + 4, :].rearrange("e q n -> q e n").bitcast(I32),
             )
-        nc.sync.dma_start(out=bias[:], in_=b)
-        nc.sync.dma_start(out=gates[0][:], in_=gate[:, SCATTERS[0][0] : SCATTERS[0][1]])
-        nc.sync.dma_start(out=w_later[:].bitcast(I32), in_=codes[:, GROUP:E, :])
-        nc.sync.dma_start(out=gates[1][:], in_=gate[:, SCATTERS[1][0] : SCATTERS[1][1]])
+        nc.sync.dma_start(out=w_later[:].bitcast(I32), in_=codes[:, 0 : E - GROUP, :])
+        nc.sync.dma_start(out=gates[1][:], in_=gate[:, GATES[1][0] : GATES[1][1]])
         nc.sync.dma_start(out=residual[:], in_=xr)
 
         width_g = GROUP * C
-        groups = range(E // GROUP)
-        halves = keep.tile([P, 2 * E * C], U32, name="halves")
+        halves = keep.tile([P, 8 * width_g], U32, name="halves")
+        blocks = halves[:].rearrange("p (b s) -> p b s", s=width_g)
 
+        windows = []
         for u, chunks in enumerate(CHUNKS):
             pairs = keep.tile([P, T, 2], BF16, name=f"pairs{u}")
             rows = raw[:, 2 * u * T : (2 * u + 2) * T].rearrange("p (j t) -> p t j", j=2)
@@ -97,40 +97,41 @@ def tile_moe_res_lin_silu_kernel(tc, xT, xr, w_words, w_scales, b, gate, offs, o
                     nc.scalar.activation(
                         woven(pairs[:, t0 + share : t0 + width, :]), woven(rows[:, t0 + share : t0 + width, :]), COPY
                     )
-            window = pairs[:].rearrange("p t j -> p (t j)").bitcast(U32)
-            for s0, s1 in GATHERS[u]:
-                nc.vector.tensor_copy(
-                    halves[:, u * E * C + s0 : u * E * C + s1], window.indirect(offsets[:, s0 // 16 : s1 // 16])
-                )
+            windows.append(pairs[:].rearrange("p t j -> p (t j)").bitcast(U32))
+            if u == 0:
+                nc.vector.tensor_copy(blocks[:, 0:8:2, :], windows[0].indirect(offsets[:]))
 
-        both = halves[:].rearrange("p (u s) -> p s u", u=2)
-        grouped = []
-        for g in groups:
-            merged = keep.tile([P, width_g, 2], U32, name=f"merged{g}", align_bytes=64)
-            nc.scalar.copy(woven(merged[:]), woven(both[:, g * width_g : (g + 1) * width_g, :]))
-            grouped.append(merged)
+        y = keep.tile([P, E * C], F32, name="y")
+        merged = {}
 
-        quantised = []
-        for g in groups:
+        def gather(g):
+            ring = 2 * g + 1 if g else 7
+            nc.vector.tensor_copy(
+                halves[:, ring * width_g : (ring + 1) * width_g],
+                windows[1].indirect(offsets[:, g * width_g // 16 : (g + 1) * width_g // 16]),
+            )
+
+        def merge(g):
+            ring = 2 * g + 1 if g else 7
+            both = blocks[:, 2 * g : ring + 1 : ring - 2 * g, :].rearrange("p u s -> p s u")
+            merged[g] = keep.tile([P, width_g, 2], U32, name=f"merged{g}" if g else "slot_words3", align_bytes=64)
+            nc.scalar.copy(woven(merged[g][:]), woven(both))
+
+        def experts(g):
             slot_words = keep.tile([P, width_g], U32, name=f"slot_words{g}", align_bytes=64)
             slot_scales = keep.tile([P, width_g], U8, name=f"slot_scales{g}", align_bytes=64)
             nc.vector.quantize_mx(
                 out=slot_words[:].bitcast(FP8X4),
                 scales=slot_scales[:],
-                in_=grouped[g][:].rearrange("p s u -> p (s u)").bitcast(BF16),
+                in_=merged[g][:].rearrange("p s u -> p (s u)").bitcast(BF16),
             )
-            quantised.append((slot_words, slot_scales))
-
-        y = keep.tile([P, E * C], F32, name="y")
-        for g in groups:
-            slot_words, slot_scales = quantised[g]
             for i in range(GROUP):
                 e = g * GROUP + i
                 cols = slice(i * C, (i + 1) * C)
                 acc = psum.tile([P, C], F32, name=f"acc{e}")
                 nc.tensor.matmul_mx(
                     out=acc[:],
-                    lhsT=(w_first[:, e, :] if g == 0 else w_later[:, e - GROUP, :]).bitcast(FP4X4),
+                    lhsT=(w_first[:, i, :] if g == 3 else w_later[:, e, :]).bitcast(FP4X4),
                     lhsT_scale=w_bytes[:, e, :],
                     rhs=slot_words[:, cols].bitcast(FP8X4),
                     rhs_scale=slot_scales[:, cols],
@@ -139,22 +140,45 @@ def tile_moe_res_lin_silu_kernel(tc, xT, xr, w_words, w_scales, b, gate, offs, o
                 )
                 nc.scalar.activation(y[:, e * C : (e + 1) * C], acc[:], SILU, bias=bias[:, e : e + 1])
 
-        for (s0, s1), weight, tile in zip(SCATTERS, gates, placed):
-            nc.vector.tensor_tensor(tile[:].indirect(offsets[:, s0 // 16 : s1 // 16]), y[:, s0:s1], weight[:], MULT)
+        def scatter(window, w, s0, s1):
+            nc.vector.tensor_tensor(
+                placed[window][:].indirect(offsets[:, s0 // 16 : s1 // 16]),
+                y[:, s0:s1],
+                gates[w][:, s0 - GATES[w][0] : s1 - GATES[w][0]],
+                MULT,
+            )
 
-        turned = []
-        for k in range(T // BANK):
-            summed = psum.tile([P, BANK], F32, name=f"acc{k}")
+        for g in (3, 2, 1):
+            gather(g)
+            merge(g)
+        experts(3)
+        gather(0)
+        merge(0)
+        experts(2)
+        experts(1)
+        scatter(0, 0, 832, 1024)
+        experts(0)
+        scatter(0, 1, 640, 832)
+        scatter(1, 1, 0, 640)
+
+        sums = []
+        for k, bank in enumerate((7, 6, 5)):
+            summed = psum.tile([P, BANK], F32, name=f"acc{bank}")
             for c0 in range(0, BANK, P):
                 cols = slice(k * BANK + c0, k * BANK + c0 + P)
-                nc.tensor.matmul(summed[:, c0 : c0 + P], residual[:, cols], ident[:], is_transpose=True, start=True, stop=False)
-                nc.tensor.matmul(summed[:, c0 : c0 + P], placed[0][:, cols], ident[:], is_transpose=True, start=False, stop=True)
+                nc.tensor.matmul(summed[:, c0 : c0 + P], residual[:, cols], ident[:], is_transpose=True, start=c0 == 0, stop=False)
+            sums.append(summed)
+        turned = []
+        for k, summed in enumerate(sums):
+            for c0 in range(0, BANK, P):
+                cols = slice(k * BANK + c0, k * BANK + c0 + P)
+                nc.tensor.matmul(summed[:, c0 : c0 + P], placed[0][:, cols], ident[:], is_transpose=True, start=False, stop=c0 == BANK - P)
             by_token = keep.tile([P, BANK], F32, name=f"by_token{k}")
             nc.scalar.copy(by_token[:], summed[:])
             turned.append(by_token)
         partial = []
         for i, (t0, t1) in enumerate(STORES):
-            back = psum.tile([P, t1 - t0], F32, name=f"acc{T // BANK + i}")
+            back = psum.tile([P, t1 - t0], F32, name=f"acc{4 - i}")
             for c0 in range(t0, t1, P):
                 nc.tensor.transpose(back[:, c0 - t0 : c0 - t0 + P], turned[c0 // BANK][:, c0 % BANK : c0 % BANK + P], ident[:])
             partial.append(back)

@@ -24,8 +24,10 @@ CHUNKS = (
     ((0, 384, 0), (384, 640, 416), (1024, 512, 352)),
 )
 GROUP = 2
-GATES = ((832, 1024), (0, 832))
-STORES = ((0, 128), (128, 384), (384, 640), (640, 1024), (1024, 1536))
+GATES = ((576, 1024), (0, 576))
+STORES = ((0, 192), (704, 960), (192, 704), (960, 1536))
+SIDE = (192, 512)
+BANK_OF = (1, 0, 4, 4, 3, 2, 1, 0)
 BANK = 512
 
 
@@ -45,7 +47,7 @@ def tile_moe_res_lin_silu_kernel(tc, xT, xr, w_words, w_scales, b, gate, offs, o
         w_bytes = keep.tile([P, E, N], U8, name="w_bytes", align_bytes=64)
         bias = keep.tile([P, E], F32, name="bias")
         gates = [keep.tile([P, s1 - s0], F32, name=f"gates{s0}") for s0, s1 in GATES]
-        residual = keep.tile([P, T], F32, name="residual")
+        residual = [keep.tile([P, BANK], F32, name=f"residual{k}") for k in range(T // BANK)]
         placed = [keep.tile([P, T], F32, name=f"placed{s0}") for s0, s1 in GATES]
         ident = keep.tile([P, P], F32, name="ident")
         warm = keep.tile([P, 1], F32, name="warm")
@@ -79,8 +81,10 @@ def tile_moe_res_lin_silu_kernel(tc, xT, xr, w_words, w_scales, b, gate, offs, o
                 in_=w_scales[:, 0, 4 * q : 4 * q + 4, :].rearrange("e q n -> q e n").bitcast(I32),
             )
         nc.sync.dma_start(out=w_later[:].bitcast(I32), in_=codes[:, 0 : E - GROUP, :])
-        nc.sync.dma_start(out=gates[1][:], in_=gate[:, GATES[1][0] : GATES[1][1]])
-        nc.sync.dma_start(out=residual[:], in_=xr)
+        for k in range(T // BANK):
+            if k == 2:
+                nc.sync.dma_start(out=gates[1][:], in_=gate[:, GATES[1][0] : GATES[1][1]])
+            nc.sync.dma_start(out=residual[k][:], in_=xr[:, k * BANK : (k + 1) * BANK])
 
         width_g = GROUP * C
         halves = keep.tile([P, 8 * width_g], U32, name="halves")
@@ -125,12 +129,13 @@ def tile_moe_res_lin_silu_kernel(tc, xT, xr, w_words, w_scales, b, gate, offs, o
                 scales=slot_scales[:],
                 in_=merged[g][:].rearrange("p s u -> p (s u)").bitcast(BF16),
             )
-            for i in range(GROUP):
+            shared = psum.tile([P, GROUP * C], F32, name="acc4") if g == 1 else None
+            for i in reversed(range(GROUP)):
                 e = g * GROUP + i
                 cols = slice(i * C, (i + 1) * C)
-                acc = psum.tile([P, C], F32, name=f"acc{e}")
+                acc = shared[:, cols] if g == 1 else psum.tile([P, C], F32, name=f"acc{BANK_OF[e]}")[:]
                 nc.tensor.matmul_mx(
-                    out=acc[:],
+                    out=acc,
                     lhsT=(w_first[:, i, :] if g == 3 else w_later[:, e, :]).bitcast(FP4X4),
                     lhsT_scale=w_bytes[:, e, :],
                     rhs=slot_words[:, cols].bitcast(FP8X4),
@@ -138,7 +143,7 @@ def tile_moe_res_lin_silu_kernel(tc, xT, xr, w_words, w_scales, b, gate, offs, o
                     start=True,
                     stop=True,
                 )
-                nc.scalar.activation(y[:, e * C : (e + 1) * C], acc[:], SILU, bias=bias[:, e : e + 1])
+                nc.scalar.activation(y[:, e * C : (e + 1) * C], acc, SILU, bias=bias[:, e : e + 1])
 
         def scatter(window, w, s0, s1):
             nc.vector.tensor_tensor(
@@ -158,33 +163,46 @@ def tile_moe_res_lin_silu_kernel(tc, xT, xr, w_words, w_scales, b, gate, offs, o
         experts(1)
         scatter(0, 0, 832, 1024)
         experts(0)
-        scatter(0, 1, 640, 832)
-        scatter(1, 1, 0, 640)
+        scatter(0, 0, 576, 832)
+        scatter(1, 1, 0, 576)
 
-        sums = []
-        for k, bank in enumerate((7, 6, 5)):
-            summed = psum.tile([P, BANK], F32, name=f"acc{bank}")
+        def turn(summed, source, first):
             for c0 in range(0, BANK, P):
-                cols = slice(k * BANK + c0, k * BANK + c0 + P)
-                nc.tensor.matmul(summed[:, c0 : c0 + P], residual[:, cols], ident[:], is_transpose=True, start=c0 == 0, stop=False)
-            sums.append(summed)
+                nc.tensor.matmul(
+                    summed[:, c0 : c0 + P], source[:, c0 : c0 + P], ident[:], is_transpose=True,
+                    start=first and c0 == 0, stop=not first and c0 == BANK - P,
+                )
+
+        sums = [psum.tile([P, BANK], F32, name=f"acc{bank}") for bank in (5, 6, 7)]
+        for k in range(3):
+            turn(sums[k], residual[k][:], True)
         turned = []
         for k, summed in enumerate(sums):
-            for c0 in range(0, BANK, P):
-                cols = slice(k * BANK + c0, k * BANK + c0 + P)
-                nc.tensor.matmul(summed[:, c0 : c0 + P], placed[0][:, cols], ident[:], is_transpose=True, start=False, stop=c0 == BANK - P)
+            turn(summed, placed[0][:, k * BANK : (k + 1) * BANK], False)
             by_token = keep.tile([P, BANK], F32, name=f"by_token{k}")
             nc.scalar.copy(by_token[:], summed[:])
             turned.append(by_token)
         partial = []
-        for i, (t0, t1) in enumerate(STORES):
-            back = psum.tile([P, t1 - t0], F32, name=f"acc{4 - i}")
-            for c0 in range(t0, t1, P):
-                nc.tensor.transpose(back[:, c0 - t0 : c0 - t0 + P], turned[c0 // BANK][:, c0 % BANK : c0 % BANK + P], ident[:])
+        for k, by_token in enumerate(turned):
+            back = psum.tile([P, BANK], F32, name=f"acc{2 + k}")
+            for c0 in range(0, BANK, P):
+                nc.tensor.transpose(back[:, c0 : c0 + P], by_token[:, c0 : c0 + P], ident[:])
             partial.append(back)
 
+        side = keep.tile([P, SIDE[1] - SIDE[0]], F32, name="side")
+        nc.scalar.copy(side[:], partial[0][:, SIDE[0] : SIDE[1]])
         for i, (t0, t1) in enumerate(STORES):
             total = keep.tile([P, t1 - t0], F32, name=f"total{i}")
-            nc.vector.tensor_tensor(total[:], placed[1][:, t0:t1], partial[i][:], ADD)
-            queue = nc.scalar if i % 2 == 0 else nc.sync
+            begin = t0
+            if t0 == SIDE[0]:
+                nc.gpsimd.tensor_tensor(total[:, 0 : SIDE[1] - t0], placed[1][:, t0 : SIDE[1]], side[:], ADD)
+                begin = SIDE[1]
+            while begin < t1:
+                end = min(t1, (begin // BANK + 1) * BANK)
+                k = begin // BANK
+                nc.vector.tensor_tensor(
+                    total[:, begin - t0 : end - t0], placed[1][:, begin:end], partial[k][:, begin - k * BANK : end - k * BANK], ADD
+                )
+                begin = end
+            queue = nc.scalar if i == len(STORES) - 1 else nc.sync
             queue.dma_start(out=out[:, t0:t1], in_=total[:])

@@ -21,13 +21,12 @@ PACK = 4
 
 CHUNKS = (
     ((0, 896, 576), (896, 640, 416)),
-    ((0, 384, 0), (384, 640, 416), (1024, 512, 352)),
+    ((0, 448, 0), (448, 704, 496), (1152, 384, 256)),
 )
 GROUP = 2
-GATES = ((576, 1024), (0, 576))
+GATES = ((640, 1024), (0, 640))
 STORES = ((0, 192), (704, 960), (192, 704), (960, 1536))
 SIDE = (192, 512)
-BANK_OF = (1, 0, 4, 4, 3, 2, 1, 0)
 BANK = 512
 
 
@@ -82,9 +81,8 @@ def tile_moe_res_lin_silu_kernel(tc, xT, xr, w_words, w_scales, b, gate, offs, o
             )
         nc.sync.dma_start(out=w_later[:].bitcast(I32), in_=codes[:, 0 : E - GROUP, :])
         for k in range(T // BANK):
-            if k == 2:
-                nc.sync.dma_start(out=gates[1][:], in_=gate[:, GATES[1][0] : GATES[1][1]])
             nc.sync.dma_start(out=residual[k][:], in_=xr[:, k * BANK : (k + 1) * BANK])
+        nc.sync.dma_start(out=gates[1][:], in_=gate[:, GATES[1][0] : GATES[1][1]])
 
         width_g = GROUP * C
         halves = keep.tile([P, 8 * width_g], U32, name="halves")
@@ -129,11 +127,10 @@ def tile_moe_res_lin_silu_kernel(tc, xT, xr, w_words, w_scales, b, gate, offs, o
                 scales=slot_scales[:],
                 in_=merged[g][:].rearrange("p s u -> p (s u)").bitcast(BF16),
             )
-            shared = psum.tile([P, GROUP * C], F32, name="acc4") if g == 1 else None
             for i in reversed(range(GROUP)):
                 e = g * GROUP + i
                 cols = slice(i * C, (i + 1) * C)
-                acc = shared[:, cols] if g == 1 else psum.tile([P, C], F32, name=f"acc{BANK_OF[e]}")[:]
+                acc = psum.tile([P, C], F32, name=f"acc{e}")[:]
                 nc.tensor.matmul_mx(
                     out=acc,
                     lhsT=(w_first[:, i, :] if g == 3 else w_later[:, e, :]).bitcast(FP4X4),
@@ -163,8 +160,8 @@ def tile_moe_res_lin_silu_kernel(tc, xT, xr, w_words, w_scales, b, gate, offs, o
         experts(1)
         scatter(0, 0, 832, 1024)
         experts(0)
-        scatter(0, 0, 576, 832)
-        scatter(1, 1, 0, 576)
+        scatter(0, 0, 640, 832)
+        scatter(1, 1, 0, 640)
 
         def turn(summed, source, first):
             for c0 in range(0, BANK, P):
@@ -173,7 +170,7 @@ def tile_moe_res_lin_silu_kernel(tc, xT, xr, w_words, w_scales, b, gate, offs, o
                     start=first and c0 == 0, stop=not first and c0 == BANK - P,
                 )
 
-        sums = [psum.tile([P, BANK], F32, name=f"acc{bank}") for bank in (5, 6, 7)]
+        sums = [psum.tile([P, BANK], F32, name=f"acc{bank}") for bank in (7, 6, 1)]
         for k in range(3):
             turn(sums[k], residual[k][:], True)
         turned = []
@@ -184,7 +181,7 @@ def tile_moe_res_lin_silu_kernel(tc, xT, xr, w_words, w_scales, b, gate, offs, o
             turned.append(by_token)
         partial = []
         for k, by_token in enumerate(turned):
-            back = psum.tile([P, BANK], F32, name=f"acc{2 + k}")
+            back = psum.tile([P, BANK], F32, name=f"acc{5 - k}")
             for c0 in range(0, BANK, P):
                 nc.tensor.transpose(back[:, c0 : c0 + P], by_token[:, c0 : c0 + P], ident[:])
             partial.append(back)

@@ -24,10 +24,11 @@ CHUNKS = (
     ((0, 448, 0), (448, 704, 496), (1152, 384, 256)),
 )
 GROUP = 2
-GATES = ((640, 1024), (0, 640))
+GATES = ((608, 1024), (0, 608))
 STORES = ((0, 192), (704, 960), (192, 704), (960, 1536))
 SIDE = (192, 512)
 BANK = 512
+RUN = 128
 
 
 def woven(ap):
@@ -85,8 +86,11 @@ def tile_moe_res_lin_silu_kernel(tc, xT, xr, w_words, w_scales, b, gate, offs, o
         nc.sync.dma_start(out=gates[1][:], in_=gate[:, GATES[1][0] : GATES[1][1]])
 
         width_g = GROUP * C
-        halves = keep.tile([P, 8 * width_g], U32, name="halves")
-        blocks = halves[:].rearrange("p (b s) -> p b s", s=width_g)
+        halves = keep.tile([P, 3072], U32, name="halves")
+        runs = halves[:].rearrange("p (n s) -> p n s", s=RUN)
+
+        def listed(s0, s1):
+            return offsets[:, s0 // 16 : s1 // 16]
 
         windows = []
         for u, chunks in enumerate(CHUNKS):
@@ -101,39 +105,40 @@ def tile_moe_res_lin_silu_kernel(tc, xT, xr, w_words, w_scales, b, gate, offs, o
                     )
             windows.append(pairs[:].rearrange("p t j -> p (t j)").bitcast(U32))
             if u == 0:
-                nc.vector.tensor_copy(blocks[:, 0:8:2, :], windows[0].indirect(offsets[:]))
+                nc.vector.tensor_copy(runs[:, 0:16:2, :], windows[0].indirect(offsets[:]))
 
         y = keep.tile([P, E * C], F32, name="y")
-        merged = {}
+        first = keep.tile([P, 2 * width_g], U32, name="first", align_bytes=64)
+        middle = keep.tile([P, 3 * width_g], U32, name="middle", align_bytes=64)
 
-        def gather(g):
-            ring = 2 * g + 1 if g else 7
-            nc.vector.tensor_copy(
-                halves[:, ring * width_g : (ring + 1) * width_g],
-                windows[1].indirect(offsets[:, g * width_g // 16 : (g + 1) * width_g // 16]),
-            )
+        def gather(s0, s1, at):
+            nc.vector.tensor_copy(runs[:, at : at + 2 * (s1 - s0) // RUN - 1 : 2, :], windows[1].indirect(listed(s0, s1)))
 
-        def merge(g):
-            ring = 2 * g + 1 if g else 7
-            both = blocks[:, 2 * g : ring + 1 : ring - 2 * g, :].rearrange("p u s -> p s u")
-            merged[g] = keep.tile([P, width_g, 2], U32, name=f"merged{g}" if g else "slot_words3", align_bytes=64)
-            nc.scalar.copy(woven(merged[g][:]), woven(both))
+        def merge(into, slot, s0, s1, at):
+            low, count = 2 * s0 // RUN, (s1 - s0) // RUN
+            if at == low + 1:
+                both = runs[:, low : low + 2 * count, :].rearrange("p (b u) (c i) -> p b c u i", u=2, i=4)
+            else:
+                far = runs[:, low : 2 * at - low, :].rearrange("p (u b h) s -> p u b h s", u=2, h=2)
+                both = far[:, :, 0:count, 0, :].rearrange("p u b (c i) -> p b c u i", i=4)
+            words = into[:, 2 * slot : 2 * (slot + s1 - s0)].rearrange("p (b c i u) -> p b c u i", b=count, i=4, u=2)
+            nc.scalar.copy(words, both)
 
-        def experts(g):
-            slot_words = keep.tile([P, width_g], U32, name=f"slot_words{g}", align_bytes=64)
-            slot_scales = keep.tile([P, width_g], U8, name=f"slot_scales{g}", align_bytes=64)
+        def experts(e0, count, merged):
+            slot_words = keep.tile([P, count * C], U32, name=f"slot_words{e0}", align_bytes=64)
+            slot_scales = keep.tile([P, count * C], U8, name=f"slot_scales{e0}", align_bytes=64)
             nc.vector.quantize_mx(
                 out=slot_words[:].bitcast(FP8X4),
                 scales=slot_scales[:],
-                in_=merged[g][:].rearrange("p s u -> p (s u)").bitcast(BF16),
+                in_=merged.bitcast(BF16),
             )
-            for i in reversed(range(GROUP)):
-                e = g * GROUP + i
+            for i in reversed(range(count)):
+                e = e0 + i
                 cols = slice(i * C, (i + 1) * C)
                 acc = psum.tile([P, C], F32, name=f"acc{e}")[:]
                 nc.tensor.matmul_mx(
                     out=acc,
-                    lhsT=(w_first[:, i, :] if g == 3 else w_later[:, e, :]).bitcast(FP4X4),
+                    lhsT=(w_first[:, i, :] if e0 == E - GROUP else w_later[:, e, :]).bitcast(FP4X4),
                     lhsT_scale=w_bytes[:, e, :],
                     rhs=slot_words[:, cols].bitcast(FP8X4),
                     rhs_scale=slot_scales[:, cols],
@@ -150,18 +155,21 @@ def tile_moe_res_lin_silu_kernel(tc, xT, xr, w_words, w_scales, b, gate, offs, o
                 MULT,
             )
 
-        for g in (3, 2, 1):
-            gather(g)
-            merge(g)
-        experts(3)
-        gather(0)
-        merge(0)
-        experts(2)
-        experts(1)
+        gather(768, 1024, 13)
+        merge(first, 0, 768, 1024, 13)
+        gather(384, 768, 7)
+        merge(middle, 0, 384, 768, 7)
+        experts(6, 2, first[:])
+        gather(0, 384, 12)
+        last = keep.tile([P, 3 * width_g], U32, name="slot_words6", align_bytes=64)
+        merge(last, 0, 0, 384, 12)
+        experts(4, 2, middle[:, 256:768])
+        experts(3, 1, middle[:, 0:256])
         scatter(0, 0, 832, 1024)
-        experts(0)
-        scatter(0, 0, 640, 832)
-        scatter(1, 1, 0, 640)
+        experts(0, 2, last[:, 0:512])
+        experts(2, 1, last[:, 512:768])
+        scatter(0, 0, 608, 832)
+        scatter(1, 1, 0, 608)
 
         def turn(summed, source, first):
             for c0 in range(0, BANK, P):

@@ -21,7 +21,7 @@ PACK = 4
 
 CHUNKS = (
     ((0, 896, 576), (896, 640, 416)),
-    ((0, 448, 0), (448, 704, 496), (1152, 384, 256)),
+    ((0, 448, 0), (448, 704, 496), (1152, 384, 224)),
 )
 GROUP = 2
 GATES = ((608, 1024), (0, 608))
@@ -80,9 +80,10 @@ def tile_moe_res_lin_silu_kernel(tc, xT, xr, w_words, w_scales, b, gate, offs, o
                 out=w_bytes[32 * q : 32 * q + 4, :, :].bitcast(I32),
                 in_=w_scales[:, 0, 4 * q : 4 * q + 4, :].rearrange("e q n -> q e n").bitcast(I32),
             )
-        nc.sync.dma_start(out=w_later[:].bitcast(I32), in_=codes[:, 0 : E - GROUP, :])
         for k in range(T // BANK):
             nc.sync.dma_start(out=residual[k][:], in_=xr[:, k * BANK : (k + 1) * BANK])
+            if k == 0:
+                nc.sync.dma_start(out=w_later[:].bitcast(I32), in_=codes[:, 0 : E - GROUP, :])
         nc.sync.dma_start(out=gates[1][:], in_=gate[:, GATES[1][0] : GATES[1][1]])
 
         width_g = GROUP * C
@@ -138,7 +139,7 @@ def tile_moe_res_lin_silu_kernel(tc, xT, xr, w_words, w_scales, b, gate, offs, o
                 acc = psum.tile([P, C], F32, name=f"acc{e}")[:]
                 nc.tensor.matmul_mx(
                     out=acc,
-                    lhsT=(w_first[:, i, :] if e0 == E - GROUP else w_later[:, e, :]).bitcast(FP4X4),
+                    lhsT=(w_first[:, e - E + GROUP, :] if e >= E - GROUP else w_later[:, e, :]).bitcast(FP4X4),
                     lhsT_scale=w_bytes[:, e, :],
                     rhs=slot_words[:, cols].bitcast(FP8X4),
                     rhs_scale=slot_scales[:, cols],
@@ -156,10 +157,12 @@ def tile_moe_res_lin_silu_kernel(tc, xT, xr, w_words, w_scales, b, gate, offs, o
             )
 
         gather(768, 1024, 13)
-        merge(first, 0, 768, 1024, 13)
+        merge(first, 128, 896, 1024, 15)
+        merge(first, 0, 768, 896, 13)
         gather(384, 768, 7)
         merge(middle, 0, 384, 768, 7)
-        experts(6, 2, first[:])
+        experts(7, 1, first[:, 256:512])
+        experts(6, 1, first[:, 0:256])
         gather(0, 384, 12)
         last = keep.tile([P, 3 * width_g], U32, name="slot_words6", align_bytes=64)
         merge(last, 0, 0, 384, 12)

@@ -20,8 +20,8 @@ P = 128
 PACK = 4
 
 CHUNKS = (
-    ((0, 896, 576), (896, 640, 416)),
-    ((0, 448, 0), (448, 704, 496), (1152, 384, 224)),
+    ((0, 1024, 672), (1024, 512, 336)),
+    ((0, 640, 0), (640, 576, 400), (1216, 320, 192)),
 )
 GROUP = 2
 GATES = ((608, 1024), (0, 608))
@@ -53,14 +53,18 @@ def tile_moe_res_lin_silu_kernel(tc, xT, xr, w_words, w_scales, b, gate, offs, o
         warm = keep.tile([P, 1], F32, name="warm")
         warmed = keep.tile([P, 1], F32, name="warmed")
 
-        tokens = xT.rearrange("(p j) t -> p (j t)", j=PACK)
-        raw = keep.tile([P, PACK * T], F32, name="raw")
+        tokens = xT.rearrange("(p j) t -> p j t", j=PACK)
+        raw = {}
         for u, chunks in enumerate(CHUNKS):
-            begin = 2 * u * T
             for t0, width, share in chunks:
-                end = (2 * u + 1) * T + t0 + width
-                nc.sync.dma_start(out=raw[:, begin:end], in_=tokens[:, begin:end])
-                begin = end
+                raw[u, t0] = keep.tile([P, 2 * width], F32, name=f"raw{u}_{t0}")
+                if u == 0 or t0 == 0:
+                    nc.sync.dma_start(out=raw[u, t0][:, 0:width], in_=tokens[:, 2 * u, t0 : t0 + width])
+                    nc.scalar.dma_start(out=raw[u, t0][:, width : 2 * width], in_=tokens[:, 2 * u + 1, t0 : t0 + width])
+                else:
+                    nc.sync.dma_start(
+                        out=raw[u, t0][:].rearrange("p (j t) -> p j t", j=2), in_=tokens[:, 2 * u : 2 * u + 2, t0 : t0 + width]
+                    )
             if u == 0:
                 nc.sync.dma_start(offsets[:], offs)
 
@@ -96,13 +100,13 @@ def tile_moe_res_lin_silu_kernel(tc, xT, xr, w_words, w_scales, b, gate, offs, o
         windows = []
         for u, chunks in enumerate(CHUNKS):
             pairs = keep.tile([P, T, 2], BF16, name=f"pairs{u}")
-            rows = raw[:, 2 * u * T : (2 * u + 2) * T].rearrange("p (j t) -> p t j", j=2)
             for t0, width, share in chunks:
+                rows = raw[u, t0][:].rearrange("p (j t) -> p t j", j=2)
                 if share:
-                    nc.vector.tensor_copy(woven(pairs[:, t0 : t0 + share, :]), woven(rows[:, t0 : t0 + share, :]))
+                    nc.vector.tensor_copy(woven(pairs[:, t0 : t0 + share, :]), woven(rows[:, 0:share, :]))
                 if share < width:
                     nc.scalar.activation(
-                        woven(pairs[:, t0 + share : t0 + width, :]), woven(rows[:, t0 + share : t0 + width, :]), COPY
+                        woven(pairs[:, t0 + share : t0 + width, :]), woven(rows[:, share:width, :]), COPY
                     )
             windows.append(pairs[:].rearrange("p t j -> p (t j)").bitcast(U32))
             if u == 0:

@@ -21,7 +21,7 @@ PACK = 4
 
 CHUNKS = (
     ((0, 1024, 672), (1024, 512, 336)),
-    ((0, 640, 0), (640, 576, 400), (1216, 320, 192)),
+    ((0, 896, 256), (896, 640, 416)),
 )
 GROUP = 2
 GATES = ((608, 1024), (0, 608))
@@ -57,13 +57,17 @@ def tile_moe_res_lin_silu_kernel(tc, xT, xr, w_words, w_scales, b, gate, offs, o
         raw = {}
         for u, chunks in enumerate(CHUNKS):
             for t0, width, share in chunks:
-                raw[u, t0] = keep.tile([P, 2 * width], F32, name=f"raw{u}_{t0}")
+                columns = T if (u, t0) == (0, 1024) else 2 * width
+                holder = keep.tile([P, columns], F32, name=f"raw{u}_{t0}")
+                raw[u, t0] = holder[:, 0 : 2 * width]
+                if columns == T:
+                    reused = holder
                 if u == 0 or t0 == 0:
                     nc.sync.dma_start(out=raw[u, t0][:, 0:width], in_=tokens[:, 2 * u, t0 : t0 + width])
                     nc.scalar.dma_start(out=raw[u, t0][:, width : 2 * width], in_=tokens[:, 2 * u + 1, t0 : t0 + width])
                 else:
                     nc.sync.dma_start(
-                        out=raw[u, t0][:].rearrange("p (j t) -> p j t", j=2), in_=tokens[:, 2 * u : 2 * u + 2, t0 : t0 + width]
+                        out=raw[u, t0].rearrange("p (j t) -> p j t", j=2), in_=tokens[:, 2 * u : 2 * u + 2, t0 : t0 + width]
                     )
             if u == 0:
                 nc.sync.dma_start(offsets[:], offs)
@@ -99,16 +103,18 @@ def tile_moe_res_lin_silu_kernel(tc, xT, xr, w_words, w_scales, b, gate, offs, o
 
         windows = []
         for u, chunks in enumerate(CHUNKS):
-            pairs = keep.tile([P, T, 2], BF16, name=f"pairs{u}")
+            if u == 0:
+                reused_or_new = keep.tile([P, T], F32, name="pairs0")
+            else:
+                reused_or_new = reused
+            pairs = reused_or_new[:].bitcast(BF16).rearrange("p (t j) -> p t j", j=2)
             for t0, width, share in chunks:
-                rows = raw[u, t0][:].rearrange("p (j t) -> p t j", j=2)
+                rows = raw[u, t0].rearrange("p (j t) -> p t j", j=2)
+                cut = width - share
                 if share:
-                    nc.vector.tensor_copy(woven(pairs[:, t0 : t0 + share, :]), woven(rows[:, 0:share, :]))
-                if share < width:
-                    nc.scalar.activation(
-                        woven(pairs[:, t0 + share : t0 + width, :]), woven(rows[:, share:width, :]), COPY
-                    )
-            windows.append(pairs[:].rearrange("p t j -> p (t j)").bitcast(U32))
+                    nc.vector.tensor_copy(woven(pairs[:, t0 + cut : t0 + width, :]), woven(rows[:, cut:width, :]))
+                nc.scalar.activation(woven(pairs[:, t0 : t0 + cut, :]), woven(rows[:, 0:cut, :]), COPY)
+            windows.append(reused_or_new[:].bitcast(U32))
             if u == 0:
                 nc.vector.tensor_copy(runs[:, 0:16:2, :], windows[0].indirect(offsets[:]))
 

@@ -59,16 +59,11 @@ def tile_moe_res_lin_silu_kernel(tc, xT, xr, w_words, w_scales, b, gate, offs, o
             for t0, width, share in chunks:
                 columns = T if (u, t0) == (0, 1024) else 2 * width
                 holder = keep.tile([P, columns], F32, name=f"raw{u}_{t0}")
-                raw[u, t0] = holder[:, 0 : 2 * width]
+                raw[u, t0] = holder[:, columns - 2 * width : columns]
                 if columns == T:
                     reused = holder
-                if u == 0 or t0 == 0:
-                    nc.sync.dma_start(out=raw[u, t0][:, 0:width], in_=tokens[:, 2 * u, t0 : t0 + width])
-                    nc.scalar.dma_start(out=raw[u, t0][:, width : 2 * width], in_=tokens[:, 2 * u + 1, t0 : t0 + width])
-                else:
-                    nc.sync.dma_start(
-                        out=raw[u, t0].rearrange("p (j t) -> p j t", j=2), in_=tokens[:, 2 * u : 2 * u + 2, t0 : t0 + width]
-                    )
+                nc.sync.dma_start(out=raw[u, t0][:, 0:width], in_=tokens[:, 2 * u, t0 : t0 + width])
+                nc.scalar.dma_start(out=raw[u, t0][:, width : 2 * width], in_=tokens[:, 2 * u + 1, t0 : t0 + width])
             if u == 0:
                 nc.sync.dma_start(offsets[:], offs)
 

@@ -21,7 +21,7 @@ PACK = 4
 
 CHUNKS = (
     ((0, 1024, 672), (1024, 512, 336)),
-    ((0, 896, 256), (896, 640, 416)),
+    ((0, 768, 128), (768, 512, 336), (1280, 256, 160)),
 )
 GROUP = 2
 GATES = ((608, 1024), (0, 608))
@@ -47,25 +47,34 @@ def tile_moe_res_lin_silu_kernel(tc, xT, xr, w_words, w_scales, b, gate, offs, o
         w_bytes = keep.tile([P, E, N], U8, name="w_bytes", align_bytes=64)
         bias = keep.tile([P, E], F32, name="bias")
         gates = [keep.tile([P, s1 - s0], F32, name=f"gates{s0}") for s0, s1 in GATES]
-        residual = [keep.tile([P, BANK], F32, name=f"residual{k}") for k in range(T // BANK)]
+        residual_first = keep.tile([P, BANK], F32, name="residual_first")
+        residual_rest = keep.tile([P, T - BANK], F32, name="residual_rest")
+        residual = [residual_first[:], residual_rest[:, 0:BANK], residual_rest[:, BANK : 2 * BANK]]
         placed = [keep.tile([P, T], F32, name=f"placed{s0}") for s0, s1 in GATES]
         ident = keep.tile([P, P], F32, name="ident")
         warm = keep.tile([P, 1], F32, name="warm")
         warmed = keep.tile([P, 1], F32, name="warmed")
 
         tokens = xT.rearrange("(p j) t -> p j t", j=PACK)
-        raw = {}
-        for u, chunks in enumerate(CHUNKS):
-            for t0, width, share in chunks:
-                columns = T if (u, t0) == (0, 1024) else 2 * width
-                holder = keep.tile([P, columns], F32, name=f"raw{u}_{t0}")
-                raw[u, t0] = holder[:, columns - 2 * width : columns]
-                if columns == T:
-                    reused = holder
-                nc.sync.dma_start(out=raw[u, t0][:, 0:width], in_=tokens[:, 2 * u, t0 : t0 + width])
-                nc.scalar.dma_start(out=raw[u, t0][:, width : 2 * width], in_=tokens[:, 2 * u + 1, t0 : t0 + width])
-            if u == 0:
+        first_rows = keep.tile([P, 2048], F32, name="first_rows")
+        reused = keep.tile([P, T], F32, name="reused")
+        third_rows = keep.tile([P, T], F32, name="third_rows")
+        last_rows = keep.tile([P, T], F32, name="last_rows")
+        views = {
+            (0, 0): first_rows[:].rearrange("p (j t) -> p j t", j=2),
+            (0, 1024): reused[:, 512:T].rearrange("p (j t) -> p j t", j=2),
+            (1, 0): third_rows[:].rearrange("p (j t) -> p j t", j=2),
+            (1, 768): last_rows[:].rearrange("p (j t) -> p j t", j=2)[:, :, 0:512],
+            (1, 1280): last_rows[:].rearrange("p (j t) -> p j t", j=2)[:, :, 512:768],
+        }
+        for u, t0, width in ((0, 0, 1024), (0, 1024, 512), (1, 0, 768)):
+            nc.sync.dma_start(out=views[u, t0][:, 0, :], in_=tokens[:, 2 * u, t0 : t0 + width])
+            nc.scalar.dma_start(out=views[u, t0][:, 1, :], in_=tokens[:, 2 * u + 1, t0 : t0 + width])
+            if t0 == 1024:
                 nc.sync.dma_start(offsets[:], offs)
+        nc.sync.dma_start(out=last_rows[:, 0:768], in_=tokens[:, 2, 768:T])
+        nc.scalar.dma_start(out=last_rows[:, 768:1280], in_=tokens[:, 3, 768:1280])
+        nc.sync.dma_start(out=last_rows[:, 1280:T], in_=tokens[:, 3, 1280:T])
 
         nc.vector.memset(warm[:], 0.0)
         nc.scalar.activation(warmed[:], warm[:], SILU)
@@ -83,10 +92,9 @@ def tile_moe_res_lin_silu_kernel(tc, xT, xr, w_words, w_scales, b, gate, offs, o
                 out=w_bytes[32 * q : 32 * q + 4, :, :].bitcast(I32),
                 in_=w_scales[:, 0, 4 * q : 4 * q + 4, :].rearrange("e q n -> q e n").bitcast(I32),
             )
-        for k in range(T // BANK):
-            nc.sync.dma_start(out=residual[k][:], in_=xr[:, k * BANK : (k + 1) * BANK])
-            if k == 0:
-                nc.sync.dma_start(out=w_later[:].bitcast(I32), in_=codes[:, 0 : E - GROUP, :])
+        nc.sync.dma_start(out=residual_first[:], in_=xr[:, 0:BANK])
+        nc.sync.dma_start(out=w_later[:].bitcast(I32), in_=codes[:, 0 : E - GROUP, :])
+        nc.sync.dma_start(out=residual_rest[:], in_=xr[:, BANK:T])
         nc.sync.dma_start(out=gates[1][:], in_=gate[:, GATES[1][0] : GATES[1][1]])
 
         width_g = GROUP * C
@@ -104,7 +112,7 @@ def tile_moe_res_lin_silu_kernel(tc, xT, xr, w_words, w_scales, b, gate, offs, o
                 reused_or_new = reused
             pairs = reused_or_new[:].bitcast(BF16).rearrange("p (t j) -> p t j", j=2)
             for t0, width, share in chunks:
-                rows = raw[u, t0].rearrange("p (j t) -> p t j", j=2)
+                rows = views[u, t0].rearrange("p j t -> p t j")
                 cut = width - share
                 if share:
                     nc.vector.tensor_copy(woven(pairs[:, t0 + cut : t0 + width, :]), woven(rows[:, cut:width, :]))
@@ -188,7 +196,7 @@ def tile_moe_res_lin_silu_kernel(tc, xT, xr, w_words, w_scales, b, gate, offs, o
 
         sums = [psum.tile([P, BANK], F32, name=f"acc{bank}") for bank in (7, 6, 1)]
         for k in range(3):
-            turn(sums[k], residual[k][:], True)
+            turn(sums[k], residual[k], True)
         turned = []
         for k, summed in enumerate(sums):
             turn(summed, placed[0][:, k * BANK : (k + 1) * BANK], False)

@@ -19,20 +19,15 @@ COPY = mybir.ActivationFunctionType.Copy
 P = 128
 PACK = 4
 
-CHUNKS = (
-    ((0, 1024, 672), (1024, 512, 336)),
-    ((0, 768, 128), (768, 512, 336), (1280, 256, 160)),
-)
+PIECE = 512
+DIRECT = 448
+SHARE = 1024
 GROUP = 2
 GATES = ((608, 1024), (0, 608))
 STORES = ((0, 192), (704, 960), (192, 704), (960, 1536))
 SIDE = (192, 512)
 BANK = 512
-RUN = 128
-
-
-def woven(ap):
-    return ap.rearrange("p (c i) j -> p c j i", i=4)
+RUN = 64
 
 
 def tile_moe_res_lin_silu_kernel(tc, xT, xr, w_words, w_scales, b, gate, offs, out):
@@ -46,7 +41,9 @@ def tile_moe_res_lin_silu_kernel(tc, xT, xr, w_words, w_scales, b, gate, offs, o
         w_later = keep.tile([P, E - GROUP, 2 * N], U8, name="w_later", align_bytes=64)
         w_bytes = keep.tile([P, E, N], U8, name="w_bytes", align_bytes=64)
         bias = keep.tile([P, E], F32, name="bias")
-        gates = [keep.tile([P, s1 - s0], F32, name=f"gates{s0}") for s0, s1 in GATES]
+        row3 = keep.tile([P, T + GATES[0][1] - GATES[0][0]], F32, name="row3")
+        gate_later = keep.tile([P, GATES[1][1] - GATES[1][0]], F32, name="gate_later")
+        gates = [row3[:, T : T + GATES[0][1] - GATES[0][0]], gate_later[:]]
         residual_first = keep.tile([P, BANK], F32, name="residual_first")
         residual_rest = keep.tile([P, T - BANK], F32, name="residual_rest")
         residual = [residual_first[:], residual_rest[:, 0:BANK], residual_rest[:, BANK : 2 * BANK]]
@@ -56,25 +53,15 @@ def tile_moe_res_lin_silu_kernel(tc, xT, xr, w_words, w_scales, b, gate, offs, o
         warmed = keep.tile([P, 1], F32, name="warmed")
 
         tokens = xT.rearrange("(p j) t -> p j t", j=PACK)
-        first_rows = keep.tile([P, 2048], F32, name="first_rows")
-        reused = keep.tile([P, T], F32, name="reused")
-        third_rows = keep.tile([P, T], F32, name="third_rows")
-        last_rows = keep.tile([P, T], F32, name="last_rows")
-        views = {
-            (0, 0): first_rows[:].rearrange("p (j t) -> p j t", j=2),
-            (0, 1024): reused[:, 512:T].rearrange("p (j t) -> p j t", j=2),
-            (1, 0): third_rows[:].rearrange("p (j t) -> p j t", j=2),
-            (1, 768): last_rows[:].rearrange("p (j t) -> p j t", j=2)[:, :, 0:512],
-            (1, 1280): last_rows[:].rearrange("p (j t) -> p j t", j=2)[:, :, 512:768],
-        }
-        for u, t0, width in ((0, 0, 1024), (0, 1024, 512), (1, 0, 768)):
-            nc.sync.dma_start(out=views[u, t0][:, 0, :], in_=tokens[:, 2 * u, t0 : t0 + width])
-            nc.scalar.dma_start(out=views[u, t0][:, 1, :], in_=tokens[:, 2 * u + 1, t0 : t0 + width])
-            if t0 == 1024:
-                nc.sync.dma_start(offsets[:], offs)
-        nc.sync.dma_start(out=last_rows[:, 0:768], in_=tokens[:, 2, 768:T])
-        nc.scalar.dma_start(out=last_rows[:, 768:1280], in_=tokens[:, 3, 768:1280])
-        nc.sync.dma_start(out=last_rows[:, 1280:T], in_=tokens[:, 3, 1280:T])
+        row0 = keep.tile([P, T], F32, name="row0")
+        row1 = keep.tile([P, T], F32, name="row1")
+        row2 = keep.tile([P, T], F32, name="row2")
+        nc.sync.dma_start(offsets[:], offs)
+        nc.sync.dma_start(out=row0[:], in_=tokens[:, 0, :])
+        nc.sync.dma_start(out=row2[:], in_=tokens[:, 2, :])
+        for t0 in range(0, T, PIECE):
+            nc.sync.dma_start(out=row1[:, t0 : t0 + PIECE], in_=tokens[:, 1, t0 : t0 + PIECE])
+        nc.sync.dma_start(out=row3[:, 0:T], in_=tokens[:, 3, :])
 
         nc.vector.memset(warm[:], 0.0)
         nc.scalar.activation(warmed[:], warm[:], SILU)
@@ -85,7 +72,7 @@ def tile_moe_res_lin_silu_kernel(tc, xT, xr, w_words, w_scales, b, gate, offs, o
 
         codes = w_words.rearrange("e a p n -> p (e a) n").bitcast(I32)
         nc.sync.dma_start(out=bias[:], in_=b)
-        nc.sync.dma_start(out=gates[0][:], in_=gate[:, GATES[0][0] : GATES[0][1]])
+        nc.sync.dma_start(out=gates[0], in_=gate[:, GATES[0][0] : GATES[0][1]])
         nc.sync.dma_start(out=w_first[:].bitcast(I32), in_=codes[:, E - GROUP : E, :])
         for q in range(4):
             nc.sync.dma_start(
@@ -95,46 +82,40 @@ def tile_moe_res_lin_silu_kernel(tc, xT, xr, w_words, w_scales, b, gate, offs, o
         nc.sync.dma_start(out=residual_first[:], in_=xr[:, 0:BANK])
         nc.sync.dma_start(out=w_later[:].bitcast(I32), in_=codes[:, 0 : E - GROUP, :])
         nc.sync.dma_start(out=residual_rest[:], in_=xr[:, BANK:T])
-        nc.sync.dma_start(out=gates[1][:], in_=gate[:, GATES[1][0] : GATES[1][1]])
+        nc.sync.dma_start(out=gates[1], in_=gate[:, GATES[1][0] : GATES[1][1]])
 
         width_g = GROUP * C
-        halves = keep.tile([P, 3072], U32, name="halves")
-        runs = halves[:].rearrange("p (n s) -> p n s", s=RUN)
+        halves = keep.tile([P, 2 * E * C], U32, name="halves")
+        values = halves[:].bitcast(BF16).rearrange("p (r u s j) -> p r u s j", u=2, s=RUN, j=2)
 
         def listed(s0, s1):
             return offsets[:, s0 // 16 : s1 // 16]
 
-        windows = []
-        for u, chunks in enumerate(CHUNKS):
-            if u == 0:
-                reused_or_new = keep.tile([P, T], F32, name="pairs0")
-            else:
-                reused_or_new = reused
-            pairs = reused_or_new[:].bitcast(BF16).rearrange("p (t j) -> p t j", j=2)
-            for t0, width, share in chunks:
-                rows = views[u, t0].rearrange("p j t -> p t j")
-                cut = width - share
-                if share:
-                    nc.vector.tensor_copy(woven(pairs[:, t0 + cut : t0 + width, :]), woven(rows[:, cut:width, :]))
-                nc.scalar.activation(woven(pairs[:, t0 : t0 + cut, :]), woven(rows[:, 0:cut, :]), COPY)
-            windows.append(reused_or_new[:].bitcast(U32))
-            if u == 0:
-                nc.vector.tensor_copy(runs[:, 0:16:2, :], windows[0].indirect(offsets[:]))
+        def place(t, s0, s1):
+            return values[:, s0 // RUN : s1 // RUN, t // 2, :, t % 2]
+
+        rounded0 = keep.tile([P, T], BF16, name="rounded0")
+        rounded1 = keep.tile([P, T], BF16, name="rounded1")
+        nc.vector.tensor_copy(rounded0[:, 0:SHARE], row0[:, 0:SHARE])
+        nc.scalar.activation(rounded0[:, SHARE:T], row0[:, SHARE:T], COPY)
+        nc.vector.tensor_copy(place(0, 0, DIRECT), row0[:].indirect(listed(0, DIRECT)))
+        nc.scalar.activation(place(0, DIRECT, E * C), rounded0[:].indirect(listed(DIRECT, E * C)), COPY)
+        nc.vector.tensor_copy(place(2, 0, E * C), row2[:].indirect(offsets[:]))
+        for t0 in range(0, T, PIECE):
+            nc.scalar.activation(rounded1[:, t0 : t0 + PIECE], row1[:, t0 : t0 + PIECE], COPY)
+        nc.scalar.activation(place(1, DIRECT, E * C), rounded1[:].indirect(listed(DIRECT, E * C)), COPY)
+        nc.vector.tensor_copy(place(1, 0, DIRECT), row1[:].indirect(listed(0, DIRECT)))
 
         y = keep.tile([P, E * C], F32, name="y")
         first = keep.tile([P, 2 * width_g], U32, name="first", align_bytes=64)
         middle = keep.tile([P, 3 * width_g], U32, name="middle", align_bytes=64)
 
-        def gather(s0, s1, at):
-            nc.vector.tensor_copy(runs[:, at : at + 2 * (s1 - s0) // RUN - 1 : 2, :], windows[1].indirect(listed(s0, s1)))
+        def gather(s0, s1, more=0):
+            nc.vector.tensor_copy(place(3, s0, s1), row3[:, 0 : T + more].indirect(listed(s0, s1)))
 
-        def merge(into, slot, s0, s1, at):
-            low, count = 2 * s0 // RUN, (s1 - s0) // RUN
-            if at == low + 1:
-                both = runs[:, low : low + 2 * count, :].rearrange("p (b u) (c i) -> p b c u i", u=2, i=4)
-            else:
-                far = runs[:, low : 2 * at - low, :].rearrange("p (u b h) s -> p u b h s", u=2, h=2)
-                both = far[:, :, 0:count, 0, :].rearrange("p u b (c i) -> p b c u i", i=4)
+        def merge(into, slot, s0, s1):
+            count = (s1 - s0) // RUN
+            both = halves[:, 2 * s0 : 2 * s1].rearrange("p (b u c i) -> p b c u i", u=2, c=RUN // 4, i=4)
             words = into[:, 2 * slot : 2 * (slot + s1 - s0)].rearrange("p (b c i u) -> p b c u i", b=count, i=4, u=2)
             nc.scalar.copy(words, both)
 
@@ -169,16 +150,16 @@ def tile_moe_res_lin_silu_kernel(tc, xT, xr, w_words, w_scales, b, gate, offs, o
                 MULT,
             )
 
-        gather(768, 1024, 13)
-        merge(first, 128, 896, 1024, 15)
-        merge(first, 0, 768, 896, 13)
-        gather(384, 768, 7)
-        merge(middle, 0, 384, 768, 7)
+        gather(768, 1024)
+        merge(first, 128, 896, 1024)
+        merge(first, 0, 768, 896)
+        gather(384, 768)
+        merge(middle, 0, 384, 768)
         experts(7, 1, first[:, 256:512])
         experts(6, 1, first[:, 0:256])
-        gather(0, 384, 12)
+        gather(0, 384, 8)
         last = keep.tile([P, 3 * width_g], U32, name="slot_words6", align_bytes=64)
-        merge(last, 0, 0, 384, 12)
+        merge(last, 0, 0, 384)
         experts(4, 2, middle[:, 256:768])
         experts(3, 1, middle[:, 0:256])
         scatter(0, 0, 832, 1024)

@@ -20,10 +20,10 @@ P = 128
 PACK = 4
 
 PIECE = 512
-DIRECT = 448
-SHARE = 1024
+DIRECT = 384
+SHARE = 1184
 GROUP = 2
-GATES = ((608, 1024), (0, 608))
+GATES = ((832, 1024), (608, 832), (0, 608))
 STORES = ((0, 192), (704, 960), (192, 704), (960, 1536))
 SIDE = (192, 512)
 BANK = 512
@@ -42,12 +42,12 @@ def tile_moe_res_lin_silu_kernel(tc, xT, xr, w_words, w_scales, b, gate, offs, o
         w_bytes = keep.tile([P, E, N], U8, name="w_bytes", align_bytes=64)
         bias = keep.tile([P, E], F32, name="bias")
         row3 = keep.tile([P, T + GATES[0][1] - GATES[0][0]], F32, name="row3")
-        gate_later = keep.tile([P, GATES[1][1] - GATES[1][0]], F32, name="gate_later")
-        gates = [row3[:, T : T + GATES[0][1] - GATES[0][0]], gate_later[:]]
+        gates = [row3[:, T : T + GATES[0][1] - GATES[0][0]]]
+        gates.extend(keep.tile([P, s1 - s0], F32, name=f"gates{s0}")[:] for s0, s1 in GATES[1:])
         residual_first = keep.tile([P, BANK], F32, name="residual_first")
         residual_rest = keep.tile([P, T - BANK], F32, name="residual_rest")
         residual = [residual_first[:], residual_rest[:, 0:BANK], residual_rest[:, BANK : 2 * BANK]]
-        placed = [keep.tile([P, T], F32, name=f"placed{s0}") for s0, s1 in GATES]
+        placed = [keep.tile([P, T], F32, name=f"placed{w}") for w in range(2)]
         ident = keep.tile([P, P], F32, name="ident")
         warm = keep.tile([P, 1], F32, name="warm")
         warmed = keep.tile([P, 1], F32, name="warmed")
@@ -79,10 +79,11 @@ def tile_moe_res_lin_silu_kernel(tc, xT, xr, w_words, w_scales, b, gate, offs, o
                 out=w_bytes[32 * q : 32 * q + 4, :, :].bitcast(I32),
                 in_=w_scales[:, 0, 4 * q : 4 * q + 4, :].rearrange("e q n -> q e n").bitcast(I32),
             )
+        nc.sync.dma_start(out=gates[1], in_=gate[:, GATES[1][0] : GATES[1][1]])
         nc.sync.dma_start(out=residual_first[:], in_=xr[:, 0:BANK])
         nc.sync.dma_start(out=w_later[:].bitcast(I32), in_=codes[:, 0 : E - GROUP, :])
         nc.sync.dma_start(out=residual_rest[:], in_=xr[:, BANK:T])
-        nc.sync.dma_start(out=gates[1], in_=gate[:, GATES[1][0] : GATES[1][1]])
+        nc.sync.dma_start(out=gates[2], in_=gate[:, GATES[2][0] : GATES[2][1]])
 
         width_g = GROUP * C
         halves = keep.tile([P, 2 * E * C], U32, name="halves")
@@ -103,7 +104,8 @@ def tile_moe_res_lin_silu_kernel(tc, xT, xr, w_words, w_scales, b, gate, offs, o
         nc.vector.tensor_copy(place(2, 0, E * C), row2[:].indirect(offsets[:]))
         for t0 in range(0, T, PIECE):
             nc.scalar.activation(rounded1[:, t0 : t0 + PIECE], row1[:, t0 : t0 + PIECE], COPY)
-        nc.scalar.activation(place(1, DIRECT, E * C), rounded1[:].indirect(listed(DIRECT, E * C)), COPY)
+        nc.scalar.activation(place(1, 768, E * C), rounded1[:].indirect(listed(768, E * C)), COPY)
+        nc.scalar.activation(place(1, DIRECT, 768), rounded1[:].indirect(listed(DIRECT, 768)), COPY)
         nc.vector.tensor_copy(place(1, 0, DIRECT), row1[:].indirect(listed(0, DIRECT)))
 
         y = keep.tile([P, E * C], F32, name="y")
@@ -165,8 +167,8 @@ def tile_moe_res_lin_silu_kernel(tc, xT, xr, w_words, w_scales, b, gate, offs, o
         scatter(0, 0, 832, 1024)
         experts(0, 2, last[:, 0:512])
         experts(2, 1, last[:, 512:768])
-        scatter(0, 0, 608, 832)
-        scatter(1, 1, 0, 608)
+        scatter(0, 1, 608, 832)
+        scatter(1, 2, 0, 608)
 
         def turn(summed, source, first):
             for c0 in range(0, BANK, P):

@@ -18,16 +18,11 @@ COPY = mybir.ActivationFunctionType.Copy
 
 P = 128
 PACK = 4
-
-PIECE = 512
-DIRECT = 384
-SHARE = 1184
-GROUP = 2
-GATES = ((832, 1024), (608, 832), (0, 608))
-STORES = ((0, 192), (704, 960), (192, 704), (960, 1536))
-SIDE = (192, 512)
-BANK = 512
-RUN = 64
+PAIR = 2 * C
+CUT = 704
+PLANE = ((0, 1, 2, 3), (1, 2, 0, 1))
+TURNED = 1280
+SPANS = ((0, 256), (256, 640), (640, 1024), (1024, TURNED))
 
 
 def tile_moe_res_lin_silu_kernel(tc, xT, xr, w_words, w_scales, b, gate, offs, out):
@@ -37,176 +32,149 @@ def tile_moe_res_lin_silu_kernel(tc, xT, xr, w_words, w_scales, b, gate, offs, o
         tc.psum_pool(name="psum", bufs=1) as psum,
     ):
         offsets = keep.tile([P, E * C // 16], U16, name="offsets")
-        w_first = keep.tile([P, GROUP, 2 * N], U8, name="w_first", align_bytes=64)
-        w_later = keep.tile([P, E - GROUP, 2 * N], U8, name="w_later", align_bytes=64)
+        w_codes = keep.tile([P, E, 2 * N], U8, name="w_codes", align_bytes=64)
         w_bytes = keep.tile([P, E, N], U8, name="w_bytes", align_bytes=64)
         bias = keep.tile([P, E], F32, name="bias")
-        row3 = keep.tile([P, T + GATES[0][1] - GATES[0][0]], F32, name="row3")
-        gates = [row3[:, T : T + GATES[0][1] - GATES[0][0]]]
-        gates.extend(keep.tile([P, s1 - s0], F32, name=f"gates{s0}")[:] for s0, s1 in GATES[1:])
-        residual_first = keep.tile([P, BANK], F32, name="residual_first")
-        residual_rest = keep.tile([P, T - BANK], F32, name="residual_rest")
-        residual = [residual_first[:], residual_rest[:, 0:BANK], residual_rest[:, BANK : 2 * BANK]]
-        placed = [keep.tile([P, T], F32, name=f"placed{w}") for w in range(2)]
+        gate_high = keep.tile([P, E * C - CUT], F32, name="gate_high", align_bytes=64)
+        gate_low = keep.tile([P, CUT], F32, name="gate_low")
+        residual = keep.tile([P, T], F32, name="residual")
+        early = keep.tile([P, T], F32, name="early")
+        late = keep.tile([P, T], F32, name="late")
         ident = keep.tile([P, P], F32, name="ident")
         warm = keep.tile([P, 1], F32, name="warm")
         warmed = keep.tile([P, 1], F32, name="warmed")
 
         tokens = xT.rearrange("(p j) t -> p j t", j=PACK)
-        row0 = keep.tile([P, T], F32, name="row0")
-        row1 = keep.tile([P, T], F32, name="row1")
-        row2 = keep.tile([P, T], F32, name="row2")
+        rows = [keep.tile([P, T], F32, name=f"row{j}") for j in range(PACK)]
         nc.sync.dma_start(offsets[:], offs)
-        nc.sync.dma_start(out=row0[:], in_=tokens[:, 0, :])
-        nc.sync.dma_start(out=row2[:], in_=tokens[:, 2, :])
-        for t0 in range(0, T, PIECE):
-            nc.sync.dma_start(out=row1[:, t0 : t0 + PIECE], in_=tokens[:, 1, t0 : t0 + PIECE])
-        nc.sync.dma_start(out=row3[:, 0:T], in_=tokens[:, 3, :])
+        for j in range(PACK):
+            nc.sync.dma_start(out=rows[j][:], in_=tokens[:, j, :])
 
         nc.vector.memset(warm[:], 0.0)
         nc.scalar.activation(warmed[:], warm[:], SILU)
         nc.vector.memset(w_bytes[:].rearrange("p e n -> p (e n)").bitcast(I32), 0)
-        for tile in placed:
-            nc.vector.memset(tile[:], 0.0)
+        nc.vector.memset(early[:], 0.0)
+        nc.vector.memset(late[:], 0.0)
         make_identity(nc, ident[:])
 
         codes = w_words.rearrange("e a p n -> p (e a) n").bitcast(I32)
-        nc.sync.dma_start(out=bias[:], in_=b)
-        nc.sync.dma_start(out=gates[0], in_=gate[:, GATES[0][0] : GATES[0][1]])
-        nc.sync.dma_start(out=w_first[:].bitcast(I32), in_=codes[:, E - GROUP : E, :])
+        nc.sync.dma_start(out=w_codes[:].bitcast(I32), in_=codes)
         for q in range(4):
             nc.sync.dma_start(
                 out=w_bytes[32 * q : 32 * q + 4, :, :].bitcast(I32),
                 in_=w_scales[:, 0, 4 * q : 4 * q + 4, :].rearrange("e q n -> q e n").bitcast(I32),
             )
-        nc.sync.dma_start(out=gates[1], in_=gate[:, GATES[1][0] : GATES[1][1]])
-        nc.sync.dma_start(out=residual_first[:], in_=xr[:, 0:BANK])
-        nc.sync.dma_start(out=w_later[:].bitcast(I32), in_=codes[:, 0 : E - GROUP, :])
-        nc.sync.dma_start(out=residual_rest[:], in_=xr[:, BANK:T])
-        nc.sync.dma_start(out=gates[2], in_=gate[:, GATES[2][0] : GATES[2][1]])
-
-        width_g = GROUP * C
-        halves = keep.tile([P, 2 * E * C], U32, name="halves")
-        values = halves[:].bitcast(BF16).rearrange("p (r u s j) -> p r u s j", u=2, s=RUN, j=2)
+        nc.sync.dma_start(out=bias[:], in_=b)
+        nc.sync.dma_start(out=gate_high[:], in_=gate[:, CUT : E * C])
+        nc.sync.dma_start(out=gate_low[:], in_=gate[:, 0:CUT])
+        nc.sync.dma_start(out=residual[:], in_=xr)
 
         def listed(s0, s1):
             return offsets[:, s0 // 16 : s1 // 16]
 
-        def place(t, s0, s1):
-            return values[:, s0 // RUN : s1 // RUN, t // 2, :, t % 2]
+        woven = [keep.tile([P, PAIR, PACK], BF16, name=f"woven{g}", align_bytes=64) for g in range(4)]
+        planes = {g: keep.tile([P, max(PLANE[g]) + 1, PAIR], BF16, name=f"planes{g}") for g in (0, 1)}
 
-        rounded0 = keep.tile([P, T], BF16, name="rounded0")
-        rounded1 = keep.tile([P, T], BF16, name="rounded1")
-        nc.vector.tensor_copy(rounded0[:, 0:SHARE], row0[:, 0:SHARE])
-        nc.scalar.activation(rounded0[:, SHARE:T], row0[:, SHARE:T], COPY)
-        nc.vector.tensor_copy(place(0, 0, DIRECT), row0[:].indirect(listed(0, DIRECT)))
-        nc.scalar.activation(place(0, DIRECT, E * C), rounded0[:].indirect(listed(DIRECT, E * C)), COPY)
-        nc.vector.tensor_copy(place(2, 0, E * C), row2[:].indirect(offsets[:]))
-        for t0 in range(0, T, PIECE):
-            nc.scalar.activation(rounded1[:, t0 : t0 + PIECE], row1[:, t0 : t0 + PIECE], COPY)
-        nc.scalar.activation(place(1, 768, E * C), rounded1[:].indirect(listed(768, E * C)), COPY)
-        nc.scalar.activation(place(1, DIRECT, 768), rounded1[:].indirect(listed(DIRECT, 768)), COPY)
-        nc.vector.tensor_copy(place(1, 0, DIRECT), row1[:].indirect(listed(0, DIRECT)))
+        def gather(g, j):
+            slots = listed(g * PAIR, (g + 1) * PAIR)
+            if g in planes:
+                nc.scalar.activation(planes[g][:, PLANE[g][j], :], rows[j][:].indirect(slots), COPY)
+            else:
+                nc.vector.tensor_copy(woven[g][:, :, j], rows[j][:].indirect(slots))
+
+        def weave(copy, g, j):
+            copy(
+                woven[g][:, :, j : j + 2].rearrange("p (c i) t -> p c t i", i=4),
+                planes[g][:, PLANE[g][j] : PLANE[g][j] + 2, :].rearrange("p t (c i) -> p c t i", i=4),
+            )
 
         y = keep.tile([P, E * C], F32, name="y")
-        first = keep.tile([P, 2 * width_g], U32, name="first", align_bytes=64)
-        middle = keep.tile([P, 3 * width_g], U32, name="middle", align_bytes=64)
 
-        def gather(s0, s1, more=0):
-            nc.vector.tensor_copy(place(3, s0, s1), row3[:, 0 : T + more].indirect(listed(s0, s1)))
-
-        def merge(into, slot, s0, s1):
-            count = (s1 - s0) // RUN
-            both = halves[:, 2 * s0 : 2 * s1].rearrange("p (b u c i) -> p b c u i", u=2, c=RUN // 4, i=4)
-            words = into[:, 2 * slot : 2 * (slot + s1 - s0)].rearrange("p (b c i u) -> p b c u i", b=count, i=4, u=2)
-            nc.scalar.copy(words, both)
-
-        def experts(e0, count, merged):
-            slot_words = keep.tile([P, count * C], U32, name=f"slot_words{e0}", align_bytes=64)
-            slot_scales = keep.tile([P, count * C], U8, name=f"slot_scales{e0}", align_bytes=64)
+        def experts(g, banks):
+            slot_words = keep.tile([P, PAIR], U32, name=f"slot_words{g}", align_bytes=64)
+            slot_scales = keep.tile([P, PAIR], U8, name=f"slot_scales{g}", align_bytes=64)
             nc.vector.quantize_mx(
                 out=slot_words[:].bitcast(FP8X4),
                 scales=slot_scales[:],
-                in_=merged.bitcast(BF16),
+                in_=woven[g][:].rearrange("p s t -> p (s t)"),
             )
-            for i in reversed(range(count)):
-                e = e0 + i
+            for i in (1, 0):
+                e = 2 * g + i
                 cols = slice(i * C, (i + 1) * C)
-                acc = psum.tile([P, C], F32, name=f"acc{e}")[:]
                 nc.tensor.matmul_mx(
-                    out=acc,
-                    lhsT=(w_first[:, e - E + GROUP, :] if e >= E - GROUP else w_later[:, e, :]).bitcast(FP4X4),
+                    out=banks[i],
+                    lhsT=w_codes[:, e, :].bitcast(FP4X4),
                     lhsT_scale=w_bytes[:, e, :],
                     rhs=slot_words[:, cols].bitcast(FP8X4),
                     rhs_scale=slot_scales[:, cols],
                     start=True,
                     stop=True,
                 )
-                nc.scalar.activation(y[:, e * C : (e + 1) * C], acc, SILU, bias=bias[:, e : e + 1])
 
-        def scatter(window, w, s0, s1):
-            nc.vector.tensor_tensor(
-                placed[window][:].indirect(offsets[:, s0 // 16 : s1 // 16]),
-                y[:, s0:s1],
-                gates[w][:, s0 - GATES[w][0] : s1 - GATES[w][0]],
-                MULT,
-            )
+        def silus(g, banks):
+            for i in (1, 0):
+                e = 2 * g + i
+                nc.scalar.activation(y[:, e * C : (e + 1) * C], banks[i], SILU, bias=bias[:, e : e + 1])
 
-        gather(768, 1024)
-        merge(first, 128, 896, 1024)
-        merge(first, 0, 768, 896)
-        gather(384, 768)
-        merge(middle, 0, 384, 768)
-        experts(7, 1, first[:, 256:512])
-        experts(6, 1, first[:, 0:256])
-        gather(0, 384, 8)
-        last = keep.tile([P, 3 * width_g], U32, name="slot_words6", align_bytes=64)
-        merge(last, 0, 0, 384)
-        experts(4, 2, middle[:, 256:768])
-        experts(3, 1, middle[:, 0:256])
-        scatter(0, 0, 832, 1024)
-        experts(0, 2, last[:, 0:512])
-        experts(2, 1, last[:, 512:768])
-        scatter(0, 1, 608, 832)
-        scatter(1, 2, 0, 608)
+        acc = {3: [psum.tile([P, C], F32, name=f"bank{i}")[:] for i in range(2)]}
+        for g in (2, 1, 0):
+            both = psum.tile([P, PAIR], F32, name=f"bank{4 - g}")
+            acc[g] = [both[:, 0:C], both[:, C:PAIR]]
 
-        def turn(summed, source, first):
-            for c0 in range(0, BANK, P):
+        for j in range(PACK - 1):
+            for g in (3, 1, 2, 0):
+                gather(g, j)
+            if j == 1:
+                weave(nc.gpsimd.tensor_copy, 1, 0)
+                weave(nc.gpsimd.tensor_copy, 0, 0)
+        for g in (3, 1, 2, 0):
+            gather(g, 3)
+        experts(3, acc[3])
+        experts(2, acc[2])
+        weave(nc.vector.tensor_copy, 1, 2)
+        weave(nc.scalar.copy, 0, 2)
+        experts(1, acc[1])
+        experts(0, acc[0])
+        silus(3, acc[3])
+        silus(2, acc[2])
+        gated = keep.tile([P, E * C - CUT], F32, name="gated")
+        for s0, s1 in ((3 * PAIR, E * C), (CUT, 3 * PAIR)):
+            nc.vector.tensor_tensor(gated[:, s0 - CUT : s1 - CUT], y[:, s0:s1], gate_high[:, s0 - CUT : s1 - CUT], MULT)
+        silus(1, acc[1])
+        silus(0, acc[0])
+        nc.scalar.activation(early[:].indirect(listed(CUT, E * C)), gated[:], COPY)
+        for s0, s1 in ((2 * PAIR, CUT), (0, 2 * PAIR)):
+            nc.vector.tensor_tensor(late[:].indirect(listed(s0, s1)), y[:, s0:s1], gate_low[:, s0:s1], MULT)
+
+        sums = [psum.tile([P, t1 - t0], F32, name=f"bank{bank}") for bank, (t0, t1) in zip((5, 6, 7, 0), SPANS)]
+
+        def turn(k, source, first):
+            t0, t1 = SPANS[k]
+            for c0 in range(0, t1 - t0, P):
                 nc.tensor.matmul(
-                    summed[:, c0 : c0 + P], source[:, c0 : c0 + P], ident[:], is_transpose=True,
-                    start=first and c0 == 0, stop=not first and c0 == BANK - P,
+                    sums[k][:, c0 : c0 + P], source[:, t0 + c0 : t0 + c0 + P], ident[:], is_transpose=True,
+                    start=first and c0 == 0, stop=not first and c0 == t1 - t0 - P,
                 )
 
-        sums = [psum.tile([P, BANK], F32, name=f"acc{bank}") for bank in (7, 6, 1)]
-        for k in range(3):
-            turn(sums[k], residual[k], True)
-        turned = []
-        for k, summed in enumerate(sums):
-            turn(summed, placed[0][:, k * BANK : (k + 1) * BANK], False)
-            by_token = keep.tile([P, BANK], F32, name=f"by_token{k}")
-            nc.scalar.copy(by_token[:], summed[:])
-            turned.append(by_token)
+        for k in range(len(SPANS)):
+            turn(k, residual, True)
         partial = []
-        for k, by_token in enumerate(turned):
-            back = psum.tile([P, BANK], F32, name=f"acc{5 - k}")
-            for c0 in range(0, BANK, P):
+        for k, (t0, t1) in enumerate(SPANS):
+            turn(k, early, False)
+            by_token = keep.tile([P, t1 - t0], F32, name=f"by_token{k}")
+            nc.scalar.copy(by_token[:], sums[k][:])
+            back = psum.tile([P, t1 - t0], F32, name=f"bank{k + 1}")
+            for c0 in range(0, t1 - t0, P):
                 nc.tensor.transpose(back[:, c0 : c0 + P], by_token[:, c0 : c0 + P], ident[:])
             partial.append(back)
 
-        side = keep.tile([P, SIDE[1] - SIDE[0]], F32, name="side")
-        nc.scalar.copy(side[:], partial[0][:, SIDE[0] : SIDE[1]])
-        for i, (t0, t1) in enumerate(STORES):
-            total = keep.tile([P, t1 - t0], F32, name=f"total{i}")
-            begin = t0
-            if t0 == SIDE[0]:
-                nc.gpsimd.tensor_tensor(total[:, 0 : SIDE[1] - t0], placed[1][:, t0 : SIDE[1]], side[:], ADD)
-                begin = SIDE[1]
-            while begin < t1:
-                end = min(t1, (begin // BANK + 1) * BANK)
-                k = begin // BANK
-                nc.vector.tensor_tensor(
-                    total[:, begin - t0 : end - t0], placed[1][:, begin:end], partial[k][:, begin - k * BANK : end - k * BANK], ADD
-                )
-                begin = end
-            queue = nc.scalar if i == len(STORES) - 1 else nc.sync
-            queue.dma_start(out=out[:, t0:t1], in_=total[:])
+        side = keep.tile([P, T - TURNED], F32, name="side")
+        nc.gpsimd.tensor_tensor(side[:], late[:, TURNED:T], residual[:, TURNED:T], ADD)
+        for k, (t0, t1) in enumerate(SPANS):
+            end = T if t1 == TURNED else t1
+            total = keep.tile([P, end - t0], F32, name=f"total{k}")
+            nc.vector.tensor_tensor(total[:, 0 : t1 - t0], late[:, t0:t1], partial[k][:], ADD)
+            if end > t1:
+                nc.gpsimd.tensor_tensor(total[:, t1 - t0 : end - t0], side[:], early[:, t1:end], ADD)
+            queue = nc.scalar if end == T else nc.sync
+            queue.dma_start(out=out[:, t0:end], in_=total[:])

@@ -32,7 +32,8 @@ def tile_moe_res_lin_silu_kernel(tc, xT, xr, w_words, w_scales, b, gate, offs, o
         tc.psum_pool(name="psum", bufs=1) as psum,
     ):
         offsets = keep.tile([P, E * C // 16], U16, name="offsets")
-        w_codes = keep.tile([P, E, 2 * N], U8, name="w_codes", align_bytes=64)
+        w_first = keep.tile([P, 2, 2 * N], U8, name="w_first", align_bytes=64)
+        w_later = keep.tile([P, E - 2, 2 * N], U8, name="w_later", align_bytes=64)
         w_bytes = keep.tile([P, E, N], U8, name="w_bytes", align_bytes=64)
         bias = keep.tile([P, E], F32, name="bias")
         gate_high = keep.tile([P, E * C - CUT], F32, name="gate_high", align_bytes=64)
@@ -58,13 +59,14 @@ def tile_moe_res_lin_silu_kernel(tc, xT, xr, w_words, w_scales, b, gate, offs, o
         make_identity(nc, ident[:])
 
         codes = w_words.rearrange("e a p n -> p (e a) n").bitcast(I32)
-        nc.sync.dma_start(out=w_codes[:].bitcast(I32), in_=codes)
+        nc.sync.dma_start(out=w_first[:].bitcast(I32), in_=codes[:, E - 2 : E, :])
         for q in range(4):
             nc.sync.dma_start(
                 out=w_bytes[32 * q : 32 * q + 4, :, :].bitcast(I32),
                 in_=w_scales[:, 0, 4 * q : 4 * q + 4, :].rearrange("e q n -> q e n").bitcast(I32),
             )
         nc.sync.dma_start(out=bias[:], in_=b)
+        nc.sync.dma_start(out=w_later[:].bitcast(I32), in_=codes[:, 0 : E - 2, :])
         nc.sync.dma_start(out=gate_high[:], in_=gate[:, CUT : E * C])
         nc.sync.dma_start(out=gate_low[:], in_=gate[:, 0:CUT])
         nc.sync.dma_start(out=residual[:], in_=xr)
@@ -103,7 +105,7 @@ def tile_moe_res_lin_silu_kernel(tc, xT, xr, w_words, w_scales, b, gate, offs, o
                 cols = slice(i * C, (i + 1) * C)
                 nc.tensor.matmul_mx(
                     out=banks[i],
-                    lhsT=w_codes[:, e, :].bitcast(FP4X4),
+                    lhsT=(w_first[:, i, :] if g == 3 else w_later[:, e, :]).bitcast(FP4X4),
                     lhsT_scale=w_bytes[:, e, :],
                     rhs=slot_words[:, cols].bitcast(FP8X4),
                     rhs_scale=slot_scales[:, cols],

@@ -20,7 +20,9 @@ P = 128
 PACK = 4
 PAIR = 2 * C
 CUT = 704
-PLANE = ((0, 1, 2, 3), (1, 2, 0, 1))
+DIRECT = 704
+HALVES = ((320, DIRECT), (0, 320))
+PARTS = ((2 * PAIR, DIRECT), (PAIR, 2 * PAIR), (0, PAIR))
 TURNED = 1280
 SPANS = ((0, 256), (256, 640), (640, 1024), (1024, TURNED))
 
@@ -74,21 +76,25 @@ def tile_moe_res_lin_silu_kernel(tc, xT, xr, w_words, w_scales, b, gate, offs, o
         def listed(s0, s1):
             return offsets[:, s0 // 16 : s1 // 16]
 
-        woven = [keep.tile([P, PAIR, PACK], BF16, name=f"woven{g}", align_bytes=64) for g in range(4)]
-        planes = {g: keep.tile([P, max(PLANE[g]) + 1, PAIR], BF16, name=f"planes{g}") for g in (0, 1)}
+        woven = keep.tile([P, E * C, PACK], BF16, name="woven", align_bytes=64)
+        front = keep.tile([P, 2, DIRECT], BF16, name="front")
+        rear = keep.tile([P, 2 * (2 * DIRECT - PARTS[-1][1])], BF16, name="rear")
 
-        def gather(g, j):
-            slots = listed(g * PAIR, (g + 1) * PAIR)
-            if g in planes:
-                nc.scalar.activation(planes[g][:, PLANE[g][j], :], rows[j][:].indirect(slots), COPY)
-            else:
-                nc.vector.tensor_copy(woven[g][:, :, j], rows[j][:].indirect(slots))
+        def direct(j):
+            nc.vector.tensor_copy(woven[:, DIRECT : E * C, j], rows[j][:].indirect(listed(DIRECT, E * C)))
 
-        def weave(copy, g, j):
-            copy(
-                woven[g][:, :, j : j + 2].rearrange("p (c i) t -> p c t i", i=4),
-                planes[g][:, PLANE[g][j] : PLANE[g][j] + 2, :].rearrange("p t (c i) -> p c t i", i=4),
+        def plane(into, j, s0, s1):
+            nc.scalar.activation(into, rows[j][:].indirect(listed(s0, s1)), COPY)
+
+        def weave(j, planes, s0, s1):
+            nc.vector.tensor_copy(
+                woven[:, s0:s1, j : j + 2].rearrange("p (c i) t -> p c t i", i=4),
+                planes.rearrange("p t (c i) -> p c t i", i=4),
             )
+
+        def last_planes(s0, s1):
+            apart = 2 * DIRECT - s1 - s0
+            return rear[:, s0 : s0 + 2 * apart].rearrange("p (t s) -> p t s", t=2)[:, :, 0 : s1 - s0]
 
         y = keep.tile([P, E * C], F32, name="y")
 
@@ -98,7 +104,7 @@ def tile_moe_res_lin_silu_kernel(tc, xT, xr, w_words, w_scales, b, gate, offs, o
             nc.vector.quantize_mx(
                 out=slot_words[:].bitcast(FP8X4),
                 scales=slot_scales[:],
-                in_=woven[g][:].rearrange("p s t -> p (s t)"),
+                in_=woven[:, g * PAIR : (g + 1) * PAIR, :].rearrange("p s t -> p (s t)"),
             )
             for i in (1, 0):
                 e = 2 * g + i
@@ -123,18 +129,23 @@ def tile_moe_res_lin_silu_kernel(tc, xT, xr, w_words, w_scales, b, gate, offs, o
             both = psum.tile([P, PAIR], F32, name=f"bank{4 - g}")
             acc[g] = [both[:, 0:C], both[:, C:PAIR]]
 
-        for j in range(PACK - 1):
-            for g in (3, 1, 2, 0):
-                gather(g, j)
-            if j == 1:
-                weave(nc.gpsimd.tensor_copy, 1, 0)
-                weave(nc.gpsimd.tensor_copy, 0, 0)
-        for g in (3, 1, 2, 0):
-            gather(g, 3)
+        direct(0)
+        plane(front[:, 0, :], 0, 0, DIRECT)
+        direct(1)
+        for s0, s1 in HALVES:
+            plane(front[:, 1, s0:s1], 1, s0, s1)
+        weave(0, front[:, :, HALVES[0][0] : HALVES[0][1]], *HALVES[0])
+        direct(2)
+        plane(rear[:, 0:DIRECT], 2, 0, DIRECT)
+        weave(0, front[:, :, HALVES[1][0] : HALVES[1][1]], *HALVES[1])
+        direct(3)
+        for s0, s1 in PARTS:
+            plane(last_planes(s0, s1)[:, 1, :], 3, s0, s1)
+        weave(2, last_planes(*PARTS[0]), *PARTS[0])
         experts(3, acc[3])
         experts(2, acc[2])
-        weave(nc.vector.tensor_copy, 1, 2)
-        weave(nc.scalar.copy, 0, 2)
+        weave(2, last_planes(*PARTS[1]), *PARTS[1])
+        weave(2, last_planes(*PARTS[2]), *PARTS[2])
         experts(1, acc[1])
         experts(0, acc[0])
         silus(3, acc[3])

@@ -19,10 +19,10 @@ COPY = mybir.ActivationFunctionType.Copy
 P = 128
 PACK = 4
 PAIR = 2 * C
-CUT = 704
-DIRECT = 704
-HALVES = ((320, DIRECT), (0, 320))
-PARTS = ((2 * PAIR, DIRECT), (PAIR, 2 * PAIR), (0, PAIR))
+CUT = 736
+DIRECT = 640
+HALVES = ((PAIR, DIRECT), (0, PAIR))
+PARTS = ((2 * PAIR, DIRECT), (0, PAIR), (PAIR, 2 * PAIR))
 TURNED = 1280
 SPANS = ((0, 256), (256, 640), (640, 1024), (1024, TURNED))
 
@@ -55,7 +55,7 @@ def tile_moe_res_lin_silu_kernel(tc, xT, xr, w_words, w_scales, b, gate, offs, o
 
         nc.vector.memset(warm[:], 0.0)
         nc.scalar.activation(warmed[:], warm[:], SILU)
-        nc.vector.memset(w_bytes[:].rearrange("p e n -> p (e n)").bitcast(I32), 0)
+        nc.gpsimd.memset(w_bytes[:].rearrange("p e n -> p (e n)").bitcast(I32), 0)
         nc.vector.memset(early[:], 0.0)
         nc.vector.memset(late[:], 0.0)
         make_identity(nc, ident[:])
@@ -78,7 +78,7 @@ def tile_moe_res_lin_silu_kernel(tc, xT, xr, w_words, w_scales, b, gate, offs, o
 
         woven = keep.tile([P, E * C, PACK], BF16, name="woven", align_bytes=64)
         front = keep.tile([P, 2, DIRECT], BF16, name="front")
-        rear = keep.tile([P, 2 * (2 * DIRECT - PARTS[-1][1])], BF16, name="rear")
+        rear = keep.tile([P, PAIR + 2 * (2 * DIRECT - 2 * PAIR)], BF16, name="rear")
 
         def direct(j):
             nc.vector.tensor_copy(woven[:, DIRECT : E * C, j], rows[j][:].indirect(listed(DIRECT, E * C)))
@@ -86,14 +86,14 @@ def tile_moe_res_lin_silu_kernel(tc, xT, xr, w_words, w_scales, b, gate, offs, o
         def plane(into, j, s0, s1):
             nc.scalar.activation(into, rows[j][:].indirect(listed(s0, s1)), COPY)
 
-        def weave(j, planes, s0, s1):
-            nc.vector.tensor_copy(
+        def weave(j, planes, s0, s1, copy=nc.vector.tensor_copy):
+            copy(
                 woven[:, s0:s1, j : j + 2].rearrange("p (c i) t -> p c t i", i=4),
                 planes.rearrange("p t (c i) -> p c t i", i=4),
             )
 
         def last_planes(s0, s1):
-            apart = 2 * DIRECT - s1 - s0
+            apart = DIRECT + (DIRECT - 2 * PAIR if s0 < 2 * PAIR else -s0)
             return rear[:, s0 : s0 + 2 * apart].rearrange("p (t s) -> p t s", t=2)[:, :, 0 : s1 - s0]
 
         y = keep.tile([P, E * C], F32, name="y")
@@ -144,7 +144,7 @@ def tile_moe_res_lin_silu_kernel(tc, xT, xr, w_words, w_scales, b, gate, offs, o
         weave(2, last_planes(*PARTS[0]), *PARTS[0])
         experts(3, acc[3])
         experts(2, acc[2])
-        weave(2, last_planes(*PARTS[1]), *PARTS[1])
+        weave(2, last_planes(*PARTS[1]), *PARTS[1], copy=nc.scalar.copy)
         weave(2, last_planes(*PARTS[2]), *PARTS[2])
         experts(1, acc[1])
         experts(0, acc[0])

@@ -19,7 +19,7 @@ COPY = mybir.ActivationFunctionType.Copy
 P = 128
 PACK = 4
 PAIR = 2 * C
-CUT = 736
+CUT = 704
 DIRECT = 640
 HALVES = ((PAIR, DIRECT), (0, PAIR))
 PARTS = ((2 * PAIR, DIRECT), (0, PAIR), (PAIR, 2 * PAIR))
@@ -169,11 +169,11 @@ def tile_moe_res_lin_silu_kernel(tc, xT, xr, w_words, w_scales, b, gate, offs, o
                     start=first and c0 == 0, stop=not first and c0 == t1 - t0 - P,
                 )
 
-        for k in range(len(SPANS)):
-            turn(k, residual, True)
+        for source, opens in ((residual, True), (early, False)):
+            for k in range(len(SPANS)):
+                turn(k, source, opens)
         partial = []
         for k, (t0, t1) in enumerate(SPANS):
-            turn(k, early, False)
             by_token = keep.tile([P, t1 - t0], F32, name=f"by_token{k}")
             nc.scalar.copy(by_token[:], sums[k][:])
             back = psum.tile([P, t1 - t0], F32, name=f"bank{k + 1}")

@@ -19,10 +19,9 @@ COPY = mybir.ActivationFunctionType.Copy
 P = 128
 PACK = 4
 PAIR = 2 * C
-CUT = 704
-DIRECT = 640
-HALVES = ((PAIR, DIRECT), (0, PAIR))
-PARTS = ((2 * PAIR, DIRECT), (0, PAIR), (PAIR, 2 * PAIR))
+DIRECT = 384
+EARLY = 320
+PARTS = ((DIRECT, 2 * PAIR), (3 * PAIR, E * C), (2 * PAIR, 3 * PAIR))
 TURNED = 1280
 SPANS = ((0, 256), (256, 640), (640, 1024), (1024, TURNED))
 
@@ -38,8 +37,8 @@ def tile_moe_res_lin_silu_kernel(tc, xT, xr, w_words, w_scales, b, gate, offs, o
         w_later = keep.tile([P, E - 2, 2 * N], U8, name="w_later", align_bytes=64)
         w_bytes = keep.tile([P, E, N], U8, name="w_bytes", align_bytes=64)
         bias = keep.tile([P, E], F32, name="bias")
-        gate_high = keep.tile([P, E * C - CUT], F32, name="gate_high", align_bytes=64)
-        gate_low = keep.tile([P, CUT], F32, name="gate_low")
+        gate_early = keep.tile([P, EARLY], F32, name="gate_early")
+        gate_late = keep.tile([P, E * C - EARLY], F32, name="gate_late")
         residual = keep.tile([P, T], F32, name="residual")
         early = keep.tile([P, T], F32, name="early")
         late = keep.tile([P, T], F32, name="late")
@@ -49,9 +48,10 @@ def tile_moe_res_lin_silu_kernel(tc, xT, xr, w_words, w_scales, b, gate, offs, o
 
         tokens = xT.rearrange("(p j) t -> p j t", j=PACK)
         rows = [keep.tile([P, T], F32, name=f"row{j}") for j in range(PACK)]
-        nc.sync.dma_start(offsets[:], offs)
         for j in range(PACK):
             nc.sync.dma_start(out=rows[j][:], in_=tokens[:, j, :])
+            if j == 0:
+                nc.sync.dma_start(offsets[:], offs)
 
         nc.vector.memset(warm[:], 0.0)
         nc.scalar.activation(warmed[:], warm[:], SILU)
@@ -61,40 +61,35 @@ def tile_moe_res_lin_silu_kernel(tc, xT, xr, w_words, w_scales, b, gate, offs, o
         make_identity(nc, ident[:])
 
         codes = w_words.rearrange("e a p n -> p (e a) n").bitcast(I32)
-        nc.sync.dma_start(out=w_first[:].bitcast(I32), in_=codes[:, E - 2 : E, :])
+        nc.sync.dma_start(out=w_first[:].bitcast(I32), in_=codes[:, 0:2, :])
         for q in range(4):
             nc.sync.dma_start(
                 out=w_bytes[32 * q : 32 * q + 4, :, :].bitcast(I32),
                 in_=w_scales[:, 0, 4 * q : 4 * q + 4, :].rearrange("e q n -> q e n").bitcast(I32),
             )
         nc.sync.dma_start(out=bias[:], in_=b)
-        nc.sync.dma_start(out=w_later[:].bitcast(I32), in_=codes[:, 0 : E - 2, :])
-        nc.sync.dma_start(out=gate_high[:], in_=gate[:, CUT : E * C])
-        nc.sync.dma_start(out=gate_low[:], in_=gate[:, 0:CUT])
+        nc.sync.dma_start(out=w_later[:].bitcast(I32), in_=codes[:, 2:E, :])
+        nc.sync.dma_start(out=gate_early[:], in_=gate[:, 0:EARLY])
+        nc.sync.dma_start(out=gate_late[:], in_=gate[:, EARLY : E * C])
         nc.sync.dma_start(out=residual[:], in_=xr)
 
         def listed(s0, s1):
             return offsets[:, s0 // 16 : s1 // 16]
 
         woven = keep.tile([P, E * C, PACK], BF16, name="woven", align_bytes=64)
-        front = keep.tile([P, 2, DIRECT], BF16, name="front")
-        rear = keep.tile([P, PAIR + 2 * (2 * DIRECT - 2 * PAIR)], BF16, name="rear")
+        planes = keep.tile([P, PACK, E * C - DIRECT], BF16, name="planes")
 
         def direct(j):
-            nc.vector.tensor_copy(woven[:, DIRECT : E * C, j], rows[j][:].indirect(listed(DIRECT, E * C)))
+            nc.vector.tensor_copy(woven[:, 0:DIRECT, j], rows[j][:].indirect(listed(0, DIRECT)))
 
-        def plane(into, j, s0, s1):
-            nc.scalar.activation(into, rows[j][:].indirect(listed(s0, s1)), COPY)
+        def plane(j, s0, s1):
+            nc.scalar.activation(planes[:, j, s0 - DIRECT : s1 - DIRECT], rows[j][:].indirect(listed(s0, s1)), COPY)
 
-        def weave(j, planes, s0, s1, copy=nc.vector.tensor_copy):
+        def weave(copy, j0, j1, s0, s1):
             copy(
-                woven[:, s0:s1, j : j + 2].rearrange("p (c i) t -> p c t i", i=4),
-                planes.rearrange("p t (c i) -> p c t i", i=4),
+                woven[:, s0:s1, j0:j1].rearrange("p (c i) t -> p c t i", i=4),
+                planes[:, j0:j1, s0 - DIRECT : s1 - DIRECT].rearrange("p t (c i) -> p c t i", i=4),
             )
-
-        def last_planes(s0, s1):
-            apart = DIRECT + (DIRECT - 2 * PAIR if s0 < 2 * PAIR else -s0)
-            return rear[:, s0 : s0 + 2 * apart].rearrange("p (t s) -> p t s", t=2)[:, :, 0 : s1 - s0]
 
         y = keep.tile([P, E * C], F32, name="y")
 
@@ -106,12 +101,12 @@ def tile_moe_res_lin_silu_kernel(tc, xT, xr, w_words, w_scales, b, gate, offs, o
                 scales=slot_scales[:],
                 in_=woven[:, g * PAIR : (g + 1) * PAIR, :].rearrange("p s t -> p (s t)"),
             )
-            for i in (1, 0):
+            for i in range(2):
                 e = 2 * g + i
                 cols = slice(i * C, (i + 1) * C)
                 nc.tensor.matmul_mx(
                     out=banks[i],
-                    lhsT=(w_first[:, i, :] if g == 3 else w_later[:, e, :]).bitcast(FP4X4),
+                    lhsT=(w_later[:, e - 2, :] if g else w_first[:, e, :]).bitcast(FP4X4),
                     lhsT_scale=w_bytes[:, e, :],
                     rhs=slot_words[:, cols].bitcast(FP8X4),
                     rhs_scale=slot_scales[:, cols],
@@ -120,44 +115,46 @@ def tile_moe_res_lin_silu_kernel(tc, xT, xr, w_words, w_scales, b, gate, offs, o
                 )
 
         def silus(g, banks):
-            for i in (1, 0):
+            for i in range(2):
                 e = 2 * g + i
                 nc.scalar.activation(y[:, e * C : (e + 1) * C], banks[i], SILU, bias=bias[:, e : e + 1])
 
-        acc = {3: [psum.tile([P, C], F32, name=f"bank{i}")[:] for i in range(2)]}
-        for g in (2, 1, 0):
-            both = psum.tile([P, PAIR], F32, name=f"bank{4 - g}")
-            acc[g] = [both[:, 0:C], both[:, C:PAIR]]
+        acc = [[psum.tile([P, C], F32, name=f"bank{i}")[:] for i in range(2)]]
+        for g in range(1, 4):
+            both = psum.tile([P, PAIR], F32, name=f"bank{g + 1}")
+            acc.append([both[:, 0:C], both[:, C:PAIR]])
 
         direct(0)
-        plane(front[:, 0, :], 0, 0, DIRECT)
+        nc.vector.tensor_copy(planes[:, 0, 0:C], rows[0][:].indirect(listed(DIRECT, DIRECT + C)))
+        plane(0, DIRECT + C, E * C)
         direct(1)
-        for s0, s1 in HALVES:
-            plane(front[:, 1, s0:s1], 1, s0, s1)
-        weave(0, front[:, :, HALVES[0][0] : HALVES[0][1]], *HALVES[0])
+        plane(1, DIRECT, 3 * PAIR)
+        plane(1, 3 * PAIR, E * C)
+        weave(nc.vector.tensor_copy, 0, 2, DIRECT, 3 * PAIR)
         direct(2)
-        plane(rear[:, 0:DIRECT], 2, 0, DIRECT)
-        weave(0, front[:, :, HALVES[1][0] : HALVES[1][1]], *HALVES[1])
+        plane(2, DIRECT, E * C)
+        weave(nc.vector.tensor_copy, 0, 2, 6 * C, 7 * C)
         direct(3)
         for s0, s1 in PARTS:
-            plane(last_planes(s0, s1)[:, 1, :], 3, s0, s1)
-        weave(2, last_planes(*PARTS[0]), *PARTS[0])
-        experts(3, acc[3])
-        experts(2, acc[2])
-        weave(2, last_planes(*PARTS[1]), *PARTS[1], copy=nc.scalar.copy)
-        weave(2, last_planes(*PARTS[2]), *PARTS[2])
-        experts(1, acc[1])
+            plane(3, s0, s1)
+        weave(nc.vector.tensor_copy, 2, PACK, DIRECT, 2 * PAIR)
         experts(0, acc[0])
-        silus(3, acc[3])
-        silus(2, acc[2])
-        gated = keep.tile([P, E * C - CUT], F32, name="gated")
-        for s0, s1 in ((3 * PAIR, E * C), (CUT, 3 * PAIR)):
-            nc.vector.tensor_tensor(gated[:, s0 - CUT : s1 - CUT], y[:, s0:s1], gate_high[:, s0 - CUT : s1 - CUT], MULT)
-        silus(1, acc[1])
+        experts(1, acc[1])
+        weave(nc.scalar.copy, 0, PACK, 7 * C, E * C)
+        weave(nc.vector.tensor_copy, 2, PACK, 2 * PAIR, 3 * PAIR)
+        weave(nc.vector.tensor_copy, 2, PACK, 6 * C, 7 * C)
+        experts(2, acc[2])
+        experts(3, acc[3])
         silus(0, acc[0])
-        nc.scalar.activation(early[:].indirect(listed(CUT, E * C)), gated[:], COPY)
-        for s0, s1 in ((2 * PAIR, CUT), (0, 2 * PAIR)):
-            nc.vector.tensor_tensor(late[:].indirect(listed(s0, s1)), y[:, s0:s1], gate_low[:, s0:s1], MULT)
+        silus(1, acc[1])
+        gated = keep.tile([P, EARLY], F32, name="gated")
+        for s0, s1 in ((0, PAIR), (PAIR, EARLY)):
+            nc.vector.tensor_tensor(gated[:, s0:s1], y[:, s0:s1], gate_early[:, s0:s1], MULT)
+        silus(2, acc[2])
+        silus(3, acc[3])
+        nc.scalar.activation(early[:].indirect(listed(0, EARLY)), gated[:], COPY)
+        for s0, s1 in ((EARLY, 2 * PAIR), (2 * PAIR, E * C)):
+            nc.vector.tensor_tensor(late[:].indirect(listed(s0, s1)), y[:, s0:s1], gate_late[:, s0 - EARLY : s1 - EARLY], MULT)
 
         sums = [psum.tile([P, t1 - t0], F32, name=f"bank{bank}") for bank, (t0, t1) in zip((5, 6, 7, 0), SPANS)]
 

@@ -33,12 +33,10 @@ def tile_moe_res_lin_silu_kernel(tc, xT, xr, w_words, w_scales, b, gate, offs, o
         tc.psum_pool(name="psum", bufs=1) as psum,
     ):
         offsets = keep.tile([P, E * C // 16], U16, name="offsets")
-        w_first = keep.tile([P, 2, 2 * N], U8, name="w_first", align_bytes=64)
-        w_later = keep.tile([P, E - 2, 2 * N], U8, name="w_later", align_bytes=64)
+        w_codes = [keep.tile([P, E // 2, 2 * N], U8, name=f"w_codes{h}", align_bytes=64) for h in range(2)]
         w_bytes = keep.tile([P, E, N], U8, name="w_bytes", align_bytes=64)
         bias = keep.tile([P, E], F32, name="bias")
-        gate_early = keep.tile([P, EARLY], F32, name="gate_early")
-        gate_late = keep.tile([P, E * C - EARLY], F32, name="gate_late")
+        gates = [keep.tile([P, 2 * PAIR], F32, name=f"gates{h}") for h in range(2)]
         residual = keep.tile([P, T], F32, name="residual")
         early = keep.tile([P, T], F32, name="early")
         late = keep.tile([P, T], F32, name="late")
@@ -61,16 +59,16 @@ def tile_moe_res_lin_silu_kernel(tc, xT, xr, w_words, w_scales, b, gate, offs, o
         make_identity(nc, ident[:])
 
         codes = w_words.rearrange("e a p n -> p (e a) n").bitcast(I32)
-        nc.sync.dma_start(out=w_first[:].bitcast(I32), in_=codes[:, 0:2, :])
+        nc.sync.dma_start(out=w_codes[0][:].bitcast(I32), in_=codes[:, 0 : E // 2, :])
         for q in range(4):
             nc.sync.dma_start(
                 out=w_bytes[32 * q : 32 * q + 4, :, :].bitcast(I32),
                 in_=w_scales[:, 0, 4 * q : 4 * q + 4, :].rearrange("e q n -> q e n").bitcast(I32),
             )
         nc.sync.dma_start(out=bias[:], in_=b)
-        nc.sync.dma_start(out=w_later[:].bitcast(I32), in_=codes[:, 2:E, :])
-        nc.sync.dma_start(out=gate_early[:], in_=gate[:, 0:EARLY])
-        nc.sync.dma_start(out=gate_late[:], in_=gate[:, EARLY : E * C])
+        nc.sync.dma_start(out=w_codes[1][:].bitcast(I32), in_=codes[:, E // 2 : E, :])
+        for h in range(2):
+            nc.sync.dma_start(out=gates[h][:], in_=gate[:, h * 2 * PAIR : (h + 1) * 2 * PAIR])
         nc.sync.dma_start(out=residual[:], in_=xr)
 
         def listed(s0, s1):
@@ -106,7 +104,7 @@ def tile_moe_res_lin_silu_kernel(tc, xT, xr, w_words, w_scales, b, gate, offs, o
                 cols = slice(i * C, (i + 1) * C)
                 nc.tensor.matmul_mx(
                     out=banks[i],
-                    lhsT=(w_later[:, e - 2, :] if g else w_first[:, e, :]).bitcast(FP4X4),
+                    lhsT=w_codes[e // (E // 2)][:, e % (E // 2), :].bitcast(FP4X4),
                     lhsT_scale=w_bytes[:, e, :],
                     rhs=slot_words[:, cols].bitcast(FP8X4),
                     rhs_scale=slot_scales[:, cols],
@@ -119,10 +117,7 @@ def tile_moe_res_lin_silu_kernel(tc, xT, xr, w_words, w_scales, b, gate, offs, o
                 e = 2 * g + i
                 nc.scalar.activation(y[:, e * C : (e + 1) * C], banks[i], SILU, bias=bias[:, e : e + 1])
 
-        acc = [[psum.tile([P, C], F32, name=f"bank{i}")[:] for i in range(2)]]
-        for g in range(1, 4):
-            both = psum.tile([P, PAIR], F32, name=f"bank{g + 1}")
-            acc.append([both[:, 0:C], both[:, C:PAIR]])
+        acc = [[psum.tile([P, C], F32, name=f"bank{2 * g + i}")[:] for i in range(2)] for g in range(4)]
 
         direct(0)
         nc.vector.tensor_copy(planes[:, 0, 0:C], rows[0][:].indirect(listed(DIRECT, DIRECT + C)))
@@ -149,14 +144,14 @@ def tile_moe_res_lin_silu_kernel(tc, xT, xr, w_words, w_scales, b, gate, offs, o
         silus(1, acc[1])
         gated = keep.tile([P, EARLY], F32, name="gated")
         for s0, s1 in ((0, PAIR), (PAIR, EARLY)):
-            nc.vector.tensor_tensor(gated[:, s0:s1], y[:, s0:s1], gate_early[:, s0:s1], MULT)
+            nc.vector.tensor_tensor(gated[:, s0:s1], y[:, s0:s1], gates[0][:, s0:s1], MULT)
         silus(2, acc[2])
         silus(3, acc[3])
         nc.scalar.activation(early[:].indirect(listed(0, EARLY)), gated[:], COPY)
-        for s0, s1 in ((EARLY, 2 * PAIR), (2 * PAIR, E * C)):
-            nc.vector.tensor_tensor(late[:].indirect(listed(s0, s1)), y[:, s0:s1], gate_late[:, s0 - EARLY : s1 - EARLY], MULT)
+        nc.vector.tensor_tensor(late[:].indirect(listed(EARLY, 2 * PAIR)), y[:, EARLY : 2 * PAIR], gates[0][:, EARLY:], MULT)
+        nc.vector.tensor_tensor(late[:].indirect(listed(2 * PAIR, E * C)), y[:, 2 * PAIR :], gates[1][:], MULT)
 
-        sums = [psum.tile([P, t1 - t0], F32, name=f"bank{bank}") for bank, (t0, t1) in zip((5, 6, 7, 0), SPANS)]
+        sums = [psum.tile([P, t1 - t0], F32, name=f"bank{bank}") for bank, (t0, t1) in enumerate(SPANS)]
 
         def turn(k, source, first):
             t0, t1 = SPANS[k]
@@ -173,18 +168,18 @@ def tile_moe_res_lin_silu_kernel(tc, xT, xr, w_words, w_scales, b, gate, offs, o
         for k, (t0, t1) in enumerate(SPANS):
             by_token = keep.tile([P, t1 - t0], F32, name=f"by_token{k}")
             nc.scalar.copy(by_token[:], sums[k][:])
-            back = psum.tile([P, t1 - t0], F32, name=f"bank{k + 1}")
+            back = psum.tile([P, t1 - t0], F32, name=f"bank{k + len(SPANS)}")
             for c0 in range(0, t1 - t0, P):
                 nc.tensor.transpose(back[:, c0 : c0 + P], by_token[:, c0 : c0 + P], ident[:])
             partial.append(back)
 
         side = keep.tile([P, T - TURNED], F32, name="side")
-        nc.gpsimd.tensor_tensor(side[:], late[:, TURNED:T], residual[:, TURNED:T], ADD)
+        nc.gpsimd.tensor_tensor(side[:], early[:, TURNED:T], residual[:, TURNED:T], ADD)
         for k, (t0, t1) in enumerate(SPANS):
             end = T if t1 == TURNED else t1
             total = keep.tile([P, end - t0], F32, name=f"total{k}")
             nc.vector.tensor_tensor(total[:, 0 : t1 - t0], late[:, t0:t1], partial[k][:], ADD)
             if end > t1:
-                nc.gpsimd.tensor_tensor(total[:, t1 - t0 : end - t0], side[:], early[:, t1:end], ADD)
+                nc.gpsimd.tensor_tensor(total[:, t1 - t0 : end - t0], side[:], late[:, t1:end], ADD)
             queue = nc.scalar if end == T else nc.sync
             queue.dma_start(out=out[:, t0:end], in_=total[:])

@@ -19,9 +19,9 @@ COPY = mybir.ActivationFunctionType.Copy
 P = 128
 PACK = 4
 PAIR = 2 * C
-DIRECT = 384
+DIRECT = 352
 EARLY = 320
-PARTS = ((DIRECT, 2 * PAIR), (3 * PAIR, E * C), (2 * PAIR, 3 * PAIR))
+PARTS = ((DIRECT, 2 * PAIR), (2 * PAIR, 3 * PAIR), (3 * PAIR, E * C))
 TURNED = 1280
 SPANS = ((0, 256), (256, 640), (640, 1024), (1024, TURNED))
 
@@ -123,21 +123,20 @@ def tile_moe_res_lin_silu_kernel(tc, xT, xr, w_words, w_scales, b, gate, offs, o
         nc.vector.tensor_copy(planes[:, 0, 0:C], rows[0][:].indirect(listed(DIRECT, DIRECT + C)))
         plane(0, DIRECT + C, E * C)
         direct(1)
-        plane(1, DIRECT, 3 * PAIR)
-        plane(1, 3 * PAIR, E * C)
-        weave(nc.vector.tensor_copy, 0, 2, DIRECT, 3 * PAIR)
+        plane(1, DIRECT, 2 * DIRECT)
+        plane(1, 2 * DIRECT, E * C)
+        weave(nc.vector.tensor_copy, 0, 2, DIRECT, 2 * DIRECT)
         direct(2)
         plane(2, DIRECT, E * C)
-        weave(nc.vector.tensor_copy, 0, 2, 6 * C, 7 * C)
+        weave(nc.vector.tensor_copy, 0, 2, 2 * DIRECT, E * C)
         direct(3)
         for s0, s1 in PARTS:
             plane(3, s0, s1)
         weave(nc.vector.tensor_copy, 2, PACK, DIRECT, 2 * PAIR)
         experts(0, acc[0])
         experts(1, acc[1])
-        weave(nc.scalar.copy, 0, PACK, 7 * C, E * C)
-        weave(nc.vector.tensor_copy, 2, PACK, 2 * PAIR, 3 * PAIR)
-        weave(nc.vector.tensor_copy, 2, PACK, 6 * C, 7 * C)
+        for e in range(4, E):
+            weave(nc.scalar.copy if e % 2 else nc.vector.tensor_copy, 2, PACK, e * C, (e + 1) * C)
         experts(2, acc[2])
         experts(3, acc[3])
         silus(0, acc[0])

@@ -128,7 +128,7 @@ def tile_moe_res_lin_silu_kernel(tc, xT, xr, w_words, w_scales, b, gate, offs, o
         weave(nc.vector.tensor_copy, 0, 2, DIRECT, 2 * DIRECT)
         direct(2)
         plane(2, DIRECT, E * C)
-        weave(nc.vector.tensor_copy, 0, 2, 2 * DIRECT, E * C)
+        weave(nc.vector.tensor_copy, 0, 2, 2 * DIRECT, 7 * C)
         direct(3)
         for s0, s1 in PARTS:
             plane(3, s0, s1)
@@ -136,7 +136,7 @@ def tile_moe_res_lin_silu_kernel(tc, xT, xr, w_words, w_scales, b, gate, offs, o
         experts(0, acc[0])
         experts(1, acc[1])
         for e in range(4, E):
-            weave(nc.scalar.copy if e % 2 else nc.vector.tensor_copy, 2, PACK, e * C, (e + 1) * C)
+            weave(nc.scalar.copy if e % 2 else nc.vector.tensor_copy, 0 if e == E - 1 else 2, PACK, e * C, (e + 1) * C)
         experts(2, acc[2])
         experts(3, acc[3])
         silus(0, acc[0])

@@ -19,9 +19,14 @@ COPY = mybir.ActivationFunctionType.Copy
 P = 128
 PACK = 4
 PAIR = 2 * C
-DIRECT = 352
-EARLY = 320
-PARTS = ((DIRECT, 2 * PAIR), (2 * PAIR, 3 * PAIR), (3 * PAIR, E * C))
+EARLY = 384
+MIDDLE = 576
+ROW_ORDER = (0, 2, 1, 3)
+LOW_VECTOR = (2 * C, 832)
+LOW_SCALAR = ((0, 2 * C), (832, E * C))
+HIGH_VECTOR = (2 * C, 5 * C)
+HIGH_SCALAR = ((0, C), (C, 2 * C), (5 * C, 7 * C), (7 * C, E * C))
+SETS = ((0, 1), (1, 2), (2, 5), (5, 7), (7, 8))
 TURNED = 1280
 SPANS = ((0, 256), (256, 640), (640, 1024), (1024, TURNED))
 
@@ -36,7 +41,7 @@ def tile_moe_res_lin_silu_kernel(tc, xT, xr, w_words, w_scales, b, gate, offs, o
         w_codes = [keep.tile([P, E // 2, 2 * N], U8, name=f"w_codes{h}", align_bytes=64) for h in range(2)]
         w_bytes = keep.tile([P, E, N], U8, name="w_bytes", align_bytes=64)
         bias = keep.tile([P, E], F32, name="bias")
-        gates = [keep.tile([P, 2 * PAIR], F32, name=f"gates{h}") for h in range(2)]
+        gates = [keep.tile([P, s1 - s0], F32, name=f"gates{s0}") for s0, s1 in ((0, MIDDLE), (MIDDLE, E * C))]
         residual = keep.tile([P, T], F32, name="residual")
         early = keep.tile([P, T], F32, name="early")
         late = keep.tile([P, T], F32, name="late")
@@ -46,9 +51,9 @@ def tile_moe_res_lin_silu_kernel(tc, xT, xr, w_words, w_scales, b, gate, offs, o
 
         tokens = xT.rearrange("(p j) t -> p j t", j=PACK)
         rows = [keep.tile([P, T], F32, name=f"row{j}") for j in range(PACK)]
-        for j in range(PACK):
+        for j in ROW_ORDER:
             nc.sync.dma_start(out=rows[j][:], in_=tokens[:, j, :])
-            if j == 0:
+            if j == ROW_ORDER[0]:
                 nc.sync.dma_start(offsets[:], offs)
 
         nc.vector.memset(warm[:], 0.0)
@@ -67,43 +72,36 @@ def tile_moe_res_lin_silu_kernel(tc, xT, xr, w_words, w_scales, b, gate, offs, o
             )
         nc.sync.dma_start(out=bias[:], in_=b)
         nc.sync.dma_start(out=w_codes[1][:].bitcast(I32), in_=codes[:, E // 2 : E, :])
-        for h in range(2):
-            nc.sync.dma_start(out=gates[h][:], in_=gate[:, h * 2 * PAIR : (h + 1) * 2 * PAIR])
+        nc.sync.dma_start(out=gates[0][:], in_=gate[:, 0:MIDDLE])
+        nc.sync.dma_start(out=gates[1][:], in_=gate[:, MIDDLE:])
         nc.sync.dma_start(out=residual[:], in_=xr)
 
         def listed(s0, s1):
             return offsets[:, s0 // 16 : s1 // 16]
 
         woven = keep.tile([P, E * C, PACK], BF16, name="woven", align_bytes=64)
-        planes = keep.tile([P, PACK, E * C - DIRECT], BF16, name="planes")
 
-        def direct(j):
-            nc.vector.tensor_copy(woven[:, 0:DIRECT, j], rows[j][:].indirect(listed(0, DIRECT)))
+        def on_vector(j, s0, s1):
+            nc.vector.tensor_copy(woven[:, s0:s1, j], rows[j][:].indirect(listed(s0, s1)))
 
-        def plane(j, s0, s1):
-            nc.scalar.activation(planes[:, j, s0 - DIRECT : s1 - DIRECT], rows[j][:].indirect(listed(s0, s1)), COPY)
-
-        def weave(copy, j0, j1, s0, s1):
-            copy(
-                woven[:, s0:s1, j0:j1].rearrange("p (c i) t -> p c t i", i=4),
-                planes[:, j0:j1, s0 - DIRECT : s1 - DIRECT].rearrange("p t (c i) -> p c t i", i=4),
-            )
+        def on_scalar(j, s0, s1):
+            nc.scalar.activation(woven[:, s0:s1, j], rows[j][:].indirect(listed(s0, s1)), COPY)
 
         y = keep.tile([P, E * C], F32, name="y")
+        acc = [psum.tile([P, C], F32, name=f"bank{e}")[:] for e in range(E)]
 
-        def experts(g, banks):
-            slot_words = keep.tile([P, PAIR], U32, name=f"slot_words{g}", align_bytes=64)
-            slot_scales = keep.tile([P, PAIR], U8, name=f"slot_scales{g}", align_bytes=64)
+        def experts(e0, e1):
+            slot_words = keep.tile([P, (e1 - e0) * C], U32, name=f"slot_words{e0}", align_bytes=64)
+            slot_scales = keep.tile([P, (e1 - e0) * C], U8, name=f"slot_scales{e0}", align_bytes=64)
             nc.vector.quantize_mx(
                 out=slot_words[:].bitcast(FP8X4),
                 scales=slot_scales[:],
-                in_=woven[:, g * PAIR : (g + 1) * PAIR, :].rearrange("p s t -> p (s t)"),
+                in_=woven[:, e0 * C : e1 * C, :].rearrange("p s t -> p (s t)"),
             )
-            for i in range(2):
-                e = 2 * g + i
-                cols = slice(i * C, (i + 1) * C)
+            for e in range(e0, e1):
+                cols = slice((e - e0) * C, (e - e0 + 1) * C)
                 nc.tensor.matmul_mx(
-                    out=banks[i],
+                    out=acc[e],
                     lhsT=w_codes[e // (E // 2)][:, e % (E // 2), :].bitcast(FP4X4),
                     lhsT_scale=w_bytes[:, e, :],
                     rhs=slot_words[:, cols].bitcast(FP8X4),
@@ -112,43 +110,25 @@ def tile_moe_res_lin_silu_kernel(tc, xT, xr, w_words, w_scales, b, gate, offs, o
                     stop=True,
                 )
 
-        def silus(g, banks):
-            for i in range(2):
-                e = 2 * g + i
-                nc.scalar.activation(y[:, e * C : (e + 1) * C], banks[i], SILU, bias=bias[:, e : e + 1])
+        for j in ROW_ORDER:
+            on_vector(j, *(LOW_VECTOR if j < 2 else HIGH_VECTOR))
+            for s0, s1 in LOW_SCALAR if j < 2 else HIGH_SCALAR:
+                on_scalar(j, s0, s1)
+        for e0, e1 in SETS:
+            experts(e0, e1)
 
-        acc = [[psum.tile([P, C], F32, name=f"bank{2 * g + i}")[:] for i in range(2)] for g in range(4)]
+        def silus(e0, e1):
+            for e in range(e0, e1):
+                nc.scalar.activation(y[:, e * C : (e + 1) * C], acc[e], SILU, bias=bias[:, e : e + 1])
 
-        direct(0)
-        nc.vector.tensor_copy(planes[:, 0, 0:C], rows[0][:].indirect(listed(DIRECT, DIRECT + C)))
-        plane(0, DIRECT + C, E * C)
-        direct(1)
-        plane(1, DIRECT, 2 * DIRECT)
-        plane(1, 2 * DIRECT, E * C)
-        weave(nc.vector.tensor_copy, 0, 2, DIRECT, 2 * DIRECT)
-        direct(2)
-        plane(2, DIRECT, E * C)
-        weave(nc.vector.tensor_copy, 0, 2, 2 * DIRECT, 7 * C)
-        direct(3)
-        for s0, s1 in PARTS:
-            plane(3, s0, s1)
-        weave(nc.vector.tensor_copy, 2, PACK, DIRECT, 2 * PAIR)
-        experts(0, acc[0])
-        experts(1, acc[1])
-        for e in range(4, E):
-            weave(nc.scalar.copy if e % 2 else nc.vector.tensor_copy, 0 if e == E - 1 else 2, PACK, e * C, (e + 1) * C)
-        experts(2, acc[2])
-        experts(3, acc[3])
-        silus(0, acc[0])
-        silus(1, acc[1])
+        silus(0, E // 2)
         gated = keep.tile([P, EARLY], F32, name="gated")
         for s0, s1 in ((0, PAIR), (PAIR, EARLY)):
             nc.vector.tensor_tensor(gated[:, s0:s1], y[:, s0:s1], gates[0][:, s0:s1], MULT)
-        silus(2, acc[2])
-        silus(3, acc[3])
+        silus(E // 2, E)
         nc.scalar.activation(early[:].indirect(listed(0, EARLY)), gated[:], COPY)
-        nc.vector.tensor_tensor(late[:].indirect(listed(EARLY, 2 * PAIR)), y[:, EARLY : 2 * PAIR], gates[0][:, EARLY:], MULT)
-        nc.vector.tensor_tensor(late[:].indirect(listed(2 * PAIR, E * C)), y[:, 2 * PAIR :], gates[1][:], MULT)
+        nc.vector.tensor_tensor(late[:].indirect(listed(EARLY, MIDDLE)), y[:, EARLY:MIDDLE], gates[0][:, EARLY:], MULT)
+        nc.vector.tensor_tensor(late[:].indirect(listed(MIDDLE, E * C)), y[:, MIDDLE:], gates[1][:], MULT)
 
         sums = [psum.tile([P, t1 - t0], F32, name=f"bank{bank}") for bank, (t0, t1) in enumerate(SPANS)]
 

@@ -21,12 +21,8 @@ PACK = 4
 PAIR = 2 * C
 EARLY = 384
 MIDDLE = 576
-ROW_ORDER = (0, 2, 1, 3)
-LOW_VECTOR = (2 * C, 832)
-LOW_SCALAR = ((0, 2 * C), (832, E * C))
-HIGH_VECTOR = (2 * C, 5 * C)
-HIGH_SCALAR = ((0, C), (C, 2 * C), (5 * C, 7 * C), (7 * C, E * C))
-SETS = ((0, 1), (1, 2), (2, 5), (5, 7), (7, 8))
+ROW_ORDER = (2, 0, 1, 3)
+SHARED = 576
 TURNED = 1280
 SPANS = ((0, 256), (256, 640), (640, 1024), (1024, TURNED))
 
@@ -79,24 +75,40 @@ def tile_moe_res_lin_silu_kernel(tc, xT, xr, w_words, w_scales, b, gate, offs, o
         def listed(s0, s1):
             return offsets[:, s0 // 16 : s1 // 16]
 
-        woven = keep.tile([P, E * C, PACK], BF16, name="woven", align_bytes=64)
+        groups = ((0, 3), (3, 5), (5, 7), (7, 8))
+        woven = {
+            e0: keep.tile([P, (e1 - e0) * C, PACK], BF16, name=f"woven{e0}", align_bytes=64) for e0, e1 in groups
+        }
+        pairs = {e0: keep.tile([P, 2, PAIR, 2], BF16, name=f"pairs{e0}") for e0 in (3, 5)}
 
-        def on_vector(j, s0, s1):
-            nc.vector.tensor_copy(woven[:, s0:s1, j], rows[j][:].indirect(listed(s0, s1)))
+        def on_vector(target, j, s0, s1):
+            nc.vector.tensor_copy(target, rows[j][:].indirect(listed(s0, s1)))
 
-        def on_scalar(j, s0, s1):
-            nc.scalar.activation(woven[:, s0:s1, j], rows[j][:].indirect(listed(s0, s1)), COPY)
+        def on_scalar(target, j, s0, s1):
+            nc.scalar.activation(target, rows[j][:].indirect(listed(s0, s1)), COPY)
+
+        def stepped(gather, j, e0, s0, s1):
+            gather(woven[e0][:, s0 - e0 * C : s1 - e0 * C, j], j, s0, s1)
+
+        def paired(gather, j, e0, s0, s1):
+            gather(pairs[e0][:, j // 2, s0 - e0 * C : s1 - e0 * C, j % 2], j, s0, s1)
+
+        def merge(e0):
+            nc.vector.tensor_copy(
+                woven[e0][:].bitcast(I32),
+                pairs[e0][:].rearrange("p h s t -> p h (s t)").bitcast(I32).rearrange("p h s -> p s h"),
+            )
 
         y = keep.tile([P, E * C], F32, name="y")
         acc = [psum.tile([P, C], F32, name=f"bank{e}")[:] for e in range(E)]
 
-        def experts(e0, e1):
+        def experts(group, e0, e1):
             slot_words = keep.tile([P, (e1 - e0) * C], U32, name=f"slot_words{e0}", align_bytes=64)
             slot_scales = keep.tile([P, (e1 - e0) * C], U8, name=f"slot_scales{e0}", align_bytes=64)
             nc.vector.quantize_mx(
                 out=slot_words[:].bitcast(FP8X4),
                 scales=slot_scales[:],
-                in_=woven[:, e0 * C : e1 * C, :].rearrange("p s t -> p (s t)"),
+                in_=woven[group][:, (e0 - group) * C : (e1 - group) * C, :].rearrange("p s t -> p (s t)"),
             )
             for e in range(e0, e1):
                 cols = slice((e - e0) * C, (e - e0 + 1) * C)
@@ -111,21 +123,36 @@ def tile_moe_res_lin_silu_kernel(tc, xT, xr, w_words, w_scales, b, gate, offs, o
                 )
 
         for j in ROW_ORDER:
-            on_vector(j, *(LOW_VECTOR if j < 2 else HIGH_VECTOR))
-            for s0, s1 in LOW_SCALAR if j < 2 else HIGH_SCALAR:
-                on_scalar(j, s0, s1)
-        for e0, e1 in SETS:
-            experts(e0, e1)
+            if j < 2:
+                stepped(on_vector, j, 0, 0, 3 * C)
+                paired(on_vector, j, 3, 3 * C, SHARED)
+                paired(on_scalar, j, 3, SHARED, 5 * C)
+            else:
+                stepped(on_vector, j, 0, 0, 2 * C)
+                paired(on_scalar, j, 3, 3 * C, 5 * C)
+            paired(on_scalar, j, 5, 5 * C, 7 * C)
+            if j >= 2:
+                stepped(on_scalar, j, 0, 2 * C, 3 * C)
+            stepped(on_scalar, j, 7, 7 * C, E * C)
+        merge(3)
+        experts(0, 0, 2)
+        experts(3, 3, 5)
+        merge(5)
+        experts(0, 2, 3)
+        experts(5, 5, 7)
+        experts(7, 7, 8)
 
         def silus(e0, e1):
             for e in range(e0, e1):
                 nc.scalar.activation(y[:, e * C : (e + 1) * C], acc[e], SILU, bias=bias[:, e : e + 1])
 
-        silus(0, E // 2)
+        silus(0, 2)
+        silus(3, 5)
+        silus(2, 3)
         gated = keep.tile([P, EARLY], F32, name="gated")
         for s0, s1 in ((0, PAIR), (PAIR, EARLY)):
             nc.vector.tensor_tensor(gated[:, s0:s1], y[:, s0:s1], gates[0][:, s0:s1], MULT)
-        silus(E // 2, E)
+        silus(5, E)
         nc.scalar.activation(early[:].indirect(listed(0, EARLY)), gated[:], COPY)
         nc.vector.tensor_tensor(late[:].indirect(listed(EARLY, MIDDLE)), y[:, EARLY:MIDDLE], gates[0][:, EARLY:], MULT)
         nc.vector.tensor_tensor(late[:].indirect(listed(MIDDLE, E * C)), y[:, MIDDLE:], gates[1][:], MULT)

@@ -23,8 +23,9 @@ EARLY = 384
 MIDDLE = 576
 ROW_ORDER = (2, 0, 1, 3)
 SHARED = 576
-TURNED = 1280
-SPANS = ((0, 256), (256, 640), (640, 1024), (1024, TURNED))
+NEAR = 384
+NEAR_SPANS = ((0, 192), (192, NEAR))
+SPANS = ((NEAR, 768), (768, 1280), (1280, T))
 
 
 def tile_moe_res_lin_silu_kernel(tc, xT, xr, w_words, w_scales, b, gate, offs, out):
@@ -179,13 +180,11 @@ def tile_moe_res_lin_silu_kernel(tc, xT, xr, w_words, w_scales, b, gate, offs, o
                 nc.tensor.transpose(back[:, c0 : c0 + P], by_token[:, c0 : c0 + P], ident[:])
             partial.append(back)
 
-        side = keep.tile([P, T - TURNED], F32, name="side")
-        nc.gpsimd.tensor_tensor(side[:], early[:, TURNED:T], residual[:, TURNED:T], ADD)
-        for k, (t0, t1) in enumerate(SPANS):
-            end = T if t1 == TURNED else t1
-            total = keep.tile([P, end - t0], F32, name=f"total{k}")
-            nc.vector.tensor_tensor(total[:, 0 : t1 - t0], late[:, t0:t1], partial[k][:], ADD)
-            if end > t1:
-                nc.gpsimd.tensor_tensor(total[:, t1 - t0 : end - t0], side[:], late[:, t1:end], ADD)
-            queue = nc.scalar if end == T else nc.sync
-            queue.dma_start(out=out[:, t0:end], in_=total[:])
+        near = keep.tile([P, NEAR], F32, name="near")
+        for t0, t1 in NEAR_SPANS:
+            nc.vector.tensor_tensor(near[:, t0:t1], early[:, t0:t1], residual[:, t0:t1], ADD)
+        addends = [near[:, t0:t1] for t0, t1 in NEAR_SPANS] + [back[:] for back in partial]
+        for (t0, t1), addend in zip(NEAR_SPANS + SPANS, addends):
+            total = keep.tile([P, t1 - t0], F32, name=f"total{t0}")
+            nc.vector.tensor_tensor(total[:], late[:, t0:t1], addend, ADD)
+            nc.sync.dma_start(out=out[:, t0:t1], in_=total[:])

@@ -25,7 +25,7 @@ ROW_ORDER = (2, 0, 1, 3)
 SHARED = 576
 NEAR = 384
 NEAR_SPANS = ((0, 192), (192, NEAR))
-SPANS = ((NEAR, 768), (768, 1280), (1280, T))
+SPANS = ((NEAR, 640), (640, 1024), (1024, 1280), (1280, T))
 
 
 def tile_moe_res_lin_silu_kernel(tc, xT, xr, w_words, w_scales, b, gate, offs, out):
@@ -39,7 +39,8 @@ def tile_moe_res_lin_silu_kernel(tc, xT, xr, w_words, w_scales, b, gate, offs, o
         w_bytes = keep.tile([P, E, N], U8, name="w_bytes", align_bytes=64)
         bias = keep.tile([P, E], F32, name="bias")
         gates = [keep.tile([P, s1 - s0], F32, name=f"gates{s0}") for s0, s1 in ((0, MIDDLE), (MIDDLE, E * C))]
-        residual = keep.tile([P, T], F32, name="residual")
+        near_residual = keep.tile([P, NEAR], F32, name="near_residual")
+        far_residual = keep.tile([P, T - NEAR], F32, name="far_residual")
         early = keep.tile([P, T], F32, name="early")
         late = keep.tile([P, T], F32, name="late")
         ident = keep.tile([P, P], F32, name="ident")
@@ -71,7 +72,8 @@ def tile_moe_res_lin_silu_kernel(tc, xT, xr, w_words, w_scales, b, gate, offs, o
         nc.sync.dma_start(out=w_codes[1][:].bitcast(I32), in_=codes[:, E // 2 : E, :])
         nc.sync.dma_start(out=gates[0][:], in_=gate[:, 0:MIDDLE])
         nc.sync.dma_start(out=gates[1][:], in_=gate[:, MIDDLE:])
-        nc.sync.dma_start(out=residual[:], in_=xr)
+        nc.sync.dma_start(out=far_residual[:], in_=xr[:, NEAR:])
+        nc.sync.dma_start(out=near_residual[:], in_=xr[:, 0:NEAR])
 
         def listed(s0, s1):
             return offsets[:, s0 // 16 : s1 // 16]
@@ -164,11 +166,11 @@ def tile_moe_res_lin_silu_kernel(tc, xT, xr, w_words, w_scales, b, gate, offs, o
             t0, t1 = SPANS[k]
             for c0 in range(0, t1 - t0, P):
                 nc.tensor.matmul(
-                    sums[k][:, c0 : c0 + P], source[:, t0 + c0 : t0 + c0 + P], ident[:], is_transpose=True,
+                    sums[k][:, c0 : c0 + P], source[:, t0 - NEAR + c0 : t0 - NEAR + c0 + P], ident[:], is_transpose=True,
                     start=first and c0 == 0, stop=not first and c0 == t1 - t0 - P,
                 )
 
-        for source, opens in ((residual, True), (early, False)):
+        for source, opens in ((far_residual[:], True), (early[:, NEAR:], False)):
             for k in range(len(SPANS)):
                 turn(k, source, opens)
         partial = []
@@ -182,7 +184,7 @@ def tile_moe_res_lin_silu_kernel(tc, xT, xr, w_words, w_scales, b, gate, offs, o
 
         near = keep.tile([P, NEAR], F32, name="near")
         for t0, t1 in NEAR_SPANS:
-            nc.vector.tensor_tensor(near[:, t0:t1], early[:, t0:t1], residual[:, t0:t1], ADD)
+            nc.vector.tensor_tensor(near[:, t0:t1], early[:, t0:t1], near_residual[:, t0:t1], ADD)
         addends = [near[:, t0:t1] for t0, t1 in NEAR_SPANS] + [back[:] for back in partial]
         for (t0, t1), addend in zip(NEAR_SPANS + SPANS, addends):
             total = keep.tile([P, t1 - t0], F32, name=f"total{t0}")

@@ -20,9 +20,9 @@ P = 128
 PACK = 4
 PAIR = 2 * C
 EARLY = 384
-MIDDLE = 576
 ROW_ORDER = (2, 0, 1, 3)
-SHARED = 576
+SHARED = 288
+WEIGHT_LOADS = ((0, 2), (2, 5), (5, E))
 NEAR = 384
 NEAR_SPANS = ((0, 192), (192, NEAR))
 SPANS = ((NEAR, 640), (640, 1024), (1024, 1280), (1280, T))
@@ -35,10 +35,11 @@ def tile_moe_res_lin_silu_kernel(tc, xT, xr, w_words, w_scales, b, gate, offs, o
         tc.psum_pool(name="psum", bufs=1) as psum,
     ):
         offsets = keep.tile([P, E * C // 16], U16, name="offsets")
-        w_codes = [keep.tile([P, E // 2, 2 * N], U8, name=f"w_codes{h}", align_bytes=64) for h in range(2)]
+        w_loads = [keep.tile([P, e1 - e0, 2 * N], U8, name=f"w_codes{e0}", align_bytes=64) for e0, e1 in WEIGHT_LOADS]
+        w_codes = [tile[:, e - e0, :] for tile, (e0, e1) in zip(w_loads, WEIGHT_LOADS) for e in range(e0, e1)]
         w_bytes = keep.tile([P, E, N], U8, name="w_bytes", align_bytes=64)
         bias = keep.tile([P, E], F32, name="bias")
-        gates = [keep.tile([P, s1 - s0], F32, name=f"gates{s0}") for s0, s1 in ((0, MIDDLE), (MIDDLE, E * C))]
+        gates = [keep.tile([P, s1 - s0], F32, name=f"gates{s0}") for s0, s1 in ((0, EARLY), (EARLY, E * C))]
         near_residual = keep.tile([P, NEAR], F32, name="near_residual")
         far_residual = keep.tile([P, T - NEAR], F32, name="far_residual")
         early = keep.tile([P, T], F32, name="early")
@@ -62,16 +63,22 @@ def tile_moe_res_lin_silu_kernel(tc, xT, xr, w_words, w_scales, b, gate, offs, o
         make_identity(nc, ident[:])
 
         codes = w_words.rearrange("e a p n -> p (e a) n").bitcast(I32)
-        nc.sync.dma_start(out=w_codes[0][:].bitcast(I32), in_=codes[:, 0 : E // 2, :])
+
+        def load_weights(h):
+            e0, e1 = WEIGHT_LOADS[h]
+            nc.sync.dma_start(out=w_loads[h][:].bitcast(I32), in_=codes[:, e0:e1, :])
+
+        load_weights(0)
         for q in range(4):
             nc.sync.dma_start(
                 out=w_bytes[32 * q : 32 * q + 4, :, :].bitcast(I32),
                 in_=w_scales[:, 0, 4 * q : 4 * q + 4, :].rearrange("e q n -> q e n").bitcast(I32),
             )
         nc.sync.dma_start(out=bias[:], in_=b)
-        nc.sync.dma_start(out=w_codes[1][:].bitcast(I32), in_=codes[:, E // 2 : E, :])
-        nc.sync.dma_start(out=gates[0][:], in_=gate[:, 0:MIDDLE])
-        nc.sync.dma_start(out=gates[1][:], in_=gate[:, MIDDLE:])
+        load_weights(1)
+        load_weights(2)
+        nc.sync.dma_start(out=gates[0][:], in_=gate[:, 0:EARLY])
+        nc.sync.dma_start(out=gates[1][:], in_=gate[:, EARLY:])
         nc.sync.dma_start(out=far_residual[:], in_=xr[:, NEAR:])
         nc.sync.dma_start(out=near_residual[:], in_=xr[:, 0:NEAR])
 
@@ -117,7 +124,7 @@ def tile_moe_res_lin_silu_kernel(tc, xT, xr, w_words, w_scales, b, gate, offs, o
                 cols = slice((e - e0) * C, (e - e0 + 1) * C)
                 nc.tensor.matmul_mx(
                     out=acc[e],
-                    lhsT=w_codes[e // (E // 2)][:, e % (E // 2), :].bitcast(FP4X4),
+                    lhsT=w_codes[e].bitcast(FP4X4),
                     lhsT_scale=w_bytes[:, e, :],
                     rhs=slot_words[:, cols].bitcast(FP8X4),
                     rhs_scale=slot_scales[:, cols],
@@ -127,9 +134,9 @@ def tile_moe_res_lin_silu_kernel(tc, xT, xr, w_words, w_scales, b, gate, offs, o
 
         for j in ROW_ORDER:
             if j < 2:
-                stepped(on_vector, j, 0, 0, 3 * C)
-                paired(on_vector, j, 3, 3 * C, SHARED)
-                paired(on_scalar, j, 3, SHARED, 5 * C)
+                stepped(on_vector, j, 0, 0, SHARED)
+                paired(on_vector, j, 3, 3 * C, 5 * C)
+                stepped(on_scalar, j, 0, SHARED, 3 * C)
             else:
                 stepped(on_vector, j, 0, 0, 2 * C)
                 paired(on_scalar, j, 3, 3 * C, 5 * C)
@@ -157,8 +164,7 @@ def tile_moe_res_lin_silu_kernel(tc, xT, xr, w_words, w_scales, b, gate, offs, o
             nc.vector.tensor_tensor(gated[:, s0:s1], y[:, s0:s1], gates[0][:, s0:s1], MULT)
         silus(5, E)
         nc.scalar.activation(early[:].indirect(listed(0, EARLY)), gated[:], COPY)
-        nc.vector.tensor_tensor(late[:].indirect(listed(EARLY, MIDDLE)), y[:, EARLY:MIDDLE], gates[0][:, EARLY:], MULT)
-        nc.vector.tensor_tensor(late[:].indirect(listed(MIDDLE, E * C)), y[:, MIDDLE:], gates[1][:], MULT)
+        nc.vector.tensor_tensor(late[:].indirect(listed(EARLY, E * C)), y[:, EARLY:], gates[1][:], MULT)
 
         sums = [psum.tile([P, t1 - t0], F32, name=f"bank{bank}") for bank, (t0, t1) in enumerate(SPANS)]
 

@@ -19,7 +19,7 @@ COPY = mybir.ActivationFunctionType.Copy
 P = 128
 PACK = 4
 PAIR = 2 * C
-EARLY = 384
+EARLY = 416
 ROW_ORDER = (2, 0, 1, 3)
 SHARED = 288
 WEIGHT_LOADS = ((0, 2), (2, 5), (5, E))
@@ -45,6 +45,7 @@ def tile_moe_res_lin_silu_kernel(tc, xT, xr, w_words, w_scales, b, gate, offs, o
         early = keep.tile([P, T], F32, name="early")
         late = keep.tile([P, T], F32, name="late")
         ident = keep.tile([P, P], F32, name="ident")
+        one = keep.tile([P, 1], F32, name="one")
         warm = keep.tile([P, 1], F32, name="warm")
         warmed = keep.tile([P, 1], F32, name="warmed")
 
@@ -58,6 +59,7 @@ def tile_moe_res_lin_silu_kernel(tc, xT, xr, w_words, w_scales, b, gate, offs, o
         nc.vector.memset(warm[:], 0.0)
         nc.scalar.activation(warmed[:], warm[:], SILU)
         nc.gpsimd.memset(w_bytes[:].rearrange("p e n -> p (e n)").bitcast(I32), 0)
+        nc.vector.memset(one[:], 1.0)
         nc.vector.memset(early[:], 0.0)
         nc.vector.memset(late[:], 0.0)
         make_identity(nc, ident[:])
@@ -163,7 +165,7 @@ def tile_moe_res_lin_silu_kernel(tc, xT, xr, w_words, w_scales, b, gate, offs, o
         for s0, s1 in ((0, PAIR), (PAIR, EARLY)):
             nc.vector.tensor_tensor(gated[:, s0:s1], y[:, s0:s1], gates[0][:, s0:s1], MULT)
         silus(5, E)
-        nc.scalar.activation(early[:].indirect(listed(0, EARLY)), gated[:], COPY)
+        nc.scalar.activation(early[:].indirect(listed(0, EARLY)), gated[:], COPY, scale=one[:])
         nc.vector.tensor_tensor(late[:].indirect(listed(EARLY, E * C)), y[:, EARLY:], gates[1][:], MULT)
 
         sums = [psum.tile([P, t1 - t0], F32, name=f"bank{bank}") for bank, (t0, t1) in enumerate(SPANS)]

@@ -25,7 +25,8 @@ SHARED = 288
 WEIGHT_LOADS = ((0, 2), (2, 5), (5, E))
 NEAR = 384
 NEAR_SPANS = ((0, 192), (192, NEAR))
-SPANS = ((NEAR, 640), (640, 1024), (1024, 1280), (1280, T))
+TURNED = 1408
+SPANS = ((NEAR, 640), (640, 896), (896, 1152), (1152, TURNED))
 
 
 def tile_moe_res_lin_silu_kernel(tc, xT, xr, w_words, w_scales, b, gate, offs, out):
@@ -193,8 +194,16 @@ def tile_moe_res_lin_silu_kernel(tc, xT, xr, w_words, w_scales, b, gate, offs, o
         near = keep.tile([P, NEAR], F32, name="near")
         for t0, t1 in NEAR_SPANS:
             nc.vector.tensor_tensor(near[:, t0:t1], early[:, t0:t1], near_residual[:, t0:t1], ADD)
-        addends = [near[:, t0:t1] for t0, t1 in NEAR_SPANS] + [back[:] for back in partial]
-        for (t0, t1), addend in zip(NEAR_SPANS + SPANS, addends):
+        for t0, t1 in NEAR_SPANS:
             total = keep.tile([P, t1 - t0], F32, name=f"total{t0}")
-            nc.vector.tensor_tensor(total[:], late[:, t0:t1], addend, ADD)
+            nc.vector.tensor_tensor(total[:], late[:, t0:t1], near[:, t0:t1], ADD)
             nc.sync.dma_start(out=out[:, t0:t1], in_=total[:])
+        side = keep.tile([P, T - TURNED], F32, name="near")
+        nc.gpsimd.tensor_tensor(side[:], early[:, TURNED:T], far_residual[:, TURNED - NEAR :], ADD)
+        for (t0, t1), back in zip(SPANS, partial):
+            end = T if t1 == TURNED else t1
+            total = keep.tile([P, end - t0], F32, name=f"total{t0}")
+            nc.vector.tensor_tensor(total[:, 0 : t1 - t0], late[:, t0:t1], back[:], ADD)
+            if end > t1:
+                nc.gpsimd.tensor_tensor(total[:, t1 - t0 :], side[:], late[:, t1:end], ADD)
+            nc.sync.dma_start(out=out[:, t0:end], in_=total[:])

@@ -21,7 +21,7 @@ PACK = 4
 PAIR = 2 * C
 EARLY = 416
 ROW_ORDER = (2, 0, 1, 3)
-SHARED = 288
+SHARED = 320
 WEIGHT_LOADS = ((0, 2), (2, 5), (5, E))
 NEAR = 384
 NEAR_SPANS = ((0, 192), (192, NEAR))
@@ -88,11 +88,11 @@ def tile_moe_res_lin_silu_kernel(tc, xT, xr, w_words, w_scales, b, gate, offs, o
         def listed(s0, s1):
             return offsets[:, s0 // 16 : s1 // 16]
 
-        groups = ((0, 3), (3, 5), (5, 7), (7, 8))
+        groups = ((0, 3), (3, 5), (5, 6), (6, E))
         woven = {
             e0: keep.tile([P, (e1 - e0) * C, PACK], BF16, name=f"woven{e0}", align_bytes=64) for e0, e1 in groups
         }
-        pairs = {e0: keep.tile([P, 2, PAIR, 2], BF16, name=f"pairs{e0}") for e0 in (3, 5)}
+        pairs = {e0: keep.tile([P, 2, (e1 - e0) * C, 2], BF16, name=f"pairs{e0}") for e0, e1 in groups[1:3]}
 
         def on_vector(target, j, s0, s1):
             nc.vector.tensor_copy(target, rows[j][:].indirect(listed(s0, s1)))
@@ -143,17 +143,20 @@ def tile_moe_res_lin_silu_kernel(tc, xT, xr, w_words, w_scales, b, gate, offs, o
             else:
                 stepped(on_vector, j, 0, 0, 2 * C)
                 paired(on_scalar, j, 3, 3 * C, 5 * C)
-            paired(on_scalar, j, 5, 5 * C, 7 * C)
+            paired(on_scalar, j, 5, 5 * C, 6 * C)
             if j >= 2:
                 stepped(on_scalar, j, 0, 2 * C, 3 * C)
-            stepped(on_scalar, j, 7, 7 * C, E * C)
+            step = 1 if j == ROW_ORDER[-1] else 2
+            for e in range(6, E, step):
+                stepped(on_scalar, j, 6, e * C, (e + step) * C)
         merge(3)
         experts(0, 0, 2)
         experts(3, 3, 5)
         merge(5)
         experts(0, 2, 3)
-        experts(5, 5, 7)
-        experts(7, 7, 8)
+        experts(5, 5, 6)
+        experts(6, 6, 7)
+        experts(6, 7, 8)
 
         def silus(e0, e1):
             for e in range(e0, e1):

@@ -143,32 +143,30 @@ def tile_moe_res_lin_silu_kernel(tc, xT, xr, w_words, w_scales, b, gate, offs, o
             else:
                 stepped(on_vector, j, 0, 0, 2 * C)
                 paired(on_scalar, j, 3, 3 * C, 5 * C)
-            paired(on_scalar, j, 5, 5 * C, 6 * C)
-            if j >= 2:
                 stepped(on_scalar, j, 0, 2 * C, 3 * C)
+            paired(on_scalar, j, 5, 5 * C, 6 * C)
             step = 1 if j == ROW_ORDER[-1] else 2
             for e in range(6, E, step):
                 stepped(on_scalar, j, 6, e * C, (e + step) * C)
         merge(3)
         experts(0, 0, 2)
+        experts(0, 2, 3)
         experts(3, 3, 5)
         merge(5)
-        experts(0, 2, 3)
-        experts(5, 5, 6)
         experts(6, 6, 7)
+        experts(5, 5, 6)
         experts(6, 7, 8)
 
         def silus(e0, e1):
             for e in range(e0, e1):
                 nc.scalar.activation(y[:, e * C : (e + 1) * C], acc[e], SILU, bias=bias[:, e : e + 1])
 
-        silus(0, 2)
-        silus(3, 5)
-        silus(2, 3)
+        silus(0, 5)
         gated = keep.tile([P, EARLY], F32, name="gated")
-        for s0, s1 in ((0, PAIR), (PAIR, EARLY)):
+        for s0, s1 in ((0, 2 * C), (2 * C, 3 * C), (3 * C, EARLY)):
             nc.vector.tensor_tensor(gated[:, s0:s1], y[:, s0:s1], gates[0][:, s0:s1], MULT)
-        silus(5, E)
+        for e in (6, 5, 7):
+            silus(e, e + 1)
         nc.scalar.activation(early[:].indirect(listed(0, EARLY)), gated[:], COPY, scale=one[:])
         nc.vector.tensor_tensor(late[:].indirect(listed(EARLY, E * C)), y[:, EARLY:], gates[1][:], MULT)
 

@@ -19,14 +19,14 @@ COPY = mybir.ActivationFunctionType.Copy
 P = 128
 PACK = 4
 PAIR = 2 * C
-EARLY = 416
+LONG = 576
 ROW_ORDER = (2, 0, 1, 3)
 SHARED = 320
 WEIGHT_LOADS = ((0, 2), (2, 5), (5, E))
-NEAR = 384
-NEAR_SPANS = ((0, 192), (192, NEAR))
-TURNED = 1408
-SPANS = ((NEAR, 640), (640, 896), (896, 1152), (1152, TURNED))
+NEAR = 1024
+FOLDS = ((0, 448), (448, NEAR))
+NEAR_SPANS = ((0, 192), (192, 448), (448, 704), (704, NEAR))
+SPANS = ((NEAR, 1280), (1280, T))
 
 
 def tile_moe_res_lin_silu_kernel(tc, xT, xr, w_words, w_scales, b, gate, offs, out):
@@ -40,7 +40,7 @@ def tile_moe_res_lin_silu_kernel(tc, xT, xr, w_words, w_scales, b, gate, offs, o
         w_codes = [tile[:, e - e0, :] for tile, (e0, e1) in zip(w_loads, WEIGHT_LOADS) for e in range(e0, e1)]
         w_bytes = keep.tile([P, E, N], U8, name="w_bytes", align_bytes=64)
         bias = keep.tile([P, E], F32, name="bias")
-        gates = [keep.tile([P, s1 - s0], F32, name=f"gates{s0}") for s0, s1 in ((0, EARLY), (EARLY, E * C))]
+        gates = [keep.tile([P, s1 - s0], F32, name=f"gates{s0}") for s0, s1 in ((0, LONG), (LONG, E * C))]
         near_residual = keep.tile([P, NEAR], F32, name="near_residual")
         far_residual = keep.tile([P, T - NEAR], F32, name="far_residual")
         early = keep.tile([P, T], F32, name="early")
@@ -80,8 +80,8 @@ def tile_moe_res_lin_silu_kernel(tc, xT, xr, w_words, w_scales, b, gate, offs, o
         nc.sync.dma_start(out=bias[:], in_=b)
         load_weights(1)
         load_weights(2)
-        nc.sync.dma_start(out=gates[0][:], in_=gate[:, 0:EARLY])
-        nc.sync.dma_start(out=gates[1][:], in_=gate[:, EARLY:])
+        nc.sync.dma_start(out=gates[0][:], in_=gate[:, 0:LONG])
+        nc.sync.dma_start(out=gates[1][:], in_=gate[:, LONG:])
         nc.sync.dma_start(out=far_residual[:], in_=xr[:, NEAR:])
         nc.sync.dma_start(out=near_residual[:], in_=xr[:, 0:NEAR])
 
@@ -162,13 +162,13 @@ def tile_moe_res_lin_silu_kernel(tc, xT, xr, w_words, w_scales, b, gate, offs, o
                 nc.scalar.activation(y[:, e * C : (e + 1) * C], acc[e], SILU, bias=bias[:, e : e + 1])
 
         silus(0, 5)
-        gated = keep.tile([P, EARLY], F32, name="gated")
-        for s0, s1 in ((0, 2 * C), (2 * C, 3 * C), (3 * C, EARLY)):
+        gated = keep.tile([P, LONG], F32, name="gated")
+        for s0, s1 in ((0, 2 * C), (2 * C, 3 * C), (3 * C, LONG)):
             nc.vector.tensor_tensor(gated[:, s0:s1], y[:, s0:s1], gates[0][:, s0:s1], MULT)
         for e in (6, 5, 7):
             silus(e, e + 1)
-        nc.scalar.activation(early[:].indirect(listed(0, EARLY)), gated[:], COPY, scale=one[:])
-        nc.vector.tensor_tensor(late[:].indirect(listed(EARLY, E * C)), y[:, EARLY:], gates[1][:], MULT)
+        nc.scalar.activation(late[:].indirect(listed(0, LONG)), gated[:], COPY, scale=one[:])
+        nc.vector.tensor_tensor(early[:].indirect(listed(LONG, E * C)), y[:, LONG:], gates[1][:], MULT)
 
         sums = [psum.tile([P, t1 - t0], F32, name=f"bank{bank}") for bank, (t0, t1) in enumerate(SPANS)]
 
@@ -183,6 +183,9 @@ def tile_moe_res_lin_silu_kernel(tc, xT, xr, w_words, w_scales, b, gate, offs, o
         for source, opens in ((far_residual[:], True), (early[:, NEAR:], False)):
             for k in range(len(SPANS)):
                 turn(k, source, opens)
+        near = keep.tile([P, NEAR], F32, name="near")
+        for t0, t1 in FOLDS:
+            nc.vector.tensor_tensor(near[:, t0:t1], early[:, t0:t1], near_residual[:, t0:t1], ADD)
         partial = []
         for k, (t0, t1) in enumerate(SPANS):
             by_token = keep.tile([P, t1 - t0], F32, name=f"by_token{k}")
@@ -190,21 +193,10 @@ def tile_moe_res_lin_silu_kernel(tc, xT, xr, w_words, w_scales, b, gate, offs, o
             back = psum.tile([P, t1 - t0], F32, name=f"bank{k + len(SPANS)}")
             for c0 in range(0, t1 - t0, P):
                 nc.tensor.transpose(back[:, c0 : c0 + P], by_token[:, c0 : c0 + P], ident[:])
-            partial.append(back)
+            partial.append(back[:])
 
-        near = keep.tile([P, NEAR], F32, name="near")
-        for t0, t1 in NEAR_SPANS:
-            nc.vector.tensor_tensor(near[:, t0:t1], early[:, t0:t1], near_residual[:, t0:t1], ADD)
-        for t0, t1 in NEAR_SPANS:
+        spans = [((t0, t1), near[:, t0:t1]) for t0, t1 in NEAR_SPANS] + list(zip(SPANS, partial))
+        for (t0, t1), summed in spans:
             total = keep.tile([P, t1 - t0], F32, name=f"total{t0}")
-            nc.vector.tensor_tensor(total[:], late[:, t0:t1], near[:, t0:t1], ADD)
+            nc.vector.tensor_tensor(total[:], late[:, t0:t1], summed, ADD)
             nc.sync.dma_start(out=out[:, t0:t1], in_=total[:])
-        side = keep.tile([P, T - TURNED], F32, name="near")
-        nc.gpsimd.tensor_tensor(side[:], early[:, TURNED:T], far_residual[:, TURNED - NEAR :], ADD)
-        for (t0, t1), back in zip(SPANS, partial):
-            end = T if t1 == TURNED else t1
-            total = keep.tile([P, end - t0], F32, name=f"total{t0}")
-            nc.vector.tensor_tensor(total[:, 0 : t1 - t0], late[:, t0:t1], back[:], ADD)
-            if end > t1:
-                nc.gpsimd.tensor_tensor(total[:, t1 - t0 :], side[:], late[:, t1:end], ADD)
-            nc.sync.dma_start(out=out[:, t0:end], in_=total[:])

@@ -19,10 +19,11 @@ COPY = mybir.ActivationFunctionType.Copy
 P = 128
 PACK = 4
 PAIR = 2 * C
-LONG = 576
+CUTS = (0, 192, 384, 768, E * C)
 ROW_ORDER = (2, 0, 1, 3)
 SHARED = 320
 WEIGHT_LOADS = ((0, 2), (2, 5), (5, E))
+GATE_LOADS = ((CUTS[0], CUTS[1]), (CUTS[1], CUTS[3]), (CUTS[3], CUTS[4]))
 NEAR = 1024
 FOLDS = ((0, 448), (448, NEAR))
 NEAR_SPANS = ((0, 192), (192, 448), (448, 704), (704, NEAR))
@@ -40,7 +41,7 @@ def tile_moe_res_lin_silu_kernel(tc, xT, xr, w_words, w_scales, b, gate, offs, o
         w_codes = [tile[:, e - e0, :] for tile, (e0, e1) in zip(w_loads, WEIGHT_LOADS) for e in range(e0, e1)]
         w_bytes = keep.tile([P, E, N], U8, name="w_bytes", align_bytes=64)
         bias = keep.tile([P, E], F32, name="bias")
-        gates = [keep.tile([P, s1 - s0], F32, name=f"gates{s0}") for s0, s1 in ((0, LONG), (LONG, E * C))]
+        gates = [keep.tile([P, s1 - s0], F32, name=f"gates{s0}") for s0, s1 in GATE_LOADS]
         near_residual = keep.tile([P, NEAR], F32, name="near_residual")
         far_residual = keep.tile([P, T - NEAR], F32, name="far_residual")
         early = keep.tile([P, T], F32, name="early")
@@ -80,8 +81,8 @@ def tile_moe_res_lin_silu_kernel(tc, xT, xr, w_words, w_scales, b, gate, offs, o
         nc.sync.dma_start(out=bias[:], in_=b)
         load_weights(1)
         load_weights(2)
-        nc.sync.dma_start(out=gates[0][:], in_=gate[:, 0:LONG])
-        nc.sync.dma_start(out=gates[1][:], in_=gate[:, LONG:])
+        for tile, (s0, s1) in zip(gates, GATE_LOADS):
+            nc.sync.dma_start(out=tile[:], in_=gate[:, s0:s1])
         nc.sync.dma_start(out=far_residual[:], in_=xr[:, NEAR:])
         nc.sync.dma_start(out=near_residual[:], in_=xr[:, 0:NEAR])
 
@@ -161,14 +162,27 @@ def tile_moe_res_lin_silu_kernel(tc, xT, xr, w_words, w_scales, b, gate, offs, o
             for e in range(e0, e1):
                 nc.scalar.activation(y[:, e * C : (e + 1) * C], acc[e], SILU, bias=bias[:, e : e + 1])
 
+        def gate_of(s0, s1):
+            tile, first = [(t, g0) for t, (g0, g1) in zip(gates, GATE_LOADS) if g0 <= s0 < g1][0]
+            return tile[:, s0 - first : s1 - first]
+
+        def product(s0, s1):
+            gated = keep.tile([P, s1 - s0], F32, name=f"gated{s0}")
+            nc.vector.tensor_tensor(gated[:], y[:, s0:s1], gate_of(s0, s1), MULT)
+            return gated
+
+        def put_scalar(gated, s0, s1):
+            nc.scalar.activation(late[:].indirect(listed(s0, s1)), gated[:], COPY, scale=one[:])
+
+        def put_vector(s0, s1):
+            nc.vector.tensor_tensor(early[:].indirect(listed(s0, s1)), y[:, s0:s1], gate_of(s0, s1), MULT)
+
         silus(0, 5)
-        gated = keep.tile([P, LONG], F32, name="gated")
-        for s0, s1 in ((0, 2 * C), (2 * C, 3 * C), (3 * C, LONG)):
-            nc.vector.tensor_tensor(gated[:, s0:s1], y[:, s0:s1], gates[0][:, s0:s1], MULT)
         for e in (6, 5, 7):
             silus(e, e + 1)
-        nc.scalar.activation(late[:].indirect(listed(0, LONG)), gated[:], COPY, scale=one[:])
-        nc.vector.tensor_tensor(early[:].indirect(listed(LONG, E * C)), y[:, LONG:], gates[1][:], MULT)
+        for s0, s1, s2 in (CUTS[0:3], CUTS[2:5]):
+            put_scalar(product(s0, s1), s0, s1)
+            put_vector(s1, s2)
 
         sums = [psum.tile([P, t1 - t0], F32, name=f"bank{bank}") for bank, (t0, t1) in enumerate(SPANS)]
 

import concourse.mybir as mybir
from concourse.masks import make_identity

K, T, E, C, N = 512, 1536, 8, 128, 128
FLOPS = 2 * K * N * E * C

F32 = mybir.dt.float32
BF16 = mybir.dt.bfloat16
I32 = mybir.dt.int32
U32 = mybir.dt.uint32
U16 = mybir.dt.uint16
U8 = mybir.dt.uint8
FP8X4 = mybir.dt.float8_e4m3fn_x4
FP4X4 = mybir.dt.float4_e2m1fn_x4
MULT, ADD = mybir.AluOpType.mult, mybir.AluOpType.add
SILU = mybir.ActivationFunctionType.Silu
COPY = mybir.ActivationFunctionType.Copy

P = 128
PACK = 4
PAIR = 2 * C
CUTS = (0, 192, 384, 768, E * C)
ROW_ORDER = (2, 0, 1, 3)
SHARED = 320
WEIGHT_LOADS = ((0, 2), (2, 5), (5, E))
GATE_LOADS = ((CUTS[0], CUTS[1]), (CUTS[1], CUTS[3]), (CUTS[3], CUTS[4]))
NEAR = 1024
FOLDS = ((0, 448), (448, NEAR))
NEAR_SPANS = ((0, 192), (192, 448), (448, 704), (704, NEAR))
SPANS = ((NEAR, 1280), (1280, T))


def tile_moe_res_lin_silu_kernel(tc, xT, xr, w_words, w_scales, b, gate, offs, out):
    nc = tc.nc
    with (
        tc.tile_pool(name="keep", bufs=1) as keep,
        tc.psum_pool(name="psum", bufs=1) as psum,
    ):
        offsets = keep.tile([P, E * C // 16], U16, name="offsets")
        w_loads = [keep.tile([P, e1 - e0, 2 * N], U8, name=f"w_codes{e0}", align_bytes=64) for e0, e1 in WEIGHT_LOADS]
        w_codes = [tile[:, e - e0, :] for tile, (e0, e1) in zip(w_loads, WEIGHT_LOADS) for e in range(e0, e1)]
        w_bytes = keep.tile([P, E, N], U8, name="w_bytes", align_bytes=64)
        bias = keep.tile([P, E], F32, name="bias")
        gates = [keep.tile([P, s1 - s0], F32, name=f"gates{s0}") for s0, s1 in GATE_LOADS]
        near_residual = keep.tile([P, NEAR], F32, name="near_residual")
        far_residual = keep.tile([P, T - NEAR], F32, name="far_residual")
        early = keep.tile([P, T], F32, name="early")
        late = keep.tile([P, T], F32, name="late")
        ident = keep.tile([P, P], F32, name="ident")
        one = keep.tile([P, 1], F32, name="one")
        warm = keep.tile([P, 1], F32, name="warm")
        warmed = keep.tile([P, 1], F32, name="warmed")

        tokens = xT.rearrange("(p j) t -> p j t", j=PACK)
        rows = [keep.tile([P, T], F32, name=f"row{j}") for j in range(PACK)]
        for j in ROW_ORDER:
            nc.sync.dma_start(out=rows[j][:], in_=tokens[:, j, :])
            if j == ROW_ORDER[0]:
                nc.sync.dma_start(offsets[:], offs)

        nc.vector.memset(warm[:], 0.0)
        nc.scalar.activation(warmed[:], warm[:], SILU)
        nc.gpsimd.memset(w_bytes[:].rearrange("p e n -> p (e n)").bitcast(I32), 0)
        nc.vector.memset(one[:], 1.0)
        nc.vector.memset(early[:], 0.0)
        nc.vector.memset(late[:], 0.0)
        make_identity(nc, ident[:])

        codes = w_words.rearrange("e a p n -> p (e a) n").bitcast(I32)

        def load_weights(h):
            e0, e1 = WEIGHT_LOADS[h]
            nc.sync.dma_start(out=w_loads[h][:].bitcast(I32), in_=codes[:, e0:e1, :])

        load_weights(0)
        for q in range(4):
            nc.sync.dma_start(
                out=w_bytes[32 * q : 32 * q + 4, :, :].bitcast(I32),
                in_=w_scales[:, 0, 4 * q : 4 * q + 4, :].rearrange("e q n -> q e n").bitcast(I32),
            )
        nc.sync.dma_start(out=bias[:], in_=b)
        load_weights(1)
        load_weights(2)
        for tile, (s0, s1) in zip(gates, GATE_LOADS):
            nc.sync.dma_start(out=tile[:], in_=gate[:, s0:s1])
        nc.sync.dma_start(out=far_residual[:], in_=xr[:, NEAR:])
        nc.sync.dma_start(out=near_residual[:], in_=xr[:, 0:NEAR])

        def listed(s0, s1):
            return offsets[:, s0 // 16 : s1 // 16]

        groups = ((0, 3), (3, 5), (5, 6), (6, E))
        woven = {
            e0: keep.tile([P, (e1 - e0) * C, PACK], BF16, name=f"woven{e0}", align_bytes=64) for e0, e1 in groups
        }
        pairs = {e0: keep.tile([P, 2, (e1 - e0) * C, 2], BF16, name=f"pairs{e0}") for e0, e1 in groups[1:3]}

        def on_vector(target, j, s0, s1):
            nc.vector.tensor_copy(target, rows[j][:].indirect(listed(s0, s1)))

        def on_scalar(target, j, s0, s1):
            nc.scalar.activation(target, rows[j][:].indirect(listed(s0, s1)), COPY)

        def stepped(gather, j, e0, s0, s1):
            gather(woven[e0][:, s0 - e0 * C : s1 - e0 * C, j], j, s0, s1)

        def paired(gather, j, e0, s0, s1):
            gather(pairs[e0][:, j // 2, s0 - e0 * C : s1 - e0 * C, j % 2], j, s0, s1)

        def merge(e0):
            nc.vector.tensor_copy(
                woven[e0][:].bitcast(I32),
                pairs[e0][:].rearrange("p h s t -> p h (s t)").bitcast(I32).rearrange("p h s -> p s h"),
            )

        y = keep.tile([P, E * C], F32, name="y")
        acc = [psum.tile([P, C], F32, name=f"bank{e}")[:] for e in range(E)]

        def experts(group, e0, e1):
            slot_words = keep.tile([P, (e1 - e0) * C], U32, name=f"slot_words{e0}", align_bytes=64)
            slot_scales = keep.tile([P, (e1 - e0) * C], U8, name=f"slot_scales{e0}", align_bytes=64)
            nc.vector.quantize_mx(
                out=slot_words[:].bitcast(FP8X4),
                scales=slot_scales[:],
                in_=woven[group][:, (e0 - group) * C : (e1 - group) * C, :].rearrange("p s t -> p (s t)"),
            )
            for e in range(e0, e1):
                cols = slice((e - e0) * C, (e - e0 + 1) * C)
                nc.tensor.matmul_mx(
                    out=acc[e],
                    lhsT=w_codes[e].bitcast(FP4X4),
                    lhsT_scale=w_bytes[:, e, :],
                    rhs=slot_words[:, cols].bitcast(FP8X4),
                    rhs_scale=slot_scales[:, cols],
                    start=True,
                    stop=True,
                )

        for j in ROW_ORDER:
            if j < 2:
                stepped(on_vector, j, 0, 0, SHARED)
                paired(on_vector, j, 3, 3 * C, 5 * C)
                stepped(on_scalar, j, 0, SHARED, 3 * C)
            else:
                stepped(on_vector, j, 0, 0, 2 * C)
                paired(on_scalar, j, 3, 3 * C, 5 * C)
                stepped(on_scalar, j, 0, 2 * C, 3 * C)
            paired(on_scalar, j, 5, 5 * C, 6 * C)
            step = 1 if j == ROW_ORDER[-1] else 2
            for e in range(6, E, step):
                stepped(on_scalar, j, 6, e * C, (e + step) * C)
        merge(3)
        experts(0, 0, 2)
        experts(0, 2, 3)
        experts(3, 3, 5)
        merge(5)
        experts(6, 6, 7)
        experts(5, 5, 6)
        experts(6, 7, 8)

        def silus(e0, e1):
            for e in range(e0, e1):
                nc.scalar.activation(y[:, e * C : (e + 1) * C], acc[e], SILU, bias=bias[:, e : e + 1])

        def gate_of(s0, s1):
            tile, first = [(t, g0) for t, (g0, g1) in zip(gates, GATE_LOADS) if g0 <= s0 < g1][0]
            return tile[:, s0 - first : s1 - first]

        def product(s0, s1):
            gated = keep.tile([P, s1 - s0], F32, name=f"gated{s0}")
            nc.vector.tensor_tensor(gated[:], y[:, s0:s1], gate_of(s0, s1), MULT)
            return gated

        def put_scalar(gated, s0, s1):
            nc.scalar.activation(late[:].indirect(listed(s0, s1)), gated[:], COPY, scale=one[:])

        def put_vector(s0, s1):
            nc.vector.tensor_tensor(early[:].indirect(listed(s0, s1)), y[:, s0:s1], gate_of(s0, s1), MULT)

        silus(0, 5)
        for e in (6, 5, 7):
            silus(e, e + 1)
        for s0, s1, s2 in (CUTS[0:3], CUTS[2:5]):
            put_scalar(product(s0, s1), s0, s1)
            put_vector(s1, s2)

        sums = [psum.tile([P, t1 - t0], F32, name=f"bank{bank}") for bank, (t0, t1) in enumerate(SPANS)]

        def turn(k, source, first):
            t0, t1 = SPANS[k]
            for c0 in range(0, t1 - t0, P):
                nc.tensor.matmul(
                    sums[k][:, c0 : c0 + P], source[:, t0 - NEAR + c0 : t0 - NEAR + c0 + P], ident[:], is_transpose=True,
                    start=first and c0 == 0, stop=not first and c0 == t1 - t0 - P,
                )

        for source, opens in ((far_residual[:], True), (early[:, NEAR:], False)):
            for k in range(len(SPANS)):
                turn(k, source, opens)
        near = keep.tile([P, NEAR], F32, name="near")
        for t0, t1 in FOLDS:
            nc.vector.tensor_tensor(near[:, t0:t1], early[:, t0:t1], near_residual[:, t0:t1], ADD)
        partial = []
        for k, (t0, t1) in enumerate(SPANS):
            by_token = keep.tile([P, t1 - t0], F32, name=f"by_token{k}")
            nc.scalar.copy(by_token[:], sums[k][:])
            back = psum.tile([P, t1 - t0], F32, name=f"bank{k + len(SPANS)}")
            for c0 in range(0, t1 - t0, P):
                nc.tensor.transpose(back[:, c0 : c0 + P], by_token[:, c0 : c0 + P], ident[:])
            partial.append(back[:])

        spans = [((t0, t1), near[:, t0:t1]) for t0, t1 in NEAR_SPANS] + list(zip(SPANS, partial))
        for (t0, t1), summed in spans:
            total = keep.tile([P, t1 - t0], F32, name=f"total{t0}")
            nc.vector.tensor_tensor(total[:], late[:, t0:t1], summed, ADD)
            nc.sync.dma_start(out=out[:, t0:t1], in_=total[:])
